import numpy as np
import ml_dtypes


def mxq(x, axis, fmt="e4m3"):
    dtype, down = {"e4m3": (ml_dtypes.float8_e4m3fn, 7), "e5m2": (ml_dtypes.float8_e5m2, 14)}[fmt]
    v = np.moveaxis(np.asarray(x, np.float32).astype(ml_dtypes.bfloat16).astype(np.float64), axis, -1)
    blocks = v.reshape(v.shape[:-1] + (-1, 32))
    amax = np.abs(blocks).max(-1, keepdims=True)
    byte = np.maximum(np.where(amax > 0, np.frexp(amax)[1] - 1 + 127, 0) - down, 1)
    scale = np.exp2(byte - 127.0)
    codes = (blocks / scale).astype(np.float32).astype(dtype).astype(np.float64)
    return np.moveaxis((codes * scale).reshape(v.shape), -1, axis)


WIDE = False


def mx_kscale(k):
    if not WIDE:
        return np.ones(k)
    levels = np.array([10, -10, 5, -5, 0])
    if k % 512:
        return np.exp2(np.random.permutation(np.resize(levels, k // 32))).repeat(32)
    a = np.empty((k // 512, 16))
    for p in range(k // 512):
        a[p, :8] = np.random.permutation(np.resize(levels, 8))
        for g in range(8):
            far = levels[np.abs(levels - a[p, g]) >= 10]
            a[p, g + 8] = far[np.random.randint(len(far))]
    return np.exp2(a.ravel()).repeat(32)


def f64(x):
    return np.asarray(x).astype(np.float64)


def striped(idx):
    return np.tile(idx.reshape(-1, 16).T, (8, 1)).astype(np.uint16)


def unstriped(offs):
    return offs[:16].T.reshape(-1).astype(np.int64)


E2M1 = np.array([0.0, 0.5, 1.0, 1.5, 2.0, 3.0, 4.0, 6.0, -0.0, -0.5, -1.0, -1.5, -2.0, -3.0, -4.0, -6.0])


def pack_weight(w, fmt):
    k, n = w.shape
    w = f64(np.asarray(w, np.float32).astype(ml_dtypes.bfloat16)).reshape(k // 32, 32, n)
    amax = np.abs(w).max(1)
    if fmt == "e4m3":
        byte = np.frexp(amax)[1] - 1 + 127 - 7
    else:
        mant, ex = np.frexp(amax / 6.0)
        byte = np.where(mant > 0.5, ex, ex - 1) + 127
    byte = np.clip(np.where(amax > 0, byte, 1), 1, 254)
    scaled = (w * np.exp2(127.0 - byte)[:, None, :]).reshape(k, n).astype(np.float32)
    by_word = np.ascontiguousarray(scaled.reshape(k // 512, 128, 4, n).transpose(0, 1, 3, 2))
    if fmt == "e4m3":
        words = by_word.astype(ml_dtypes.float8_e4m3fn).view(np.uint8)
    else:
        c = by_word.astype(ml_dtypes.float4_e2m1fn).view(np.uint8) & 0xF
        words = (c[..., 0::2] | (c[..., 1::2] << 4)).reshape(k // 512, 128, 2 * n)
    return np.ascontiguousarray(words), np.ascontiguousarray(byte.astype(np.uint8).reshape(k // 512, 16, n))


def unpack_weight(words, scales, fmt):
    g, _, n = scales.shape
    words = np.ascontiguousarray(words).reshape(g, 128, n, -1)
    if fmt == "e4m3":
        vals = words.view(ml_dtypes.float8_e4m3fn).astype(np.float64)
    else:
        nib = np.empty((g, 128, n, 4), np.uint8)
        nib[..., 0::2] = words & 0xF
        nib[..., 1::2] = words >> 4
        vals = E2M1[nib]
    vals = vals * np.repeat(np.exp2(scales.astype(np.float64) - 127.0), 8, axis=1)[..., None]
    return vals.transpose(0, 1, 3, 2).reshape(g * 512, n)


def planes(y):
    n, m = y.shape
    v = y.astype(np.float32).astype(ml_dtypes.bfloat16).astype(np.float64).reshape(n // 32, 32, m)
    top = np.abs(v).max(1)
    byte = np.clip(np.where(top > 0, np.frexp(top)[1] - 1 + 127 - 7, 1), 1, 254)
    codes = (v * np.exp2(127.0 - byte)[:, None, :]).reshape(n, m).astype(np.float32).astype(ml_dtypes.float8_e4m3fn).view(np.uint8)
    words = codes.reshape(n // 512, 128, 4, m).transpose(0, 1, 3, 2)
    return np.ascontiguousarray(words), np.ascontiguousarray(byte.astype(np.uint8).reshape(n // 512, 16, m))


def relu2(v):
    return np.maximum(v, 0.0) ** 2


K, T, E, C, H, HS, N = 512, 512, 4, 128, 512, 1024, 512


def by_expert(wq, xq):
    return np.concatenate([wq[e].T @ xq[:, e * C:(e + 1) * C] for e in range(E)], axis=1)


def setup_inputs():
    n = np.random.standard_normal
    s = mx_kscale(K)
    u = mx_kscale(H)
    v = mx_kscale(HS)
    slot_token = np.random.permutation(T)[:E * C]
    x = pack_weight(n((K, T)) * s[:, None], "e4m3")
    w1 = [pack_weight(m, "e2m1") for m in n((E, K, H)) / np.sqrt(K) / s[None, :, None] * u]
    w2 = [pack_weight(m, "e2m1") for m in n((E, H, N)) / np.sqrt(H) / u[None, :, None] ** 2]
    w1s = pack_weight(n((K, HS)) / np.sqrt(K) / s[:, None] * v, "e4m3")
    w2s = pack_weight(n((HS, N)) / np.sqrt(HS) / v[:, None] ** 2, "e4m3")
    return {
        "x_words": x[0],
        "x_scales": x[1],
        "w1_words": np.stack([m[0] for m in w1]),
        "w1_scales": np.stack([m[1] for m in w1]),
        "w2_words": np.stack([m[0] for m in w2]),
        "w2_scales": np.stack([m[1] for m in w2]),
        "w1s_words": w1s[0],
        "w1s_scales": w1s[1],
        "w2s_words": w2s[0],
        "w2s_scales": w2s[1],
        "gate": np.tile(np.random.uniform(0.2, 1.0, E * C), (128, 1)).astype(np.float32),
        "offs": striped(slot_token),
    }


def reference(x_words, x_scales, w1_words, w1_scales, w2_words, w2_scales, w1s_words, w1s_scales, w2s_words, w2s_scales, gate, offs):
    w1 = np.stack([unpack_weight(w1_words[e], w1_scales[e], "e2m1") for e in range(E)])
    w2 = np.stack([unpack_weight(w2_words[e], w2_scales[e], "e2m1") for e in range(E)])
    w1s = unpack_weight(w1s_words, w1s_scales, "e4m3")
    w2s = unpack_weight(w2s_words, w2s_scales, "e4m3")
    idx = unstriped(offs)
    x = unpack_weight(x_words, x_scales, "e4m3")
    hs = relu2(w1s.T @ x)
    ys = w2s.T @ mxq(hs, 0, "e4m3")
    h = relu2(by_expert(w1, x[:, idx]))
    y = by_expert(w2, mxq(h, 0, "e4m3"))
    c = np.zeros((N, T))
    c[:, idx] = f64(gate[:1]) * y
    out_0 = ys + c
    return (out_0,) + planes(out_0)

@@ -1,0 +1,275 @@
+from contextlib import ExitStack
+
+import concourse.mybir as mybir
+from concourse.masks import make_identity
+
+K, T, E, C, H, HS, N = 512, 512, 4, 128, 512, 1024, 512
+FLOPS = 2 * T * (K * HS + HS * N + K * H + H * N)
+
+F32 = mybir.dt.float32
+BF16 = mybir.dt.bfloat16
+I32 = mybir.dt.int32
+U32 = mybir.dt.uint32
+U16 = mybir.dt.uint16
+U8 = mybir.dt.uint8
+FP8X4 = mybir.dt.float8_e4m3fn_x4
+FP4X4 = mybir.dt.float4_e2m1fn_x4
+ACT = mybir.ActivationFunctionType
+ALU = mybir.AluOpType
+
+P = 128
+G = HS // 512
+
+
+def tile_moe_shf_mlp_relu2_kernel(
+    tc, x_words, x_scales, w1_words, w1_scales, w2_words, w2_scales, w1s_words, w1s_scales,
+    w2s_words, w2s_scales, gate, offs, out_0, out_1, out_2,
+):
+    nc = tc.nc
+    with ExitStack() as ctx:
+        keep = ctx.enter_context(tc.tile_pool(name="keep", bufs=1))
+        ring = ctx.enter_context(tc.tile_pool(name="ring", bufs=2))
+        psum = ctx.enter_context(tc.psum_pool(name="psum", bufs=1))
+
+        def held(shape, dtype, name):
+            return keep.tile(shape, dtype, name=name, align_bytes=64)
+
+        def bank(number, shape):
+            return psum.tile(shape, F32, name="bank%d" % number)
+
+        offsets = keep.tile([P, T // 16], U16, name="offsets")
+        xw = held([P, T], I32, "xw")
+        xs = held([P, T], U8, "xs")
+        w1sc = held([P, E, H], U8, "w1sc")
+        w2sc = held([P, E, N], U8, "w2sc")
+        shsc = held([P, 512], U8, "shsc")
+        ident = held([P, P], F32, "ident")
+
+        nc.vector.memset(xs[:].bitcast(I32), 0)
+        nc.vector.memset(w1sc[:].rearrange("p e n -> p (e n)").bitcast(I32), 0)
+        nc.gpsimd.memset(w2sc[:].rearrange("p e n -> p (e n)").bitcast(I32), 0)
+        nc.gpsimd.memset(shsc[:].bitcast(I32), 0)
+        make_identity(nc, ident[:])
+
+        w1w = [held([P, 2, 2 * H], U8, "w1w%d" % a) for a in range(2)]
+        w2w = [held([P, 2, 2 * N], U8, "w2w%d" % a) for a in range(2)]
+        w1sw = held([P, HS], I32, "w1sw")
+        w2sw = held([P, G, N], I32, "w2sw")
+        gates = held([P, T], F32, "gates")
+
+        def load_pair(tile, words, a):
+            nc.sync.dma_start(
+                out=tile[:].bitcast(I32),
+                in_=words[2 * a : 2 * a + 2, 0].rearrange("e p b -> p e b").bitcast(I32),
+            )
+
+        def load_expert_scales(tile, scales):
+            for q in range(4):
+                nc.sync.dma_start(
+                    out=tile[32 * q : 32 * q + 4, :, :].bitcast(I32),
+                    in_=scales[:, 0, 4 * q : 4 * q + 4, :].rearrange("e r n -> r e n").bitcast(I32),
+                )
+
+        nc.sync.dma_start(offsets[:], offs)
+        nc.sync.dma_start(out=xw[:], in_=x_words[0].rearrange("p t d -> p (t d)").bitcast(I32))
+        for q in range(4):
+            nc.sync.dma_start(
+                out=xs[32 * q : 32 * q + 4, :].bitcast(I32),
+                in_=x_scales[0, 4 * q : 4 * q + 4, :].bitcast(I32),
+            )
+        load_pair(w1w[0], w1_words, 0)
+        load_expert_scales(w1sc, w1_scales)
+        load_pair(w2w[0], w2_words, 0)
+        load_expert_scales(w2sc, w2_scales)
+        for q in range(4):
+            nc.sync.dma_start(
+                out=shsc[32 * q : 32 * q + 8, :].bitcast(I32),
+                in_=w1s_scales[0, 4 * q : 4 * q + 4, :].bitcast(I32).rearrange("r (g n) -> g r n", g=G),
+            )
+            nc.sync.dma_start(
+                out=shsc[32 * q + 8 : 32 * q + 16, :].bitcast(I32),
+                in_=w2s_scales[:, 4 * q : 4 * q + 4, :].bitcast(I32),
+            )
+        nc.sync.dma_start(out=w1sw[:], in_=w1s_words[0].rearrange("p l d -> p (l d)").bitcast(I32))
+        load_pair(w1w[1], w1_words, 1)
+        load_pair(w2w[1], w2_words, 1)
+        nc.sync.dma_start(out=gates[:], in_=gate)
+        nc.sync.dma_start(out=w2sw[:], in_=w2s_words.rearrange("g p n d -> p g (n d)").bitcast(I32))
+
+        xg = [held([P, C], U32, "xg%d" % e) for e in range(E)]
+        xgs = [held([P, C], U8, "xgs%d" % e) for e in range(E)]
+        w2p = [held([P, 2 * N], U8, "w2p%d" % e) for e in range(E)]
+        w2scp = [held([P, N], U8, "w2scp%d" % e) for e in range(E)]
+        hq = [held([P, C], U32, "hq%d" % e) for e in range(E)]
+        hsc = [held([P, C], U8, "hsc%d" % e) for e in range(E)]
+        ysb = {}
+        win = [held([P, T], F32, "win%d" % t) for t in range(4)]
+        w1sp = held([P, HS], I32, "w1sp")
+        w2sp = held([P, G, N], I32, "w2sp")
+        shscp = held([P, 512], U8, "shscp")
+        hsb = [held([P, T, 4], BF16, "hsb%d" % g) for g in range(G)]
+        hsq = [held([P, T], U32, "hsq%d" % g) for g in range(G)]
+        hssc = [held([P, T], U8, "hssc%d" % g) for g in range(G)]
+
+        def slots(e):
+            return offsets[:, e * (C // 16) : (e + 1) * (C // 16)]
+
+        def deal(out, in_, run):
+            nc.vector.tensor_copy(
+                out=out.rearrange("p (t c i) -> p c t i", t=4, i=run),
+                in_=in_.rearrange("p (c i t) -> p c t i", t=4, i=run),
+            )
+
+        def gather(e):
+            nc.vector.tensor_copy(xg[e][:], xw[:].bitcast(U32).indirect(slots(e)))
+            nc.vector.tensor_copy(xgs[e][:], xs[:].indirect(slots(e)))
+
+        def deal_w2(e):
+            deal(w2p[e][:].bitcast(U16), w2w[e // 2][:, e % 2, :].bitcast(U16), 8)
+            deal(w2scp[e][:], w2sc[:, e, :], 16)
+
+        def routed_first(e):
+            pre = bank(e % 2, [P, H])
+            nc.tensor.matmul_mx(
+                out=pre[:], lhsT=xg[e][:].bitcast(FP8X4), lhsT_scale=xgs[e][:],
+                rhs=w1w[e // 2][:, e % 2, :].bitcast(FP4X4), rhs_scale=w1sc[:, e, :],
+                start=True, stop=True,
+            )
+            relu = ring.tile([P, 4, P], F32, name="relu_r")
+            nc.scalar.activation(relu[:], pre[:].rearrange("s (p t) -> s t p", t=4), ACT.Relu)
+            turned = bank(2 + e % 2, [P, 4, C])
+            for t in range(4):
+                nc.tensor.transpose(turned[:, t, :], relu[:, t, :], ident[:])
+            hb = ring.tile([P, C, 4], BF16, name="hb", align_bytes=64)
+            nc.scalar.activation(hb[:], turned[:].rearrange("p t s -> p s t"), ACT.Square)
+            nc.vector.quantize_mx(
+                out=hq[e][:].bitcast(FP8X4), scales=hsc[e][:], in_=hb[:].rearrange("p s t -> p (s t)")
+            )
+
+        def routed_second(e):
+            acc = bank(4 + e % 2, [P, 4, C])
+            for t in range(4):
+                nc.tensor.matmul_mx(
+                    out=acc[:, t, :],
+                    lhsT=w2p[e][:, 2 * P * t : 2 * P * (t + 1)].bitcast(FP4X4),
+                    lhsT_scale=w2scp[e][:, P * t : P * (t + 1)],
+                    rhs=hq[e][:].bitcast(FP8X4), rhs_scale=hsc[e][:],
+                    start=True, stop=True,
+                )
+            return acc
+
+        def copy_out(e, acc, first, count, name):
+            tile = held([P, count, C], F32, name)
+            nc.scalar.copy(tile[:], acc[:, first : first + count, :])
+            for t in range(count):
+                ysb[e, first + t] = tile[:, t, :]
+
+        def scatter(e, t):
+            nc.vector.tensor_tensor(
+                win[t][:].indirect(slots(e)), ysb[e, t], gates[:, e * C : (e + 1) * C], ALU.mult
+            )
+
+        def shared_first(g, pair):
+            relu = held([P, 2, P, 4], F32, "relu_s%d" % (2 * g + pair))
+            for u in range(2):
+                b = 2 * pair + u
+                pre = bank(6 + u, [P, 4, P])
+                for t in range(4):
+                    nc.tensor.matmul_mx(
+                        out=pre[:, t, :],
+                        lhsT=w1sp[:, 512 * g + P * t : 512 * g + P * (t + 1)].bitcast(FP8X4),
+                        lhsT_scale=shscp[4 * g : P, P * t : P * (t + 1)],
+                        rhs=xw[:, P * b : P * (b + 1)].bitcast(FP8X4),
+                        rhs_scale=xs[:, P * b : P * (b + 1)],
+                        start=True, stop=True,
+                    )
+                nc.scalar.activation(relu[:, u, :, :], pre[:].rearrange("p t s -> p s t"), ACT.Relu)
+            nc.scalar.activation(
+                hsb[g][:, 2 * P * pair : 2 * P * (pair + 1), :].rearrange("p s t -> p (s t)"),
+                relu[:].rearrange("p u s t -> p (u s t)"), ACT.Square,
+            )
+
+        def shared_quantize(g):
+            nc.vector.quantize_mx(
+                out=hsq[g][:].bitcast(FP8X4), scales=hssc[g][:], in_=hsb[g][:].rearrange("p s t -> p (s t)")
+            )
+
+        gather(0)
+        gather(1)
+        routed_first(0)
+        deal_w2(0)
+        routed_first(1)
+        deal_w2(1)
+        gather(2)
+        gather(3)
+        for g in range(G):
+            deal(w1sp[:, 512 * g : 512 * (g + 1)], w1sw[:, 512 * g : 512 * (g + 1)], 4)
+        deal(shscp[:], shsc[:], 16)
+        copy_out(0, routed_second(0), 0, 4, "ysb0")
+        deal_w2(2)
+        deal_w2(3)
+        routed_first(2)
+        copy_out(1, routed_second(1), 0, 4, "ysb1")
+        for t in range(4):
+            scatter(0, t)
+        for g in range(G):
+            deal(w2sp[:, g, :], w2sw[:, g, :], 4)
+        shared_first(0, 0)
+        routed_first(3)
+        copy_out(2, routed_second(2), 0, 4, "ysb2")
+        for t in range(4):
+            scatter(1, t)
+        shared_first(0, 1)
+        last = routed_second(3)
+        for t in range(4):
+            scatter(2, t)
+        shared_quantize(0)
+        copy_out(3, last, 0, 2, "relu_s1")
+        for t in range(2):
+            scatter(3, t)
+        shared_first(1, 0)
+        shared_first(1, 1)
+        shared_quantize(1)
+        copy_out(3, last, 2, 2, "relu_s3")
+
+        ys = [bank(t, [P, T]) for t in range(4)]
+        for g in range(G):
+            for t in range(4):
+                nc.tensor.matmul_mx(
+                    out=ys[t][:],
+                    lhsT=w2sp[:, g, P * t : P * (t + 1)].bitcast(FP8X4),
+                    lhsT_scale=shscp[8 + 4 * g : P, P * t : P * (t + 1)],
+                    rhs=hsq[g][:].bitcast(FP8X4), rhs_scale=hssc[g][:],
+                    start=(g == 0), stop=(g == G - 1),
+                )
+
+        total = held([P, 4, T], F32, "total")
+        rows = out_0.rearrange("(p t) c -> p t c", t=4)
+        for t in range(2, 4):
+            scatter(3, t)
+        for t in range(4):
+            nc.vector.tensor_tensor(total[:, t, :], ys[t][:], win[t][:], ALU.add)
+            nc.sync.dma_start(out=rows[:, t, :], in_=total[:, t, :])
+
+        half = T // 2
+        oq = held([P, T], U32, "oq")
+        osc = held([P, T], U8, "osc")
+        words_out = out_1[0].rearrange("p t d -> p (t d)").bitcast(I32)
+        for a in range(2):
+            cols = slice(half * a, half * (a + 1))
+            ob = held([P, half, 4], BF16, "ob%d" % a)
+            dst = ob[:].rearrange("p (c i) t -> p c t i", i=4)
+            src = total[:, :, cols].rearrange("p t (c i) -> p c t i", i=4)
+            if a == 0:
+                nc.vector.tensor_copy(out=dst, in_=src)
+            else:
+                nc.scalar.copy(dst, src)
+            nc.vector.quantize_mx(
+                out=oq[:, cols].bitcast(FP8X4), scales=osc[:, cols], in_=ob[:].rearrange("p s t -> p (s t)")
+            )
+            nc.sync.dma_start(out=words_out[:, cols], in_=oq[:, cols].bitcast(I32))
+        for q in range(4):
+            nc.scalar.dma_start(
+                out=out_2[0, 4 * q : 4 * q + 4, :].bitcast(I32),
+                in_=osc[32 * q : 32 * q + 4, :].bitcast(I32),
+            )

@@ -19,6 +19,7 @@ ALU = mybir.AluOpType
 
 P = 128
 G = HS // 512
+SHARED_BANKS = (2, 3, 4, 5, 6, 2, 3, 4)
 
 
 def tile_moe_shf_mlp_relu2_kernel(
@@ -28,7 +29,6 @@ def tile_moe_shf_mlp_relu2_kernel(
     nc = tc.nc
     with ExitStack() as ctx:
         keep = ctx.enter_context(tc.tile_pool(name="keep", bufs=1))
-        ring = ctx.enter_context(tc.tile_pool(name="ring", bufs=2))
         psum = ctx.enter_context(tc.psum_pool(name="psum", bufs=1))
 
         def held(shape, dtype, name):
@@ -42,14 +42,10 @@ def tile_moe_shf_mlp_relu2_kernel(
         xs = held([P, T], U8, "xs")
         w1sc = held([P, E, H], U8, "w1sc")
         w2sc = held([P, E, N], U8, "w2sc")
-        shsc = held([P, 512], U8, "shsc")
         ident = held([P, P], F32, "ident")
 
-        nc.vector.memset(xs[:].bitcast(I32), 0)
-        nc.vector.memset(w1sc[:].rearrange("p e n -> p (e n)").bitcast(I32), 0)
-        nc.gpsimd.memset(w2sc[:].rearrange("p e n -> p (e n)").bitcast(I32), 0)
-        nc.gpsimd.memset(shsc[:].bitcast(I32), 0)
-        make_identity(nc, ident[:])
+        nc.gpsimd.memset(xs[:].bitcast(I32), 0)
+        nc.vector.memset(w2sc[:].rearrange("p e n -> p (e n)").bitcast(I32), 0)
 
         w1w = [held([P, 2, 2 * H], U8, "w1w%d" % a) for a in range(2)]
         w2w = [held([P, 2, 2 * N], U8, "w2w%d" % a) for a in range(2)]
@@ -63,12 +59,11 @@ def tile_moe_shf_mlp_relu2_kernel(
                 in_=words[2 * a : 2 * a + 2, 0].rearrange("e p b -> p e b").bitcast(I32),
             )
 
-        def load_expert_scales(tile, scales):
-            for q in range(4):
-                nc.sync.dma_start(
-                    out=tile[32 * q : 32 * q + 4, :, :].bitcast(I32),
-                    in_=scales[:, 0, 4 * q : 4 * q + 4, :].rearrange("e r n -> r e n").bitcast(I32),
-                )
+        def load_expert_scales(queue, tile, scales, q):
+            queue.dma_start(
+                out=tile[32 * q : 32 * q + 4, :, :].bitcast(I32),
+                in_=scales[:, 0, 4 * q : 4 * q + 4, :].rearrange("e r n -> r e n").bitcast(I32),
+            )
 
         nc.sync.dma_start(offsets[:], offs)
         nc.sync.dma_start(out=xw[:], in_=x_words[0].rearrange("p t d -> p (t d)").bitcast(I32))
@@ -78,107 +73,120 @@ def tile_moe_shf_mlp_relu2_kernel(
                 in_=x_scales[0, 4 * q : 4 * q + 4, :].bitcast(I32),
             )
         load_pair(w1w[0], w1_words, 0)
-        load_expert_scales(w1sc, w1_scales)
+        for q in range(4):
+            load_expert_scales(nc.sync, w1sc, w1_scales, q)
+        make_identity(nc, ident[:])
+        for q in range(4):
+            load_expert_scales(nc.gpsimd, w2sc, w2_scales, q)
         load_pair(w2w[0], w2_words, 0)
-        load_expert_scales(w2sc, w2_scales)
+        nc.sync.dma_start(out=w1sw[:], in_=w1s_words[0].rearrange("p l d -> p (l d)").bitcast(I32))
         for q in range(4):
             nc.sync.dma_start(
-                out=shsc[32 * q : 32 * q + 8, :].bitcast(I32),
-                in_=w1s_scales[0, 4 * q : 4 * q + 4, :].bitcast(I32).rearrange("r (g n) -> g r n", g=G),
+                out=w2sc[32 * q + 4 : 32 * q + 8, 0:2, :].rearrange("r g n -> r (g n)").bitcast(I32),
+                in_=w1s_scales[0, 4 * q : 4 * q + 4, :].bitcast(I32),
             )
-            nc.sync.dma_start(
-                out=shsc[32 * q + 8 : 32 * q + 16, :].bitcast(I32),
-                in_=w2s_scales[:, 4 * q : 4 * q + 4, :].bitcast(I32),
-            )
-        nc.sync.dma_start(out=w1sw[:], in_=w1s_words[0].rearrange("p l d -> p (l d)").bitcast(I32))
         load_pair(w1w[1], w1_words, 1)
-        load_pair(w2w[1], w2_words, 1)
         nc.sync.dma_start(out=gates[:], in_=gate)
+        load_pair(w2w[1], w2_words, 1)
+        for q in range(4):
+            nc.sync.dma_start(
+                out=w2sc[32 * q + 4 : 32 * q + 8, 2:4, :].bitcast(I32),
+                in_=w2s_scales[:, 4 * q : 4 * q + 4, :].rearrange("g r n -> r g n").bitcast(I32),
+            )
         nc.sync.dma_start(out=w2sw[:], in_=w2s_words.rearrange("g p n d -> p g (n d)").bitcast(I32))
 
-        xg = [held([P, C], U32, "xg%d" % e) for e in range(E)]
-        xgs = [held([P, C], U8, "xgs%d" % e) for e in range(E)]
-        w2p = [held([P, 2 * N], U8, "w2p%d" % e) for e in range(E)]
-        w2scp = [held([P, N], U8, "w2scp%d" % e) for e in range(E)]
-        hq = [held([P, C], U32, "hq%d" % e) for e in range(E)]
-        hsc = [held([P, C], U8, "hsc%d" % e) for e in range(E)]
-        ysb = {}
+        xg = [held([P, C], U32, "xg0"), held([P, 3 * C], U32, "xg1")]
+        xgs = [held([P, C], U8, "xgs0"), held([P, 3 * C], U8, "xgs1")]
+        w2p = {}
+        w2scp = {}
+        hb = [held([P, C, 4], BF16, "hb0"), held([P, C, 4], BF16, "hb1"), held([P, 2 * C, 4], BF16, "hb2")]
+        hq = [held([P, C], U32, "hq0"), held([P, C], U32, "hq1"), held([P, 2 * C], U32, "hq2")]
+        hsc = [held([P, C], U8, "hsc0"), held([P, C], U8, "hsc1"), held([P, 2 * C], U8, "hsc2")]
         win = [held([P, T], F32, "win%d" % t) for t in range(4)]
         w1sp = held([P, HS], I32, "w1sp")
-        w2sp = held([P, G, N], I32, "w2sp")
-        shscp = held([P, 512], U8, "shscp")
         hsb = [held([P, T, 4], BF16, "hsb%d" % g) for g in range(G)]
         hsq = [held([P, T], U32, "hsq%d" % g) for g in range(G)]
         hssc = [held([P, T], U8, "hssc%d" % g) for g in range(G)]
 
-        def slots(e):
-            return offsets[:, e * (C // 16) : (e + 1) * (C // 16)]
+        def slots(first, count):
+            return offsets[:, first * (C // 16) : (first + count) * (C // 16)]
 
         def deal(out, in_, run):
             nc.vector.tensor_copy(
-                out=out.rearrange("p (t c i) -> p c t i", t=4, i=run),
-                in_=in_.rearrange("p (c i t) -> p c t i", t=4, i=run),
+                out=out.rearrange("p (g t c i) -> p g c t i", t=4, c=P // run, i=run),
+                in_=in_.rearrange("p (g c i t) -> p g c t i", t=4, c=P // run, i=run),
             )
 
-        def gather(e):
-            nc.vector.tensor_copy(xg[e][:], xw[:].bitcast(U32).indirect(slots(e)))
-            nc.vector.tensor_copy(xgs[e][:], xs[:].indirect(slots(e)))
+        def gather(a, first, count):
+            nc.vector.tensor_copy(xg[a][:], xw[:].bitcast(U32).indirect(slots(first, count)))
+            nc.vector.tensor_copy(xgs[a][:], xs[:].indirect(slots(first, count)))
 
-        def deal_w2(e):
-            deal(w2p[e][:].bitcast(U16), w2w[e // 2][:, e % 2, :].bitcast(U16), 8)
-            deal(w2scp[e][:], w2sc[:, e, :], 16)
+        def deal_w2(a, words_name, scales_name):
+            w2scp[a] = held([P, 2, N], U8, scales_name)
+            w2p[a] = held([P, 2, 2 * N], U8, words_name)
+            deal(w2p[a][:].rearrange("p e b -> p (e b)").bitcast(U16),
+                 w2w[a][:].rearrange("p e b -> p (e b)").bitcast(U16), 8)
+            deal(w2scp[a][:].rearrange("p e n -> p (e n)"),
+                 w2sc[:, 2 * a : 2 * a + 2, :].rearrange("p e n -> p (e n)"), 16)
 
-        def routed_first(e):
-            pre = bank(e % 2, [P, H])
+        turned = {}
+
+        def routed_relu(e):
+            a, cols = min(e, 1), slice(C * max(e - 1, 0), C * (max(e - 1, 0) + 1))
+            pre = bank(e, [P, H])
             nc.tensor.matmul_mx(
-                out=pre[:], lhsT=xg[e][:].bitcast(FP8X4), lhsT_scale=xgs[e][:],
+                out=pre[:], lhsT=xg[a][:, cols].bitcast(FP8X4), lhsT_scale=xgs[a][:, cols],
                 rhs=w1w[e // 2][:, e % 2, :].bitcast(FP4X4), rhs_scale=w1sc[:, e, :],
                 start=True, stop=True,
             )
-            relu = ring.tile([P, 4, P], F32, name="relu_r")
+            relu = held([P, 4, P], F32, "relu_r%d" % e)
             nc.scalar.activation(relu[:], pre[:].rearrange("s (p t) -> s t p", t=4), ACT.Relu)
-            turned = bank(2 + e % 2, [P, 4, C])
+            turned[e] = bank((e + 2) % 4, [P, 4, C])
             for t in range(4):
-                nc.tensor.transpose(turned[:, t, :], relu[:, t, :], ident[:])
-            hb = ring.tile([P, C, 4], BF16, name="hb", align_bytes=64)
-            nc.scalar.activation(hb[:], turned[:].rearrange("p t s -> p s t"), ACT.Square)
+                nc.tensor.transpose(turned[e][:, t, :], relu[:, t, :], ident[:])
+
+        def h_place(e):
+            return min(e, 2), slice(C * max(e - 2, 0), C * (max(e - 2, 0) + 1))
+
+        def routed_square(e):
+            a, cols = h_place(e)
+            nc.scalar.activation(hb[a][:, cols, :], turned[e][:].rearrange("p t s -> p s t"), ACT.Square)
+
+        def routed_quantize(a):
             nc.vector.quantize_mx(
-                out=hq[e][:].bitcast(FP8X4), scales=hsc[e][:], in_=hb[:].rearrange("p s t -> p (s t)")
+                out=hq[a][:].bitcast(FP8X4), scales=hsc[a][:], in_=hb[a][:].rearrange("p s t -> p (s t)")
             )
 
-        def routed_second(e):
-            acc = bank(4 + e % 2, [P, 4, C])
-            for t in range(4):
-                nc.tensor.matmul_mx(
-                    out=acc[:, t, :],
-                    lhsT=w2p[e][:, 2 * P * t : 2 * P * (t + 1)].bitcast(FP4X4),
-                    lhsT_scale=w2scp[e][:, P * t : P * (t + 1)],
-                    rhs=hq[e][:].bitcast(FP8X4), rhs_scale=hsc[e][:],
-                    start=True, stop=True,
-                )
-            return acc
+        def routed_second(e, t, out):
+            a, cols = h_place(e)
+            nc.tensor.matmul_mx(
+                out=out,
+                lhsT=w2p[e // 2][:, e % 2, 2 * P * t : 2 * P * (t + 1)].bitcast(FP4X4),
+                lhsT_scale=w2scp[e // 2][:, e % 2, P * t : P * (t + 1)],
+                rhs=hq[a][:, cols].bitcast(FP8X4), rhs_scale=hsc[a][:, cols],
+                start=True, stop=True,
+            )
 
-        def copy_out(e, acc, first, count, name):
-            tile = held([P, count, C], F32, name)
-            nc.scalar.copy(tile[:], acc[:, first : first + count, :])
-            for t in range(count):
-                ysb[e, first + t] = tile[:, t, :]
+        def copy_out(sums, name):
+            tile = held([P, sums.shape[1]], F32, name)
+            nc.scalar.copy(tile[:], sums)
+            return tile
 
-        def scatter(e, t):
+        def scatter(first, count, t, values):
             nc.vector.tensor_tensor(
-                win[t][:].indirect(slots(e)), ysb[e, t], gates[:, e * C : (e + 1) * C], ALU.mult
+                win[t][:].indirect(slots(first, count)), values, gates[:, first * C : (first + count) * C], ALU.mult
             )
 
         def shared_first(g, pair):
             relu = held([P, 2, P, 4], F32, "relu_s%d" % (2 * g + pair))
             for u in range(2):
                 b = 2 * pair + u
-                pre = bank(6 + u, [P, 4, P])
+                pre = bank(SHARED_BANKS[4 * g + b], [P, 4, P])
                 for t in range(4):
                     nc.tensor.matmul_mx(
                         out=pre[:, t, :],
                         lhsT=w1sp[:, 512 * g + P * t : 512 * g + P * (t + 1)].bitcast(FP8X4),
-                        lhsT_scale=shscp[4 * g : P, P * t : P * (t + 1)],
+                        lhsT_scale=w2scp[0][4:P, g, P * t : P * (t + 1)],
                         rhs=xw[:, P * b : P * (b + 1)].bitcast(FP8X4),
                         rhs_scale=xs[:, P * b : P * (b + 1)],
                         start=True, stop=True,
@@ -194,59 +202,71 @@ def tile_moe_shf_mlp_relu2_kernel(
                 out=hsq[g][:].bitcast(FP8X4), scales=hssc[g][:], in_=hsb[g][:].rearrange("p s t -> p (s t)")
             )
 
-        gather(0)
-        gather(1)
-        routed_first(0)
-        deal_w2(0)
-        routed_first(1)
-        deal_w2(1)
-        gather(2)
-        gather(3)
-        for g in range(G):
-            deal(w1sp[:, 512 * g : 512 * (g + 1)], w1sw[:, 512 * g : 512 * (g + 1)], 4)
-        deal(shscp[:], shsc[:], 16)
-        copy_out(0, routed_second(0), 0, 4, "ysb0")
-        deal_w2(2)
-        deal_w2(3)
-        routed_first(2)
-        copy_out(1, routed_second(1), 0, 4, "ysb1")
+        gather(0, 0, 1)
+        gather(1, 1, 3)
+        routed_relu(0)
+        routed_relu(1)
+        routed_square(0)
+        deal_w2(0, "w2p0", "w2scp0")
+        deal(w1sp[:], w1sw[:], 4)
+        routed_quantize(0)
+        routed_square(1)
+        routed_quantize(1)
+        first = [bank(4 + a, [P, 2 * C]) for a in range(2)]
+        second = bank(6, [P, 4 * C])
         for t in range(4):
-            scatter(0, t)
-        for g in range(G):
-            deal(w2sp[:, g, :], w2sw[:, g, :], 4)
-        shared_first(0, 0)
-        routed_first(3)
-        copy_out(2, routed_second(2), 0, 4, "ysb2")
+            routed_second(0, t, first[t // 2][:, C * (t % 2) : C * (t % 2 + 1)])
         for t in range(4):
-            scatter(1, t)
-        shared_first(0, 1)
-        last = routed_second(3)
-        for t in range(4):
-            scatter(2, t)
-        shared_quantize(0)
-        copy_out(3, last, 0, 2, "relu_s1")
+            routed_second(1, t, second[:, C * t : C * (t + 1)])
+        routed_relu(2)
+        y0a = copy_out(first[0][:], "y0a")
+        routed_relu(3)
+        deal_w2(1, "hb1", "hb0")
         for t in range(2):
-            scatter(3, t)
+            scatter(0, 1, t, y0a[:, C * t : C * (t + 1)])
+        routed_square(2)
+        routed_square(3)
+        routed_quantize(2)
+        y0b = copy_out(first[1][:], "relu_r3")
+        for t in range(2):
+            scatter(0, 1, 2 + t, y0b[:, C * t : C * (t + 1)])
+        w2sp = held([P, HS], I32, "relu_r3")
+        deal(w2sp[:], w2sw[:].rearrange("p g n -> p (g n)"), 4)
+        y1 = copy_out(second[:], "hb2")
+        for t in range(4):
+            scatter(1, 1, t, y1[:, C * t : C * (t + 1)])
+        double = [bank(a, [P, 4 * C]) for a in range(2)]
+        for t in range(4):
+            for e in range(2):
+                at = C * (2 * (t % 2) + e)
+                routed_second(2 + e, t, double[t // 2][:, at : at + C])
+        shared_first(0, 0)
+        y23a = copy_out(double[0][:], "y23a")
+        for t in range(2):
+            scatter(2, 2, t, y23a[:, 2 * C * t : 2 * C * (t + 1)])
+        shared_first(0, 1)
+        shared_quantize(0)
+        y23b = copy_out(double[1][:, 0 : 2 * C], "relu_s1")
+        scatter(2, 2, 2, y23b[:])
         shared_first(1, 0)
         shared_first(1, 1)
         shared_quantize(1)
-        copy_out(3, last, 2, 2, "relu_s3")
+        y23c = copy_out(double[1][:, 2 * C : 4 * C], "relu_s3")
+        scatter(2, 2, 3, y23c[:])
 
-        ys = [bank(t, [P, T]) for t in range(4)]
+        ys = [bank(SHARED_BANKS[4 + t], [P, T]) for t in range(4)]
         for g in range(G):
             for t in range(4):
                 nc.tensor.matmul_mx(
                     out=ys[t][:],
-                    lhsT=w2sp[:, g, P * t : P * (t + 1)].bitcast(FP8X4),
-                    lhsT_scale=shscp[8 + 4 * g : P, P * t : P * (t + 1)],
+                    lhsT=w2sp[:, 512 * g + P * t : 512 * g + P * (t + 1)].bitcast(FP8X4),
+                    lhsT_scale=w2scp[1][4:P, g, P * t : P * (t + 1)],
                     rhs=hsq[g][:].bitcast(FP8X4), rhs_scale=hssc[g][:],
                     start=(g == 0), stop=(g == G - 1),
                 )
 
         total = held([P, 4, T], F32, "total")
         rows = out_0.rearrange("(p t) c -> p t c", t=4)
-        for t in range(2, 4):
-            scatter(3, t)
         for t in range(4):
             nc.vector.tensor_tensor(total[:, t, :], ys[t][:], win[t][:], ALU.add)
             nc.sync.dma_start(out=rows[:, t, :], in_=total[:, t, :])

@@ -140,7 +140,7 @@ def tile_moe_shf_mlp_relu2_kernel(
                 start=True, stop=True,
             )
             relu = held([P, 4, P], F32, "relu_r%d" % e)
-            nc.scalar.activation(relu[:], pre[:].rearrange("s (p t) -> s t p", t=4), ACT.Relu)
+            nc.scalar.activation(relu[:].rearrange("s t p -> s p t"), pre[:].rearrange("s (p t) -> s p t", t=4), ACT.Relu)
             turned[e] = bank((e + 2) % 4, [P, 4, C])
             for t in range(4):
                 nc.tensor.transpose(turned[e][:, t, :], relu[:, t, :], ident[:])
@@ -202,6 +202,12 @@ def tile_moe_shf_mlp_relu2_kernel(
                 out=hsq[g][:].bitcast(FP8X4), scales=hssc[g][:], in_=hsb[g][:].rearrange("p s t -> p (s t)")
             )
 
+        warm = bank(7, [P, T])
+        for repeat in range(3):
+            nc.tensor.matmul_mx(
+                out=warm[:], lhsT=xw[:, 0:P].bitcast(FP8X4), lhsT_scale=xs[:, 0:P],
+                rhs=xw[:].bitcast(FP8X4), rhs_scale=xs[:], start=True, stop=True,
+            )
         gather(0, 0, 1)
         gather(1, 1, 3)
         routed_relu(0)
@@ -268,7 +274,10 @@ def tile_moe_shf_mlp_relu2_kernel(
         total = held([P, 4, T], F32, "total")
         rows = out_0.rearrange("(p t) c -> p t c", t=4)
         for t in range(4):
-            nc.vector.tensor_tensor(total[:, t, :], ys[t][:], win[t][:], ALU.add)
+            if t == 0:
+                nc.gpsimd.tensor_tensor(total[:, t, :], copy_out(ys[t][:], "ys0")[:], win[t][:], ALU.add)
+            else:
+                nc.vector.tensor_tensor(total[:, t, :], ys[t][:], win[t][:], ALU.add)
             nc.sync.dma_start(out=rows[:, t, :], in_=total[:, t, :])
 
         half = T // 2
@@ -289,7 +298,7 @@ def tile_moe_shf_mlp_relu2_kernel(
             )
             nc.sync.dma_start(out=words_out[:, cols], in_=oq[:, cols].bitcast(I32))
         for q in range(4):
-            nc.scalar.dma_start(
+            (nc.sync if q == 3 else nc.scalar).dma_start(
                 out=out_2[0, 4 * q : 4 * q + 4, :].bitcast(I32),
                 in_=osc[32 * q : 32 * q + 4, :].bitcast(I32),
             )

@@ -18,8 +18,12 @@ ACT = mybir.ActivationFunctionType
 ALU = mybir.AluOpType
 
 P = 128
-G = HS // 512
+PASS = 512
+G = HS // PASS
+HALF = T // 2
+WARM_PASSES = 3
 SHARED_BANKS = (2, 3, 4, 5, 6, 2, 3, 4)
+SCALAR_TOKENS = 192
 
 
 def tile_moe_shf_mlp_relu2_kernel(
@@ -40,12 +44,12 @@ def tile_moe_shf_mlp_relu2_kernel(
         offsets = keep.tile([P, T // 16], U16, name="offsets")
         xw = held([P, T], I32, "xw")
         xs = held([P, T], U8, "xs")
-        w1sc = held([P, E, H], U8, "w1sc")
-        w2sc = held([P, E, N], U8, "w2sc")
+        w1sc = held([P, E * H], U8, "w1sc")
+        w2sc = held([P, E * N], U8, "w2sc")
         ident = held([P, P], F32, "ident")
 
         nc.gpsimd.memset(xs[:].bitcast(I32), 0)
-        nc.vector.memset(w2sc[:].rearrange("p e n -> p (e n)").bitcast(I32), 0)
+        nc.vector.memset(w2sc[:].bitcast(I32), 0)
 
         w1w = [held([P, 2, 2 * H], U8, "w1w%d" % a) for a in range(2)]
         w2w = [held([P, 2, 2 * N], U8, "w2w%d" % a) for a in range(2)]
@@ -61,7 +65,7 @@ def tile_moe_shf_mlp_relu2_kernel(
 
         def load_expert_scales(queue, tile, scales, q):
             queue.dma_start(
-                out=tile[32 * q : 32 * q + 4, :, :].bitcast(I32),
+                out=tile[32 * q : 32 * q + 4, :].bitcast(I32).rearrange("r (e n) -> r e n", e=E),
                 in_=scales[:, 0, 4 * q : 4 * q + 4, :].rearrange("e r n -> r e n").bitcast(I32),
             )
 
@@ -82,7 +86,7 @@ def tile_moe_shf_mlp_relu2_kernel(
         nc.sync.dma_start(out=w1sw[:], in_=w1s_words[0].rearrange("p l d -> p (l d)").bitcast(I32))
         for q in range(4):
             nc.sync.dma_start(
-                out=w2sc[32 * q + 4 : 32 * q + 8, 0:2, :].rearrange("r g n -> r (g n)").bitcast(I32),
+                out=w2sc[32 * q + 4 : 32 * q + 8, 0 : 2 * N].bitcast(I32),
                 in_=w1s_scales[0, 4 * q : 4 * q + 4, :].bitcast(I32),
             )
         load_pair(w1w[1], w1_words, 1)
@@ -90,7 +94,7 @@ def tile_moe_shf_mlp_relu2_kernel(
         load_pair(w2w[1], w2_words, 1)
         for q in range(4):
             nc.sync.dma_start(
-                out=w2sc[32 * q + 4 : 32 * q + 8, 2:4, :].bitcast(I32),
+                out=w2sc[32 * q + 4 : 32 * q + 8, 2 * N : 4 * N].bitcast(I32).rearrange("r (g n) -> r g n", g=G),
                 in_=w2s_scales[:, 4 * q : 4 * q + 4, :].rearrange("g r n -> r g n").bitcast(I32),
             )
         nc.sync.dma_start(out=w2sw[:], in_=w2s_words.rearrange("g p n d -> p g (n d)").bitcast(I32))
@@ -127,7 +131,7 @@ def tile_moe_shf_mlp_relu2_kernel(
             deal(w2p[a][:].rearrange("p e b -> p (e b)").bitcast(U16),
                  w2w[a][:].rearrange("p e b -> p (e b)").bitcast(U16), 8)
             deal(w2scp[a][:].rearrange("p e n -> p (e n)"),
-                 w2sc[:, 2 * a : 2 * a + 2, :].rearrange("p e n -> p (e n)"), 16)
+                 w2sc[:, 2 * N * a : 2 * N * (a + 1)], 16)
 
         turned = {}
 
@@ -136,7 +140,7 @@ def tile_moe_shf_mlp_relu2_kernel(
             pre = bank(e, [P, H])
             nc.tensor.matmul_mx(
                 out=pre[:], lhsT=xg[a][:, cols].bitcast(FP8X4), lhsT_scale=xgs[a][:, cols],
-                rhs=w1w[e // 2][:, e % 2, :].bitcast(FP4X4), rhs_scale=w1sc[:, e, :],
+                rhs=w1w[e // 2][:, e % 2, :].bitcast(FP4X4), rhs_scale=w1sc[:, H * e : H * (e + 1)],
                 start=True, stop=True,
             )
             relu = held([P, 4, P], F32, "relu_r%d" % e)
@@ -185,7 +189,7 @@ def tile_moe_shf_mlp_relu2_kernel(
                 for t in range(4):
                     nc.tensor.matmul_mx(
                         out=pre[:, t, :],
-                        lhsT=w1sp[:, 512 * g + P * t : 512 * g + P * (t + 1)].bitcast(FP8X4),
+                        lhsT=w1sp[:, PASS * g + P * t : PASS * g + P * (t + 1)].bitcast(FP8X4),
                         lhsT_scale=w2scp[0][4:P, g, P * t : P * (t + 1)],
                         rhs=xw[:, P * b : P * (b + 1)].bitcast(FP8X4),
                         rhs_scale=xs[:, P * b : P * (b + 1)],
@@ -203,11 +207,12 @@ def tile_moe_shf_mlp_relu2_kernel(
             )
 
         warm = bank(7, [P, T])
-        for repeat in range(3):
+        for repeat in range(WARM_PASSES):
             nc.tensor.matmul_mx(
                 out=warm[:], lhsT=xw[:, 0:P].bitcast(FP8X4), lhsT_scale=xs[:, 0:P],
                 rhs=xw[:].bitcast(FP8X4), rhs_scale=xs[:], start=True, stop=True,
             )
+
         gather(0, 0, 1)
         gather(1, 1, 3)
         routed_relu(0)
@@ -222,11 +227,11 @@ def tile_moe_shf_mlp_relu2_kernel(
         second = bank(6, [P, 4 * C])
         for t in range(4):
             routed_second(0, t, first[t // 2][:, C * (t % 2) : C * (t % 2 + 1)])
+        y0a = copy_out(first[0][:], "y0a")
+        routed_relu(2)
+        routed_relu(3)
         for t in range(4):
             routed_second(1, t, second[:, C * t : C * (t + 1)])
-        routed_relu(2)
-        y0a = copy_out(first[0][:], "y0a")
-        routed_relu(3)
         deal_w2(1, "hb1", "hb0")
         for t in range(2):
             scatter(0, 1, t, y0a[:, C * t : C * (t + 1)])
@@ -241,6 +246,7 @@ def tile_moe_shf_mlp_relu2_kernel(
         y1 = copy_out(second[:], "hb2")
         for t in range(4):
             scatter(1, 1, t, y1[:, C * t : C * (t + 1)])
+
         double = [bank(a, [P, 4 * C]) for a in range(2)]
         for t in range(4):
             for e in range(2):
@@ -265,7 +271,7 @@ def tile_moe_shf_mlp_relu2_kernel(
             for t in range(4):
                 nc.tensor.matmul_mx(
                     out=ys[t][:],
-                    lhsT=w2sp[:, 512 * g + P * t : 512 * g + P * (t + 1)].bitcast(FP8X4),
+                    lhsT=w2sp[:, PASS * g + P * t : PASS * g + P * (t + 1)].bitcast(FP8X4),
                     lhsT_scale=w2scp[1][4:P, g, P * t : P * (t + 1)],
                     rhs=hsq[g][:].bitcast(FP8X4), rhs_scale=hssc[g][:],
                     start=(g == 0), stop=(g == G - 1),
@@ -280,21 +286,23 @@ def tile_moe_shf_mlp_relu2_kernel(
                 nc.vector.tensor_tensor(total[:, t, :], ys[t][:], win[t][:], ALU.add)
             nc.sync.dma_start(out=rows[:, t, :], in_=total[:, t, :])
 
-        half = T // 2
         oq = held([P, T], U32, "oq")
         osc = held([P, T], U8, "osc")
         words_out = out_1[0].rearrange("p t d -> p (t d)").bitcast(I32)
+        ob = [held([P, HALF, 4], BF16, "ob%d" % a) for a in range(2)]
+
+        def rounded(a, lo, hi):
+            dst = ob[a][:, lo:hi, :].rearrange("p (c i) t -> p c t i", i=4)
+            src = total[:, :, HALF * a + lo : HALF * a + hi].rearrange("p t (c i) -> p c t i", i=4)
+            return dst, src
+
+        nc.scalar.copy(*rounded(1, 0, SCALAR_TOKENS))
+        nc.vector.tensor_copy(*rounded(0, 0, HALF))
+        nc.vector.tensor_copy(*rounded(1, SCALAR_TOKENS, HALF))
         for a in range(2):
-            cols = slice(half * a, half * (a + 1))
-            ob = held([P, half, 4], BF16, "ob%d" % a)
-            dst = ob[:].rearrange("p (c i) t -> p c t i", i=4)
-            src = total[:, :, cols].rearrange("p t (c i) -> p c t i", i=4)
-            if a == 0:
-                nc.vector.tensor_copy(out=dst, in_=src)
-            else:
-                nc.scalar.copy(dst, src)
+            cols = slice(HALF * a, HALF * (a + 1))
             nc.vector.quantize_mx(
-                out=oq[:, cols].bitcast(FP8X4), scales=osc[:, cols], in_=ob[:].rearrange("p s t -> p (s t)")
+                out=oq[:, cols].bitcast(FP8X4), scales=osc[:, cols], in_=ob[a][:].rearrange("p s t -> p (s t)")
             )
             nc.sync.dma_start(out=words_out[:, cols], in_=oq[:, cols].bitcast(I32))
         for q in range(4):

@@ -181,24 +181,25 @@ def tile_moe_shf_mlp_relu2_kernel(
                 win[t][:].indirect(slots(first, count)), values, gates[:, first * C : (first + count) * C], ALU.mult
             )
 
-        def shared_first(g, pair):
-            relu = held([P, 2, P, 4], F32, "relu_s%d" % (2 * g + pair))
-            for u in range(2):
-                b = 2 * pair + u
-                pre = bank(SHARED_BANKS[4 * g + b], [P, 4, P])
-                for t in range(4):
-                    nc.tensor.matmul_mx(
-                        out=pre[:, t, :],
-                        lhsT=w1sp[:, PASS * g + P * t : PASS * g + P * (t + 1)].bitcast(FP8X4),
-                        lhsT_scale=w2scp[0][4:P, g, P * t : P * (t + 1)],
-                        rhs=xw[:, P * b : P * (b + 1)].bitcast(FP8X4),
-                        rhs_scale=xs[:, P * b : P * (b + 1)],
-                        start=True, stop=True,
-                    )
-                nc.scalar.activation(relu[:, u, :, :], pre[:].rearrange("p t s -> p s t"), ACT.Relu)
+        relus = {}
+
+        def shared_relus(g):
+            relus[g] = held([P, 4, T], F32, "relu_s%d" % g)
+            for t in range(4):
+                pre = bank(SHARED_BANKS[4 * g + t], [P, T])
+                nc.tensor.matmul_mx(
+                    out=pre[:],
+                    lhsT=w1sp[:, PASS * g + P * t : PASS * g + P * (t + 1)].bitcast(FP8X4),
+                    lhsT_scale=w2scp[0][4:P, g, P * t : P * (t + 1)],
+                    rhs=xw[:].bitcast(FP8X4), rhs_scale=xs[:],
+                    start=True, stop=True,
+                )
+                nc.scalar.activation(relus[g][:, t, :], pre[:], ACT.Relu)
+
+        def shared_square(g):
             nc.scalar.activation(
-                hsb[g][:, 2 * P * pair : 2 * P * (pair + 1), :].rearrange("p s t -> p (s t)"),
-                relu[:].rearrange("p u s t -> p (u s t)"), ACT.Square,
+                hsb[g][:].rearrange("p (c i) t -> p c t i", i=4),
+                relus[g][:].rearrange("p t (c i) -> p c t i", i=4), ACT.Square,
             )
 
         def shared_quantize(g):
@@ -252,18 +253,18 @@ def tile_moe_shf_mlp_relu2_kernel(
             for e in range(2):
                 at = C * (2 * (t % 2) + e)
                 routed_second(2 + e, t, double[t // 2][:, at : at + C])
-        shared_first(0, 0)
+        shared_relus(0)
         y23a = copy_out(double[0][:], "y23a")
         for t in range(2):
             scatter(2, 2, t, y23a[:, 2 * C * t : 2 * C * (t + 1)])
-        shared_first(0, 1)
+        shared_square(0)
         shared_quantize(0)
-        y23b = copy_out(double[1][:, 0 : 2 * C], "relu_s1")
+        y23b = copy_out(double[1][:, 0 : 2 * C], "relu_s0")
         scatter(2, 2, 2, y23b[:])
-        shared_first(1, 0)
-        shared_first(1, 1)
+        shared_relus(1)
+        shared_square(1)
         shared_quantize(1)
-        y23c = copy_out(double[1][:, 2 * C : 4 * C], "relu_s3")
+        y23c = copy_out(double[1][:, 2 * C : 4 * C], "relu_s1")
         scatter(2, 2, 3, y23c[:])
 
         ys = [bank(SHARED_BANKS[4 + t], [P, T]) for t in range(4)]

@@ -22,7 +22,7 @@ PASS = 512
 G = HS // PASS
 HALF = T // 2
 WARM_PASSES = 3
-SHARED_BANKS = (2, 3, 4, 5, 6, 2, 3, 4)
+SHARED_BANKS = (0, 1, 2, 3, 4, 6, 0, 1)
 SCALAR_TOKENS = 192
 
 
@@ -33,6 +33,7 @@ def tile_moe_shf_mlp_relu2_kernel(
     nc = tc.nc
     with ExitStack() as ctx:
         keep = ctx.enter_context(tc.tile_pool(name="keep", bufs=1))
+        late = ctx.enter_context(tc.tile_pool(name="late", bufs=1))
         psum = ctx.enter_context(tc.psum_pool(name="psum", bufs=1))
 
         def held(shape, dtype, name):
@@ -46,22 +47,21 @@ def tile_moe_shf_mlp_relu2_kernel(
         xs = held([P, T], U8, "xs")
         w1sc = held([P, E * H], U8, "w1sc")
         w2sc = held([P, E * N], U8, "w2sc")
+        w1ssc = held([P, N], U8, "w1ssc")
         ident = held([P, P], F32, "ident")
 
         nc.gpsimd.memset(xs[:].bitcast(I32), 0)
+        nc.vector.memset(w1ssc[:].bitcast(I32), 0)
         nc.vector.memset(w2sc[:].bitcast(I32), 0)
 
-        w1w = [held([P, 2, 2 * H], U8, "w1w%d" % a) for a in range(2)]
-        w2w = [held([P, 2, 2 * N], U8, "w2w%d" % a) for a in range(2)]
+        w1w = held([P, E, 2 * H], U8, "w1w")
+        w2w = held([P, E, 2 * N], U8, "w2w")
         w1sw = held([P, HS], I32, "w1sw")
         w2sw = held([P, G, N], I32, "w2sw")
         gates = held([P, T], F32, "gates")
 
-        def load_pair(tile, words, a):
-            nc.sync.dma_start(
-                out=tile[:].bitcast(I32),
-                in_=words[2 * a : 2 * a + 2, 0].rearrange("e p b -> p e b").bitcast(I32),
-            )
+        def load_words(tile, words):
+            nc.sync.dma_start(out=tile[:].bitcast(I32), in_=words[:, 0].rearrange("e p b -> p e b").bitcast(I32))
 
         def load_expert_scales(queue, tile, scales, q):
             queue.dma_start(
@@ -69,35 +69,52 @@ def tile_moe_shf_mlp_relu2_kernel(
                 in_=scales[:, 0, 4 * q : 4 * q + 4, :].rearrange("e r n -> r e n").bitcast(I32),
             )
 
-        nc.sync.dma_start(offsets[:], offs)
-        nc.sync.dma_start(out=xw[:], in_=x_words[0].rearrange("p t d -> p (t d)").bitcast(I32))
-        for q in range(4):
+        def load_x_scales(q):
             nc.sync.dma_start(
                 out=xs[32 * q : 32 * q + 4, :].bitcast(I32),
                 in_=x_scales[0, 4 * q : 4 * q + 4, :].bitcast(I32),
             )
-        load_pair(w1w[0], w1_words, 0)
-        for q in range(4):
-            load_expert_scales(nc.sync, w1sc, w1_scales, q)
-        make_identity(nc, ident[:])
-        for q in range(4):
-            load_expert_scales(nc.gpsimd, w2sc, w2_scales, q)
-        load_pair(w2w[0], w2_words, 0)
-        nc.sync.dma_start(out=w1sw[:], in_=w1s_words[0].rearrange("p l d -> p (l d)").bitcast(I32))
-        for q in range(4):
-            nc.sync.dma_start(
-                out=w2sc[32 * q + 4 : 32 * q + 8, 0 : 2 * N].bitcast(I32),
-                in_=w1s_scales[0, 4 * q : 4 * q + 4, :].bitcast(I32),
+
+        def load_w1s_scales(queue, q):
+            queue.dma_start(
+                out=w1ssc[32 * q : 32 * q + 4 * G, :].bitcast(I32),
+                in_=w1s_scales[0, 4 * q : 4 * q + 4, :].rearrange("r (g l) -> g r l", g=G).bitcast(I32),
             )
-        load_pair(w1w[1], w1_words, 1)
-        nc.sync.dma_start(out=gates[:], in_=gate)
-        load_pair(w2w[1], w2_words, 1)
-        for q in range(4):
-            nc.sync.dma_start(
+
+        def load_w2s_scales(queue, q):
+            queue.dma_start(
                 out=w2sc[32 * q + 4 : 32 * q + 8, 2 * N : 4 * N].bitcast(I32).rearrange("r (g n) -> r g n", g=G),
                 in_=w2s_scales[:, 4 * q : 4 * q + 4, :].rearrange("g r n -> r g n").bitcast(I32),
             )
+
+        nc.sync.dma_start(offsets[:], offs)
+        nc.sync.dma_start(out=xw[:], in_=x_words[0].rearrange("p t d -> p (t d)").bitcast(I32))
+        load_x_scales(0)
+        load_x_scales(1)
+        load_x_scales(2)
+        load_x_scales(3)
+        load_words(w1w, w1_words)
+        nc.sync.dma_start(out=w1sw[:], in_=w1s_words[0].rearrange("p l d -> p (l d)").bitcast(I32))
+        load_expert_scales(nc.sync, w1sc, w1_scales, 0)
+        load_expert_scales(nc.sync, w1sc, w1_scales, 1)
+        load_expert_scales(nc.sync, w1sc, w1_scales, 2)
+        load_expert_scales(nc.sync, w1sc, w1_scales, 3)
+        load_w1s_scales(nc.sync, 0)
+        load_w1s_scales(nc.sync, 1)
+        load_w1s_scales(nc.sync, 2)
+        load_w1s_scales(nc.sync, 3)
+        load_expert_scales(nc.sync, w2sc, w2_scales, 0)
+        load_expert_scales(nc.sync, w2sc, w2_scales, 1)
+        load_expert_scales(nc.sync, w2sc, w2_scales, 2)
+        load_expert_scales(nc.sync, w2sc, w2_scales, 3)
+        load_words(w2w, w2_words)
+        nc.sync.dma_start(out=gates[:], in_=gate)
         nc.sync.dma_start(out=w2sw[:], in_=w2s_words.rearrange("g p n d -> p g (n d)").bitcast(I32))
+        make_identity(nc, ident[:])
+        load_w2s_scales(nc.gpsimd, 0)
+        load_w2s_scales(nc.gpsimd, 1)
+        load_w2s_scales(nc.gpsimd, 2)
+        load_w2s_scales(nc.gpsimd, 3)
 
         xg = [held([P, C], U32, "xg0"), held([P, 3 * C], U32, "xg1")]
         xgs = [held([P, C], U8, "xgs0"), held([P, 3 * C], U8, "xgs1")]
@@ -106,8 +123,9 @@ def tile_moe_shf_mlp_relu2_kernel(
         hb = [held([P, C, 4], BF16, "hb0"), held([P, C, 4], BF16, "hb1"), held([P, 2 * C, 4], BF16, "hb2")]
         hq = [held([P, C], U32, "hq0"), held([P, C], U32, "hq1"), held([P, 2 * C], U32, "hq2")]
         hsc = [held([P, C], U8, "hsc0"), held([P, C], U8, "hsc1"), held([P, 2 * C], U8, "hsc2")]
-        win = [held([P, T], F32, "win%d" % t) for t in range(4)]
+        win = [held([P, T], F32, "win%d" % t) for t in range(2)]
         w1sp = held([P, HS], I32, "w1sp")
+        w1sscp = held([P, PASS], U8, "w1sscp")
         hsb = [held([P, T, 4], BF16, "hsb%d" % g) for g in range(G)]
         hsq = [held([P, T], U32, "hsq%d" % g) for g in range(G)]
         hssc = [held([P, T], U8, "hssc%d" % g) for g in range(G)]
@@ -125,13 +143,14 @@ def tile_moe_shf_mlp_relu2_kernel(
             nc.vector.tensor_copy(xg[a][:], xw[:].bitcast(U32).indirect(slots(first, count)))
             nc.vector.tensor_copy(xgs[a][:], xs[:].indirect(slots(first, count)))
 
-        def deal_w2(a, words_name, scales_name):
-            w2scp[a] = held([P, 2, N], U8, scales_name)
-            w2p[a] = held([P, 2, 2 * N], U8, words_name)
+        def deal_words(a):
+            w2p[a] = held([P, 2, 2 * N], U8, "w2p%d" % a)
             deal(w2p[a][:].rearrange("p e b -> p (e b)").bitcast(U16),
-                 w2w[a][:].rearrange("p e b -> p (e b)").bitcast(U16), 8)
-            deal(w2scp[a][:].rearrange("p e n -> p (e n)"),
-                 w2sc[:, 2 * N * a : 2 * N * (a + 1)], 16)
+                 w2w[:, 2 * a : 2 * a + 2, :].rearrange("p e b -> p (e b)").bitcast(U16), 8)
+
+        def deal_planes(a, name):
+            w2scp[a] = held([P, 2, N], U8, name)
+            deal(w2scp[a][:].rearrange("p e n -> p (e n)"), w2sc[:, 2 * N * a : 2 * N * (a + 1)], 16)
 
         turned = {}
 
@@ -140,12 +159,16 @@ def tile_moe_shf_mlp_relu2_kernel(
             pre = bank(e, [P, H])
             nc.tensor.matmul_mx(
                 out=pre[:], lhsT=xg[a][:, cols].bitcast(FP8X4), lhsT_scale=xgs[a][:, cols],
-                rhs=w1w[e // 2][:, e % 2, :].bitcast(FP4X4), rhs_scale=w1sc[:, H * e : H * (e + 1)],
+                rhs=w1w[:, e, :].bitcast(FP4X4), rhs_scale=w1sc[:, H * e : H * (e + 1)],
                 start=True, stop=True,
             )
             relu = held([P, 4, P], F32, "relu_r%d" % e)
-            nc.scalar.activation(relu[:].rearrange("s t p -> s p t"), pre[:].rearrange("s (p t) -> s p t", t=4), ACT.Relu)
-            turned[e] = bank((e + 2) % 4, [P, 4, C])
+            dst, src = relu[:].rearrange("s t p -> s p t"), pre[:].rearrange("s (p t) -> s p t", t=4)
+            if e % 2:
+                nc.vector.tensor_scalar_max(dst, src, 0.0)
+            else:
+                nc.scalar.activation(dst, src, ACT.Relu)
+            turned[e] = bank(4 + e, [P, 4, C])
             for t in range(4):
                 nc.tensor.transpose(turned[e][:, t, :], relu[:, t, :], ident[:])
 
@@ -171,30 +194,27 @@ def tile_moe_shf_mlp_relu2_kernel(
                 start=True, stop=True,
             )
 
-        def copy_out(sums, name):
-            tile = held([P, sums.shape[1]], F32, name)
-            nc.scalar.copy(tile[:], sums)
-            return tile
-
-        def scatter(first, count, t, values):
-            nc.vector.tensor_tensor(
-                win[t][:].indirect(slots(first, count)), values, gates[:, first * C : (first + count) * C], ALU.mult
-            )
-
         relus = {}
+        pres = {}
 
-        def shared_relus(g):
-            relus[g] = held([P, 4, T], F32, "relu_s%d" % g)
-            for t in range(4):
-                pre = bank(SHARED_BANKS[4 * g + t], [P, T])
+        def over_relu(g, part, columns, name):
+            return late.tile([P, columns], F32, name=name, offset=4 * T * (4 * g + part))
+
+        def shared_first(g, rows):
+            for t in rows:
+                pres[g, t] = bank(SHARED_BANKS[4 * g + t], [P, T])
                 nc.tensor.matmul_mx(
-                    out=pre[:],
+                    out=pres[g, t][:],
                     lhsT=w1sp[:, PASS * g + P * t : PASS * g + P * (t + 1)].bitcast(FP8X4),
-                    lhsT_scale=w2scp[0][4:P, g, P * t : P * (t + 1)],
+                    lhsT_scale=w1sscp[4 * g : P, P * t : P * (t + 1)],
                     rhs=xw[:].bitcast(FP8X4), rhs_scale=xs[:],
                     start=True, stop=True,
                 )
-                nc.scalar.activation(relus[g][:, t, :], pre[:], ACT.Relu)
+
+        def shared_relus(g):
+            relus[g] = late.tile([P, 4, T], F32, name="relu_s%d" % g, offset=16 * T * g)
+            for t in range(4):
+                nc.scalar.activation(relus[g][:, t, :], pres[g, t][:], ACT.Relu)
 
         def shared_square(g):
             nc.scalar.activation(
@@ -214,60 +234,82 @@ def tile_moe_shf_mlp_relu2_kernel(
                 rhs=xw[:].bitcast(FP8X4), rhs_scale=xs[:], start=True, stop=True,
             )
 
+        def gated(out, sums, a):
+            rows = sums.shape[1] // (2 * C)
+            nc.vector.tensor_tensor(
+                out.rearrange("p (t s) -> p t s", t=rows), sums.rearrange("p (t s) -> p t s", t=rows),
+                gates[:, 2 * C * a : 2 * C * (a + 1)].unsqueeze(1).to_broadcast([P, rows, 2 * C]), ALU.mult,
+            )
+
+        def scatter_vector(a, t, values):
+            nc.vector.tensor_copy(win[t][:].indirect(slots(2 * a, 2)), values)
+
+        def scatter_scalar(a, t, values):
+            nc.scalar.activation(win[t][:].indirect(slots(2 * a, 2)), values, ACT.Copy)
+
+        def second_pair(a, first_t, number):
+            out = bank(number, [P, 4 * C])
+            for t in range(2):
+                for e in range(2):
+                    at = C * (2 * t + e)
+                    routed_second(2 * a + e, first_t + t, out[:, at : at + C])
+            return out
+
+        lo, hi = slice(0, 2 * C), slice(2 * C, 4 * C)
         gather(0, 0, 1)
         gather(1, 1, 3)
         routed_relu(0)
         routed_relu(1)
-        routed_square(0)
-        deal_w2(0, "w2p0", "w2scp0")
-        deal(w1sp[:], w1sw[:], 4)
-        routed_quantize(0)
-        routed_square(1)
-        routed_quantize(1)
-        first = [bank(4 + a, [P, 2 * C]) for a in range(2)]
-        second = bank(6, [P, 4 * C])
-        for t in range(4):
-            routed_second(0, t, first[t // 2][:, C * (t % 2) : C * (t % 2 + 1)])
-        y0a = copy_out(first[0][:], "y0a")
         routed_relu(2)
+        deal(w1sp[:], w1sw[:], 4)
+        deal(w1sscp[:], w1ssc[:], 16)
         routed_relu(3)
-        for t in range(4):
-            routed_second(1, t, second[:, C * t : C * (t + 1)])
-        deal_w2(1, "hb1", "hb0")
-        for t in range(2):
-            scatter(0, 1, t, y0a[:, C * t : C * (t + 1)])
+        routed_square(0)
+        routed_square(1)
+        deal_planes(0, "w2scp0")
+        deal_words(0)
+        routed_quantize(0)
+        routed_quantize(1)
         routed_square(2)
         routed_square(3)
+        shared_first(0, range(2))
+        first = second_pair(0, 0, 5)
+        shared_first(0, range(2, 4))
+        deal_words(1)
         routed_quantize(2)
-        y0b = copy_out(first[1][:], "relu_r3")
-        for t in range(2):
-            scatter(0, 1, 2 + t, y0b[:, C * t : C * (t + 1)])
-        w2sp = held([P, HS], I32, "relu_r3")
+        ya = held([P, 4 * C], F32, "ya")
+        gated(ya[:], first[:], 0)
+        scatter_vector(0, 0, ya[:, lo])
+        scatter_vector(0, 1, ya[:, hi])
+        second = second_pair(0, 2, 7)
+        deal_planes(1, "hq1")
+        yb = held([P, 4 * C], F32, "yb")
+        gated(yb[:], second[:], 0)
+        w2sp = held([P, HS], I32, "ya")
         deal(w2sp[:], w2sw[:].rearrange("p g n -> p (g n)"), 4)
-        y1 = copy_out(second[:], "hb2")
-        for t in range(4):
-            scatter(1, 1, t, y1[:, C * t : C * (t + 1)])
-
-        double = [bank(a, [P, 4 * C]) for a in range(2)]
-        for t in range(4):
-            for e in range(2):
-                at = C * (2 * (t % 2) + e)
-                routed_second(2 + e, t, double[t // 2][:, at : at + C])
         shared_relus(0)
-        y23a = copy_out(double[0][:], "y23a")
-        for t in range(2):
-            scatter(2, 2, t, y23a[:, 2 * C * t : 2 * C * (t + 1)])
-        shared_square(0)
-        shared_quantize(0)
-        y23b = copy_out(double[1][:, 0 : 2 * C], "relu_s0")
-        scatter(2, 2, 2, y23b[:])
+        shared_first(1, range(4))
         shared_relus(1)
+        third = second_pair(1, 0, 3)
+        fourth = second_pair(1, 2, 2)
+        yc = held([P, 2 * C], F32, "yc")
+        gated(yc[:], third[:, lo], 1)
+        yd = held([P, 4 * C], F32, "yd")
+        gated(yd[:], fourth[:], 1)
+        scatter_vector(1, 0, yc[:])
+        shared_square(0)
         shared_square(1)
+        shared_quantize(0)
+        for t in range(2):
+            win.append(over_relu(0, t, T, "win%d" % (2 + t)))
+            scatter_scalar(0, 2 + t, yb[:, 2 * C * t : 2 * C * (t + 1)])
+            scatter_scalar(1, 2 + t, yd[:, 2 * C * t : 2 * C * (t + 1)])
+        ye = over_relu(1, 0, 2 * C, "ye")
+        gated(ye[:], third[:, hi], 1)
         shared_quantize(1)
-        y23c = copy_out(double[1][:, 2 * C : 4 * C], "relu_s1")
-        scatter(2, 2, 3, y23c[:])
+        scatter_vector(1, 1, ye[:])
 
-        ys = [bank(SHARED_BANKS[4 + t], [P, T]) for t in range(4)]
+        ys = [bank(b, [P, T]) for b in (5, 4, 6, 0)]
         for g in range(G):
             for t in range(4):
                 nc.tensor.matmul_mx(
@@ -281,10 +323,7 @@ def tile_moe_shf_mlp_relu2_kernel(
         total = held([P, 4, T], F32, "total")
         rows = out_0.rearrange("(p t) c -> p t c", t=4)
         for t in range(4):
-            if t == 0:
-                nc.gpsimd.tensor_tensor(total[:, t, :], copy_out(ys[t][:], "ys0")[:], win[t][:], ALU.add)
-            else:
-                nc.vector.tensor_tensor(total[:, t, :], ys[t][:], win[t][:], ALU.add)
+            nc.vector.tensor_tensor(total[:, t, :], ys[t][:], win[t][:], ALU.add)
             nc.sync.dma_start(out=rows[:, t, :], in_=total[:, t, :])
 
         oq = held([P, T], U32, "oq")

@@ -22,8 +22,10 @@ PASS = 512
 G = HS // PASS
 HALF = T // 2
 WARM_PASSES = 3
-SHARED_BANKS = (0, 1, 2, 3, 4, 6, 0, 1)
+SHARED_BANKS = (0, 1, 2, 3, 4, 5, 6, 0)
 SCALAR_TOKENS = 192
+PACKED_AT = 40 * T
+VECTOR_RELUS = (2, 3)
 
 
 def tile_moe_shf_mlp_relu2_kernel(
@@ -46,13 +48,12 @@ def tile_moe_shf_mlp_relu2_kernel(
         xw = held([P, T], I32, "xw")
         xs = held([P, T], U8, "xs")
         w1sc = held([P, E * H], U8, "w1sc")
-        w2sc = held([P, E * N], U8, "w2sc")
-        w1ssc = held([P, N], U8, "w1ssc")
+        packed = late.tile([P, PASS], U8, name="packed", offset=PACKED_AT)
         ident = held([P, P], F32, "ident")
-
+        w1ssc = held([P, PASS], U8, "w1ssc")
         nc.gpsimd.memset(xs[:].bitcast(I32), 0)
+        nc.vector.memset(packed[:].bitcast(I32), 0)
         nc.vector.memset(w1ssc[:].bitcast(I32), 0)
-        nc.vector.memset(w2sc[:].bitcast(I32), 0)
 
         w1w = held([P, E, 2 * H], U8, "w1w")
         w2w = held([P, E, 2 * N], U8, "w2w")
@@ -75,54 +76,38 @@ def tile_moe_shf_mlp_relu2_kernel(
                 in_=x_scales[0, 4 * q : 4 * q + 4, :].bitcast(I32),
             )
 
-        def load_w1s_scales(queue, q):
-            queue.dma_start(
+        nc.sync.dma_start(offsets[:], offs)
+        nc.sync.dma_start(out=xw[:], in_=x_words[0].rearrange("p t d -> p (t d)").bitcast(I32))
+        for q in range(4):
+            load_x_scales(q)
+        load_words(w1w, w1_words)
+        nc.sync.dma_start(out=w1sw[:], in_=w1s_words[0].rearrange("p l d -> p (l d)").bitcast(I32))
+        for q in range(4):
+            load_expert_scales(nc.sync, w1sc, w1_scales, q)
+        for q in range(4):
+            nc.sync.dma_start(
                 out=w1ssc[32 * q : 32 * q + 4 * G, :].bitcast(I32),
                 in_=w1s_scales[0, 4 * q : 4 * q + 4, :].rearrange("r (g l) -> g r l", g=G).bitcast(I32),
             )
-
-        def load_w2s_scales(queue, q):
-            queue.dma_start(
-                out=w2sc[32 * q + 4 : 32 * q + 8, 2 * N : 4 * N].bitcast(I32).rearrange("r (g n) -> r g n", g=G),
-                in_=w2s_scales[:, 4 * q : 4 * q + 4, :].rearrange("g r n -> r g n").bitcast(I32),
-            )
-
-        nc.sync.dma_start(offsets[:], offs)
-        nc.sync.dma_start(out=xw[:], in_=x_words[0].rearrange("p t d -> p (t d)").bitcast(I32))
-        load_x_scales(0)
-        load_x_scales(1)
-        load_x_scales(2)
-        load_x_scales(3)
-        load_words(w1w, w1_words)
-        nc.sync.dma_start(out=w1sw[:], in_=w1s_words[0].rearrange("p l d -> p (l d)").bitcast(I32))
-        load_expert_scales(nc.sync, w1sc, w1_scales, 0)
-        load_expert_scales(nc.sync, w1sc, w1_scales, 1)
-        load_expert_scales(nc.sync, w1sc, w1_scales, 2)
-        load_expert_scales(nc.sync, w1sc, w1_scales, 3)
-        load_w1s_scales(nc.sync, 0)
-        load_w1s_scales(nc.sync, 1)
-        load_w1s_scales(nc.sync, 2)
-        load_w1s_scales(nc.sync, 3)
-        load_expert_scales(nc.sync, w2sc, w2_scales, 0)
-        load_expert_scales(nc.sync, w2sc, w2_scales, 1)
-        load_expert_scales(nc.sync, w2sc, w2_scales, 2)
-        load_expert_scales(nc.sync, w2sc, w2_scales, 3)
+        nc.sync.dma_start(
+            out=packed[0:64, :].bitcast(I32), in_=w2_scales[:, 0].rearrange("e b n -> b e n").bitcast(I32)
+        )
+        nc.sync.dma_start(
+            out=packed[64:96, :].bitcast(I32), in_=w2s_scales.rearrange("g b n -> b g n").bitcast(I32)
+        )
         load_words(w2w, w2_words)
         nc.sync.dma_start(out=gates[:], in_=gate)
-        nc.sync.dma_start(out=w2sw[:], in_=w2s_words.rearrange("g p n d -> p g (n d)").bitcast(I32))
         make_identity(nc, ident[:])
-        load_w2s_scales(nc.gpsimd, 0)
-        load_w2s_scales(nc.gpsimd, 1)
-        load_w2s_scales(nc.gpsimd, 2)
-        load_w2s_scales(nc.gpsimd, 3)
 
         xg = [held([P, C], U32, "xg0"), held([P, 3 * C], U32, "xg1")]
         xgs = [held([P, C], U8, "xgs0"), held([P, 3 * C], U8, "xgs1")]
         w2p = {}
-        w2scp = {}
-        hb = [held([P, C, 4], BF16, "hb0"), held([P, C, 4], BF16, "hb1"), held([P, 2 * C, 4], BF16, "hb2")]
-        hq = [held([P, C], U32, "hq0"), held([P, C], U32, "hq1"), held([P, 2 * C], U32, "hq2")]
-        hsc = [held([P, C], U8, "hsc0"), held([P, C], U8, "hsc1"), held([P, 2 * C], U8, "hsc2")]
+        w2scp = held([P, E * N], U8, "w2scp")
+        w2sscp = held([P, G * N], U8, "w2sscp")
+        sorted_rows = held([P, PASS], U8, "sorted_rows")
+        hb = [held([P, 2 * C, 4], BF16, "hb%d" % a) for a in range(2)]
+        hq = {}
+        hsc = [held([P, 2 * C], U8, "hsc%d" % a) for a in range(2)]
         win = [held([P, T], F32, "win%d" % t) for t in range(2)]
         w1sp = held([P, HS], I32, "w1sp")
         w1sscp = held([P, PASS], U8, "w1sscp")
@@ -148,9 +133,12 @@ def tile_moe_shf_mlp_relu2_kernel(
             deal(w2p[a][:].rearrange("p e b -> p (e b)").bitcast(U16),
                  w2w[:, 2 * a : 2 * a + 2, :].rearrange("p e b -> p (e b)").bitcast(U16), 8)
 
-        def deal_planes(a, name):
-            w2scp[a] = held([P, 2, N], U8, name)
-            deal(w2scp[a][:].rearrange("p e n -> p (e n)"), w2sc[:, 2 * N * a : 2 * N * (a + 1)], 16)
+        def place_planes(tile, first, count):
+            for q in range(4):
+                nc.sync.dma_start(
+                    out=tile[32 * q : 32 * q + 4, :].bitcast(I32).rearrange("r (a n) -> r a n", a=count),
+                    in_=sorted_rows[first + 4 * count * q : first + 4 * count * (q + 1), :].bitcast(I32),
+                )
 
         turned = {}
 
@@ -162,7 +150,10 @@ def tile_moe_shf_mlp_relu2_kernel(
                 rhs=w1w[:, e, :].bitcast(FP4X4), rhs_scale=w1sc[:, H * e : H * (e + 1)],
                 start=True, stop=True,
             )
-            relu = held([P, 4, P], F32, "relu_r%d" % e)
+            if e == 3:
+                relu = late.tile([P, 4, P], F32, name="relu_r3", offset=PACKED_AT + 256 - 16 * P)
+            else:
+                relu = held([P, 4, P], F32, "relu_r%d" % e)
             dst, src = relu[:].rearrange("s t p -> s p t"), pre[:].rearrange("s (p t) -> s p t", t=4)
             if e % 2:
                 nc.vector.tensor_scalar_max(dst, src, 0.0)
@@ -173,7 +164,7 @@ def tile_moe_shf_mlp_relu2_kernel(
                 nc.tensor.transpose(turned[e][:, t, :], relu[:, t, :], ident[:])
 
         def h_place(e):
-            return min(e, 2), slice(C * max(e - 2, 0), C * (max(e - 2, 0) + 1))
+            return e // 2, slice(C * (e % 2), C * (e % 2 + 1))
 
         def routed_square(e):
             a, cols = h_place(e)
@@ -189,7 +180,7 @@ def tile_moe_shf_mlp_relu2_kernel(
             nc.tensor.matmul_mx(
                 out=out,
                 lhsT=w2p[e // 2][:, e % 2, 2 * P * t : 2 * P * (t + 1)].bitcast(FP4X4),
-                lhsT_scale=w2scp[e // 2][:, e % 2, P * t : P * (t + 1)],
+                lhsT_scale=w2scp[:, N * e + P * t : N * e + P * (t + 1)],
                 rhs=hq[a][:, cols].bitcast(FP8X4), rhs_scale=hsc[a][:, cols],
                 start=True, stop=True,
             )
@@ -214,7 +205,10 @@ def tile_moe_shf_mlp_relu2_kernel(
         def shared_relus(g):
             relus[g] = late.tile([P, 4, T], F32, name="relu_s%d" % g, offset=16 * T * g)
             for t in range(4):
-                nc.scalar.activation(relus[g][:, t, :], pres[g, t][:], ACT.Relu)
+                if 4 * g + t in VECTOR_RELUS:
+                    nc.vector.tensor_scalar_max(relus[g][:, t, :], pres[g, t][:], 0.0)
+                else:
+                    nc.scalar.activation(relus[g][:, t, :], pres[g, t][:], ACT.Relu)
 
         def shared_square(g):
             nc.scalar.activation(
@@ -247,9 +241,9 @@ def tile_moe_shf_mlp_relu2_kernel(
         def scatter_scalar(a, t, values):
             nc.scalar.activation(win[t][:].indirect(slots(2 * a, 2)), values, ACT.Copy)
 
-        def second_pair(a, first_t, number):
-            out = bank(number, [P, 4 * C])
-            for t in range(2):
+        def second_pair(a, first_t, number, rows=2):
+            out = bank(number, [P, 2 * C * rows])
+            for t in range(rows):
                 for e in range(2):
                     at = C * (2 * t + e)
                     routed_second(2 * a + e, first_t + t, out[:, at : at + C])
@@ -258,6 +252,10 @@ def tile_moe_shf_mlp_relu2_kernel(
         lo, hi = slice(0, 2 * C), slice(2 * C, 4 * C)
         gather(0, 0, 1)
         gather(1, 1, 3)
+        deal(sorted_rows[:], packed[:], 16)
+        place_planes(w2scp, 0, E)
+        nc.sync.dma_start(out=w2sw[:], in_=w2s_words.rearrange("g p n d -> p g (n d)").bitcast(I32))
+        place_planes(w2sscp, 64, G)
         routed_relu(0)
         routed_relu(1)
         routed_relu(2)
@@ -266,32 +264,31 @@ def tile_moe_shf_mlp_relu2_kernel(
         routed_relu(3)
         routed_square(0)
         routed_square(1)
-        deal_planes(0, "w2scp0")
         deal_words(0)
+        hq[0] = late.tile([P, 2 * C], U32, name="hq0", offset=PACKED_AT + 256, align_bytes=64)
         routed_quantize(0)
-        routed_quantize(1)
         routed_square(2)
         routed_square(3)
-        shared_first(0, range(2))
-        first = second_pair(0, 0, 5)
-        shared_first(0, range(2, 4))
+        shared_first(0, range(4))
         deal_words(1)
-        routed_quantize(2)
-        ya = held([P, 4 * C], F32, "ya")
-        gated(ya[:], first[:], 0)
-        scatter_vector(0, 0, ya[:, lo])
-        scatter_vector(0, 1, ya[:, hi])
-        second = second_pair(0, 2, 7)
-        deal_planes(1, "hq1")
+        shared_relus(0)
+        first = [second_pair(0, t, 5 + t, 1) for t in range(2)]
+        second = second_pair(0, 2, 0)
+        ya = [held([P, 2 * C], F32, "ya%d" % t) for t in range(2)]
+        for t in range(2):
+            gated(ya[t][:], first[t][:], 0)
         yb = held([P, 4 * C], F32, "yb")
         gated(yb[:], second[:], 0)
-        w2sp = held([P, HS], I32, "ya")
+        for t in range(2):
+            scatter_vector(0, t, ya[t][:])
+        hq[1] = held([P, 2 * C], U32, "ya0")
+        routed_quantize(1)
+        w2sp = held([P, HS], I32, "ya1")
         deal(w2sp[:], w2sw[:].rearrange("p g n -> p (g n)"), 4)
-        shared_relus(0)
         shared_first(1, range(4))
         shared_relus(1)
-        third = second_pair(1, 0, 3)
-        fourth = second_pair(1, 2, 2)
+        third = second_pair(1, 0, 5)
+        fourth = second_pair(1, 2, 6)
         yc = held([P, 2 * C], F32, "yc")
         gated(yc[:], third[:, lo], 1)
         yd = held([P, 4 * C], F32, "yd")
@@ -301,7 +298,7 @@ def tile_moe_shf_mlp_relu2_kernel(
         shared_square(1)
         shared_quantize(0)
         for t in range(2):
-            win.append(over_relu(0, t, T, "win%d" % (2 + t)))
+            win.append(over_relu(0, 1 + t, T, "win%d" % (2 + t)))
             scatter_scalar(0, 2 + t, yb[:, 2 * C * t : 2 * C * (t + 1)])
             scatter_scalar(1, 2 + t, yd[:, 2 * C * t : 2 * C * (t + 1)])
         ye = over_relu(1, 0, 2 * C, "ye")
@@ -309,13 +306,13 @@ def tile_moe_shf_mlp_relu2_kernel(
         shared_quantize(1)
         scatter_vector(1, 1, ye[:])
 
-        ys = [bank(b, [P, T]) for b in (5, 4, 6, 0)]
+        ys = [bank(b, [P, T]) for b in (1, 2, 3, 4)]
         for g in range(G):
             for t in range(4):
                 nc.tensor.matmul_mx(
                     out=ys[t][:],
                     lhsT=w2sp[:, PASS * g + P * t : PASS * g + P * (t + 1)].bitcast(FP8X4),
-                    lhsT_scale=w2scp[1][4:P, g, P * t : P * (t + 1)],
+                    lhsT_scale=w2sscp[:, N * g + P * t : N * g + P * (t + 1)],
                     rhs=hsq[g][:].bitcast(FP8X4), rhs_scale=hssc[g][:],
                     start=(g == 0), stop=(g == G - 1),
                 )

@@ -24,6 +24,7 @@ HALF = T // 2
 WARM_PASSES = 3
 SHARED_BANKS = (0, 1, 2, 3, 4, 5, 6, 0)
 SCALAR_TOKENS = 192
+FINISH = (0, 3, 1, 2)
 PACKED_AT = 40 * T
 VECTOR_RELUS = (2, 3)
 
@@ -235,11 +236,11 @@ def tile_moe_shf_mlp_relu2_kernel(
                 gates[:, 2 * C * a : 2 * C * (a + 1)].unsqueeze(1).to_broadcast([P, rows, 2 * C]), ALU.mult,
             )
 
-        def scatter_vector(a, t, values):
-            nc.vector.tensor_copy(win[t][:].indirect(slots(2 * a, 2)), values)
+        def scatter_vector(first, t, values):
+            nc.vector.tensor_copy(win[t][:].indirect(slots(first, values.shape[1] // C)), values)
 
-        def scatter_scalar(a, t, values):
-            nc.scalar.activation(win[t][:].indirect(slots(2 * a, 2)), values, ACT.Copy)
+        def scatter_scalar(first, t, values):
+            nc.scalar.activation(win[t][:].indirect(slots(first, values.shape[1] // C)), values, ACT.Copy)
 
         def second_pair(a, first_t, number, rows=2):
             out = bank(number, [P, 2 * C * rows])
@@ -293,22 +294,25 @@ def tile_moe_shf_mlp_relu2_kernel(
         gated(yc[:], third[:, lo], 1)
         yd = held([P, 4 * C], F32, "yd")
         gated(yd[:], fourth[:], 1)
-        scatter_vector(1, 0, yc[:])
+        scatter_vector(2, 0, yc[:])
         shared_square(0)
         shared_square(1)
         shared_quantize(0)
         for t in range(2):
             win.append(over_relu(0, 1 + t, T, "win%d" % (2 + t)))
-            scatter_scalar(0, 2 + t, yb[:, 2 * C * t : 2 * C * (t + 1)])
-            scatter_scalar(1, 2 + t, yd[:, 2 * C * t : 2 * C * (t + 1)])
+        scatter_vector(0, 2, yb[:, 0:C])
+        scatter_scalar(0, 3, yb[:, hi])
+        scatter_scalar(2, 3, yd[:, hi])
+        scatter_scalar(1, 2, yb[:, C : 2 * C])
+        scatter_scalar(2, 2, yd[:, lo])
         ye = over_relu(1, 0, 2 * C, "ye")
         gated(ye[:], third[:, hi], 1)
         shared_quantize(1)
-        scatter_vector(1, 1, ye[:])
+        scatter_vector(2, 1, ye[:])
 
         ys = [bank(b, [P, T]) for b in (1, 2, 3, 4)]
         for g in range(G):
-            for t in range(4):
+            for t in FINISH:
                 nc.tensor.matmul_mx(
                     out=ys[t][:],
                     lhsT=w2sp[:, PASS * g + P * t : PASS * g + P * (t + 1)].bitcast(FP8X4),
@@ -319,7 +323,7 @@ def tile_moe_shf_mlp_relu2_kernel(
 
         total = held([P, 4, T], F32, "total")
         rows = out_0.rearrange("(p t) c -> p t c", t=4)
-        for t in range(4):
+        for t in FINISH:
             nc.vector.tensor_tensor(total[:, t, :], ys[t][:], win[t][:], ALU.add)
             nc.sync.dma_start(out=rows[:, t, :], in_=total[:, t, :])
 

@@ -192,30 +192,29 @@ def tile_moe_shf_mlp_relu2_kernel(
         def over_relu(g, part, columns, name):
             return late.tile([P, columns], F32, name=name, offset=4 * T * (4 * g + part))
 
-        def shared_first(g, rows):
-            for t in rows:
-                pres[g, t] = bank(SHARED_BANKS[4 * g + t], [P, T])
-                nc.tensor.matmul_mx(
-                    out=pres[g, t][:],
-                    lhsT=w1sp[:, PASS * g + P * t : PASS * g + P * (t + 1)].bitcast(FP8X4),
-                    lhsT_scale=w1sscp[4 * g : P, P * t : P * (t + 1)],
-                    rhs=xw[:].bitcast(FP8X4), rhs_scale=xs[:],
-                    start=True, stop=True,
-                )
+        def shared_first(g, quarters):
+            for u in quarters:
+                pres[g, u] = bank(SHARED_BANKS[4 * g + u], [P, 4, P])
+                for t in range(4):
+                    nc.tensor.matmul_mx(
+                        out=pres[g, u][:, t, :],
+                        lhsT=w1sp[:, PASS * g + P * t : PASS * g + P * (t + 1)].bitcast(FP8X4),
+                        lhsT_scale=w1sscp[4 * g : P, P * t : P * (t + 1)],
+                        rhs=xw[:, P * u : P * (u + 1)].bitcast(FP8X4), rhs_scale=xs[:, P * u : P * (u + 1)],
+                        start=True, stop=True,
+                    )
 
         def shared_relus(g):
-            relus[g] = late.tile([P, 4, T], F32, name="relu_s%d" % g, offset=16 * T * g)
-            for t in range(4):
-                if 4 * g + t in VECTOR_RELUS:
-                    nc.vector.tensor_scalar_max(relus[g][:, t, :], pres[g, t][:], 0.0)
+            relus[g] = late.tile([P, T, 4], F32, name="relu_s%d" % g, offset=16 * T * g)
+            for u in range(4):
+                dst, src = relus[g][:, P * u : P * (u + 1), :], pres[g, u][:].rearrange("p t s -> p s t")
+                if 4 * g + u in VECTOR_RELUS:
+                    nc.vector.tensor_scalar_max(dst, src, 0.0)
                 else:
-                    nc.scalar.activation(relus[g][:, t, :], pres[g, t][:], ACT.Relu)
+                    nc.scalar.activation(dst, src, ACT.Relu)
 
         def shared_square(g):
-            nc.scalar.activation(
-                hsb[g][:].rearrange("p (c i) t -> p c t i", i=4),
-                relus[g][:].rearrange("p t (c i) -> p c t i", i=4), ACT.Square,
-            )
+            nc.scalar.activation(hsb[g][:], relus[g][:], ACT.Square)
 
         def shared_quantize(g):
             nc.vector.quantize_mx(

@@ -22,11 +22,10 @@ PASS = 512
 G = HS // PASS
 HALF = T // 2
 WARM_PASSES = 3
-SHARED_BANKS = (0, 1, 2, 3, 4, 5, 6, 0)
 SCALAR_TOKENS = 192
-FINISH = (0, 3, 1, 2)
-PACKED_AT = 40 * T
-VECTOR_RELUS = (2, 3)
+VECTOR_RELUS = (0, 1)
+ROW_ORDER = (2, 0, 3, 1)
+SUM_ORDER = (0, 2, 1, 3)
 
 
 def tile_moe_shf_mlp_relu2_kernel(
@@ -36,7 +35,6 @@ def tile_moe_shf_mlp_relu2_kernel(
     nc = tc.nc
     with ExitStack() as ctx:
         keep = ctx.enter_context(tc.tile_pool(name="keep", bufs=1))
-        late = ctx.enter_context(tc.tile_pool(name="late", bufs=1))
         psum = ctx.enter_context(tc.psum_pool(name="psum", bufs=1))
 
         def held(shape, dtype, name):
@@ -49,7 +47,7 @@ def tile_moe_shf_mlp_relu2_kernel(
         xw = held([P, T], I32, "xw")
         xs = held([P, T], U8, "xs")
         w1sc = held([P, E * H], U8, "w1sc")
-        packed = late.tile([P, PASS], U8, name="packed", offset=PACKED_AT)
+        packed = held([P, PASS], U8, "packed")
         ident = held([P, P], F32, "ident")
         w1ssc = held([P, PASS], U8, "w1ssc")
         nc.gpsimd.memset(xs[:].bitcast(I32), 0)
@@ -65,26 +63,20 @@ def tile_moe_shf_mlp_relu2_kernel(
         def load_words(tile, words):
             nc.sync.dma_start(out=tile[:].bitcast(I32), in_=words[:, 0].rearrange("e p b -> p e b").bitcast(I32))
 
-        def load_expert_scales(queue, tile, scales, q):
-            queue.dma_start(
-                out=tile[32 * q : 32 * q + 4, :].bitcast(I32).rearrange("r (e n) -> r e n", e=E),
-                in_=scales[:, 0, 4 * q : 4 * q + 4, :].rearrange("e r n -> r e n").bitcast(I32),
-            )
-
-        def load_x_scales(q):
+        nc.sync.dma_start(offsets[:], offs)
+        nc.sync.dma_start(out=xw[:], in_=x_words[0].rearrange("p t d -> p (t d)").bitcast(I32))
+        for q in range(4):
             nc.sync.dma_start(
                 out=xs[32 * q : 32 * q + 4, :].bitcast(I32),
                 in_=x_scales[0, 4 * q : 4 * q + 4, :].bitcast(I32),
             )
-
-        nc.sync.dma_start(offsets[:], offs)
-        nc.sync.dma_start(out=xw[:], in_=x_words[0].rearrange("p t d -> p (t d)").bitcast(I32))
-        for q in range(4):
-            load_x_scales(q)
         load_words(w1w, w1_words)
         nc.sync.dma_start(out=w1sw[:], in_=w1s_words[0].rearrange("p l d -> p (l d)").bitcast(I32))
         for q in range(4):
-            load_expert_scales(nc.sync, w1sc, w1_scales, q)
+            nc.sync.dma_start(
+                out=w1sc[32 * q : 32 * q + 4, :].bitcast(I32).rearrange("r (e n) -> r e n", e=E),
+                in_=w1_scales[:, 0, 4 * q : 4 * q + 4, :].rearrange("e r n -> r e n").bitcast(I32),
+            )
         for q in range(4):
             nc.sync.dma_start(
                 out=w1ssc[32 * q : 32 * q + 4 * G, :].bitcast(I32),
@@ -102,16 +94,17 @@ def tile_moe_shf_mlp_relu2_kernel(
 
         xg = [held([P, C], U32, "xg0"), held([P, 3 * C], U32, "xg1")]
         xgs = [held([P, C], U8, "xgs0"), held([P, 3 * C], U8, "xgs1")]
-        w2p = {}
+        w2p = held([P, E, 2 * N], U8, "w2p")
         w2scp = held([P, E * N], U8, "w2scp")
         w2sscp = held([P, G * N], U8, "w2sscp")
         sorted_rows = held([P, PASS], U8, "sorted_rows")
-        hb = [held([P, 2 * C, 4], BF16, "hb%d" % a) for a in range(2)]
-        hq = {}
-        hsc = [held([P, 2 * C], U8, "hsc%d" % a) for a in range(2)]
-        win = [held([P, T], F32, "win%d" % t) for t in range(2)]
+        hb = held([P, E * C, 4], BF16, "hb")
+        hq = held([P, E * C], U32, "hq")
+        hsc = held([P, E * C], U8, "hsc")
         w1sp = held([P, HS], I32, "w1sp")
+        w2sp = held([P, HS], I32, "w2sp")
         w1sscp = held([P, PASS], U8, "w1sscp")
+        relu_s = [held([P, T, 4], F32, "relu_s%d" % g) for g in range(G)]
         hsb = [held([P, T, 4], BF16, "hsb%d" % g) for g in range(G)]
         hsq = [held([P, T], U32, "hsq%d" % g) for g in range(G)]
         hssc = [held([P, T], U8, "hssc%d" % g) for g in range(G)]
@@ -129,11 +122,6 @@ def tile_moe_shf_mlp_relu2_kernel(
             nc.vector.tensor_copy(xg[a][:], xw[:].bitcast(U32).indirect(slots(first, count)))
             nc.vector.tensor_copy(xgs[a][:], xs[:].indirect(slots(first, count)))
 
-        def deal_words(a):
-            w2p[a] = held([P, 2, 2 * N], U8, "w2p%d" % a)
-            deal(w2p[a][:].rearrange("p e b -> p (e b)").bitcast(U16),
-                 w2w[:, 2 * a : 2 * a + 2, :].rearrange("p e b -> p (e b)").bitcast(U16), 8)
-
         def place_planes(tile, first, count):
             for q in range(4):
                 nc.sync.dma_start(
@@ -141,85 +129,53 @@ def tile_moe_shf_mlp_relu2_kernel(
                     in_=sorted_rows[first + 4 * count * q : first + 4 * count * (q + 1), :].bitcast(I32),
                 )
 
-        turned = {}
-
-        def routed_relu(e):
-            a, cols = min(e, 1), slice(C * max(e - 1, 0), C * (max(e - 1, 0) + 1))
-            pre = bank(e, [P, H])
-            nc.tensor.matmul_mx(
-                out=pre[:], lhsT=xg[a][:, cols].bitcast(FP8X4), lhsT_scale=xgs[a][:, cols],
-                rhs=w1w[:, e, :].bitcast(FP4X4), rhs_scale=w1sc[:, H * e : H * (e + 1)],
-                start=True, stop=True,
-            )
-            if e == 3:
-                relu = late.tile([P, 4, P], F32, name="relu_r3", offset=PACKED_AT + 256 - 16 * P)
-            else:
-                relu = held([P, 4, P], F32, "relu_r%d" % e)
-            dst, src = relu[:].rearrange("s t p -> s p t"), pre[:].rearrange("s (p t) -> s p t", t=4)
-            if e % 2:
+        def relu(on_vector, dst, src):
+            if on_vector:
                 nc.vector.tensor_scalar_max(dst, src, 0.0)
             else:
                 nc.scalar.activation(dst, src, ACT.Relu)
-            turned[e] = bank(4 + e, [P, 4, C])
-            for t in range(4):
-                nc.tensor.transpose(turned[e][:, t, :], relu[:, t, :], ident[:])
 
-        def h_place(e):
-            return e // 2, slice(C * (e % 2), C * (e % 2 + 1))
+        pre_r, turned, pre_s = {}, {}, {}
 
-        def routed_square(e):
-            a, cols = h_place(e)
-            nc.scalar.activation(hb[a][:, cols, :], turned[e][:].rearrange("p t s -> p s t"), ACT.Square)
-
-        def routed_quantize(a):
-            nc.vector.quantize_mx(
-                out=hq[a][:].bitcast(FP8X4), scales=hsc[a][:], in_=hb[a][:].rearrange("p s t -> p (s t)")
-            )
-
-        def routed_second(e, t, out):
-            a, cols = h_place(e)
+        def routed_first(e):
+            a, cols = min(e, 1), slice(C * max(e - 1, 0), C * (max(e - 1, 0) + 1))
+            pre_r[e] = bank(e, [P, H])
             nc.tensor.matmul_mx(
-                out=out,
-                lhsT=w2p[e // 2][:, e % 2, 2 * P * t : 2 * P * (t + 1)].bitcast(FP4X4),
-                lhsT_scale=w2scp[:, N * e + P * t : N * e + P * (t + 1)],
-                rhs=hq[a][:, cols].bitcast(FP8X4), rhs_scale=hsc[a][:, cols],
+                out=pre_r[e][:], lhsT=xg[a][:, cols].bitcast(FP8X4), lhsT_scale=xgs[a][:, cols],
+                rhs=w1w[:, e, :].bitcast(FP4X4), rhs_scale=w1sc[:, H * e : H * (e + 1)],
                 start=True, stop=True,
             )
 
-        relus = {}
-        pres = {}
+        def routed_relu(e):
+            sorted_relu = held([P, 4, P], F32, "relu_r%d" % e)
+            relu(e % 2, sorted_relu[:].rearrange("s t p -> s p t"), pre_r[e][:].rearrange("s (p t) -> s p t", t=4))
+            turned[e] = bank(4 + e, [P, 4, C])
+            for t in range(4):
+                nc.tensor.transpose(turned[e][:, t, :], sorted_relu[:, t, :], ident[:])
 
-        def over_relu(g, part, columns, name):
-            return late.tile([P, columns], F32, name=name, offset=4 * T * (4 * g + part))
-
-        def shared_first(g, quarters):
-            for u in quarters:
-                pres[g, u] = bank(SHARED_BANKS[4 * g + u], [P, 4, P])
-                for t in range(4):
-                    nc.tensor.matmul_mx(
-                        out=pres[g, u][:, t, :],
-                        lhsT=w1sp[:, PASS * g + P * t : PASS * g + P * (t + 1)].bitcast(FP8X4),
-                        lhsT_scale=w1sscp[4 * g : P, P * t : P * (t + 1)],
-                        rhs=xw[:, P * u : P * (u + 1)].bitcast(FP8X4), rhs_scale=xs[:, P * u : P * (u + 1)],
-                        start=True, stop=True,
-                    )
-
-        def shared_relus(g):
-            relus[g] = late.tile([P, T, 4], F32, name="relu_s%d" % g, offset=16 * T * g)
-            for u in range(4):
-                dst, src = relus[g][:, P * u : P * (u + 1), :], pres[g, u][:].rearrange("p t s -> p s t")
-                if 4 * g + u in VECTOR_RELUS:
-                    nc.vector.tensor_scalar_max(dst, src, 0.0)
-                else:
-                    nc.scalar.activation(dst, src, ACT.Relu)
-
-        def shared_square(g):
-            nc.scalar.activation(hsb[g][:], relus[g][:], ACT.Square)
-
-        def shared_quantize(g):
-            nc.vector.quantize_mx(
-                out=hsq[g][:].bitcast(FP8X4), scales=hssc[g][:], in_=hsb[g][:].rearrange("p s t -> p (s t)")
+        def routed_square(e):
+            nc.scalar.activation(
+                hb[:, C * e : C * (e + 1), :], turned[e][:].rearrange("p t s -> p s t"), ACT.Square
             )
+
+        def shared_first(step):
+            g, u = divmod(step, 4)
+            pre_s[step] = bank(step, [P, 4, P])
+            for t in range(4):
+                nc.tensor.matmul_mx(
+                    out=pre_s[step][:, t, :],
+                    lhsT=w1sp[:, PASS * g + P * t : PASS * g + P * (t + 1)].bitcast(FP8X4),
+                    lhsT_scale=w1sscp[4 * g : P, P * t : P * (t + 1)],
+                    rhs=xw[:, P * u : P * (u + 1)].bitcast(FP8X4), rhs_scale=xs[:, P * u : P * (u + 1)],
+                    start=True, stop=True,
+                )
+
+        def shared_relu(step):
+            g, u = divmod(step, 4)
+            relu(step in VECTOR_RELUS, relu_s[g][:, P * u : P * (u + 1), :], pre_s[step][:].rearrange("p t s -> p s t"))
+
+        def quantize(codes, scales, values):
+            nc.vector.quantize_mx(out=codes.bitcast(FP8X4), scales=scales, in_=values.rearrange("p s t -> p (s t)"))
 
         warm = bank(7, [P, T])
         for repeat in range(WARM_PASSES):
@@ -228,90 +184,74 @@ def tile_moe_shf_mlp_relu2_kernel(
                 rhs=xw[:].bitcast(FP8X4), rhs_scale=xs[:], start=True, stop=True,
             )
 
-        def gated(out, sums, a):
-            rows = sums.shape[1] // (2 * C)
-            nc.vector.tensor_tensor(
-                out.rearrange("p (t s) -> p t s", t=rows), sums.rearrange("p (t s) -> p t s", t=rows),
-                gates[:, 2 * C * a : 2 * C * (a + 1)].unsqueeze(1).to_broadcast([P, rows, 2 * C]), ALU.mult,
-            )
-
-        def scatter_vector(first, t, values):
-            nc.vector.tensor_copy(win[t][:].indirect(slots(first, values.shape[1] // C)), values)
-
-        def scatter_scalar(first, t, values):
-            nc.scalar.activation(win[t][:].indirect(slots(first, values.shape[1] // C)), values, ACT.Copy)
-
-        def second_pair(a, first_t, number, rows=2):
-            out = bank(number, [P, 2 * C * rows])
-            for t in range(rows):
-                for e in range(2):
-                    at = C * (2 * t + e)
-                    routed_second(2 * a + e, first_t + t, out[:, at : at + C])
-            return out
-
-        lo, hi = slice(0, 2 * C), slice(2 * C, 4 * C)
         gather(0, 0, 1)
         gather(1, 1, 3)
+        for e in range(E):
+            routed_first(e)
+        deal(w1sp[:], w1sw[:], 4)
+        deal(w1sscp[:], w1ssc[:], 16)
+        for e in range(E):
+            routed_relu(e)
         deal(sorted_rows[:], packed[:], 16)
         place_planes(w2scp, 0, E)
         nc.sync.dma_start(out=w2sw[:], in_=w2s_words.rearrange("g p n d -> p g (n d)").bitcast(I32))
         place_planes(w2sscp, 64, G)
-        routed_relu(0)
-        routed_relu(1)
-        routed_relu(2)
-        deal(w1sp[:], w1sw[:], 4)
-        deal(w1sscp[:], w1ssc[:], 16)
-        routed_relu(3)
-        routed_square(0)
-        routed_square(1)
-        deal_words(0)
-        hq[0] = late.tile([P, 2 * C], U32, name="hq0", offset=PACKED_AT + 256, align_bytes=64)
-        routed_quantize(0)
-        routed_square(2)
-        routed_square(3)
-        shared_first(0, range(4))
-        deal_words(1)
-        shared_relus(0)
-        first = [second_pair(0, t, 5 + t, 1) for t in range(2)]
-        second = second_pair(0, 2, 0)
-        ya = [held([P, 2 * C], F32, "ya%d" % t) for t in range(2)]
-        for t in range(2):
-            gated(ya[t][:], first[t][:], 0)
-        yb = held([P, 4 * C], F32, "yb")
-        gated(yb[:], second[:], 0)
-        for t in range(2):
-            scatter_vector(0, t, ya[t][:])
-        hq[1] = held([P, 2 * C], U32, "ya0")
-        routed_quantize(1)
-        w2sp = held([P, HS], I32, "ya1")
-        deal(w2sp[:], w2sw[:].rearrange("p g n -> p (g n)"), 4)
-        shared_first(1, range(4))
-        shared_relus(1)
-        third = second_pair(1, 0, 5)
-        fourth = second_pair(1, 2, 6)
-        yc = held([P, 2 * C], F32, "yc")
-        gated(yc[:], third[:, lo], 1)
-        yd = held([P, 4 * C], F32, "yd")
-        gated(yd[:], fourth[:], 1)
-        scatter_vector(2, 0, yc[:])
-        shared_square(0)
-        shared_square(1)
-        shared_quantize(0)
-        for t in range(2):
-            win.append(over_relu(0, 1 + t, T, "win%d" % (2 + t)))
-        scatter_vector(0, 2, yb[:, 0:C])
-        scatter_scalar(0, 3, yb[:, hi])
-        scatter_scalar(2, 3, yd[:, hi])
-        scatter_scalar(1, 2, yb[:, C : 2 * C])
-        scatter_scalar(2, 2, yd[:, lo])
-        ye = over_relu(1, 0, 2 * C, "ye")
-        gated(ye[:], third[:, hi], 1)
-        shared_quantize(1)
-        scatter_vector(2, 1, ye[:])
+        for e in range(E):
+            routed_square(e)
+        for step in range(4):
+            shared_first(step)
+        for a in range(2):
+            deal(w2p[:, 2 * a : 2 * a + 2, :].rearrange("p e b -> p (e b)").bitcast(U16),
+                 w2w[:, 2 * a : 2 * a + 2, :].rearrange("p e b -> p (e b)").bitcast(U16), 8)
+        quantize(hq[:], hsc[:], hb[:])
+        for step in range(4):
+            shared_relu(step)
+        for step in range(4, 8):
+            shared_first(step)
 
-        ys = [bank(b, [P, T]) for b in (1, 2, 3, 4)]
+        y = {}
+        for place, t in enumerate(ROW_ORDER):
+            sums = bank(place, [P, T])
+            for e in range(E):
+                cols = slice(C * e, C * (e + 1))
+                nc.tensor.matmul_mx(
+                    out=sums[:, cols],
+                    lhsT=w2p[:, e, 2 * P * t : 2 * P * (t + 1)].bitcast(FP4X4),
+                    lhsT_scale=w2scp[:, N * e + P * t : N * e + P * (t + 1)],
+                    rhs=hq[:, cols].bitcast(FP8X4), rhs_scale=hsc[:, cols],
+                    start=True, stop=True,
+                )
+            y[t] = held([P, T], F32, "y%d" % t)
+            nc.vector.tensor_tensor(y[t][:], sums[:], gates[:], ALU.mult)
+
+        for step in range(4, 8):
+            shared_relu(step)
         for g in range(G):
-            for t in FINISH:
+            nc.scalar.activation(hsb[g][:], relu_s[g][:], ACT.Square)
+        deal(w2sp[:], w2sw[:].rearrange("p g n -> p (g n)"), 4)
+
+        def scatter(on_vector, window, values):
+            for a in range(2):
+                out, in_ = window[:].indirect(slots(2 * a, 2)), values[:, HALF * a : HALF * (a + 1)]
+                if on_vector:
+                    nc.vector.tensor_copy(out, in_)
+                else:
+                    nc.scalar.activation(out, in_, ACT.Copy)
+
+        win = {}
+        win[0] = held([P, T], F32, "win0")
+        scatter(True, win[0], y[0])
+        for g in range(G):
+            quantize(hsq[g][:], hssc[g][:], hsb[g][:])
+        win[1] = held([P, T], F32, "hsb1")
+        scatter(True, win[1], y[1])
+        for t in (2, 3):
+            win[t] = held([P, T], F32, "win%d" % t)
+            scatter(False, win[t], y[t])
+
+        ys = {t: bank(4 + place, [P, T]) for place, t in enumerate(SUM_ORDER)}
+        for g in range(G):
+            for t in SUM_ORDER:
                 nc.tensor.matmul_mx(
                     out=ys[t][:],
                     lhsT=w2sp[:, PASS * g + P * t : PASS * g + P * (t + 1)].bitcast(FP8X4),
@@ -322,7 +262,7 @@ def tile_moe_shf_mlp_relu2_kernel(
 
         total = held([P, 4, T], F32, "total")
         rows = out_0.rearrange("(p t) c -> p t c", t=4)
-        for t in FINISH:
+        for t in SUM_ORDER:
             nc.vector.tensor_tensor(total[:, t, :], ys[t][:], win[t][:], ALU.add)
             nc.sync.dma_start(out=rows[:, t, :], in_=total[:, t, :])
 
@@ -341,9 +281,7 @@ def tile_moe_shf_mlp_relu2_kernel(
         nc.vector.tensor_copy(*rounded(1, SCALAR_TOKENS, HALF))
         for a in range(2):
             cols = slice(HALF * a, HALF * (a + 1))
-            nc.vector.quantize_mx(
-                out=oq[:, cols].bitcast(FP8X4), scales=osc[:, cols], in_=ob[a][:].rearrange("p s t -> p (s t)")
-            )
+            quantize(oq[:, cols], osc[:, cols], ob[a][:])
             nc.sync.dma_start(out=words_out[:, cols], in_=oq[:, cols].bitcast(I32))
         for q in range(4):
             (nc.sync if q == 3 else nc.scalar).dma_start(

@@ -21,11 +21,14 @@ P = 128
 PASS = 512
 G = HS // PASS
 HALF = T // 2
-WARM_PASSES = 3
+WARM_PASSES = 2
+EXTRA_SLOTS = 64
 SCALAR_TOKENS = 192
-VECTOR_RELUS = (0, 1)
-ROW_ORDER = (2, 0, 3, 1)
+ROW_ORDER = (2, 3, 1, 0)
 SUM_ORDER = (0, 2, 1, 3)
+SHARED_BANKS = (0, 7, 1, 0, 3, 4, 2, 1)
+RESULT_BANKS = (2, 1, 7, 0)
+SUM_BANKS = (5, 6, 3, 4)
 
 
 def tile_moe_shf_mlp_relu2_kernel(
@@ -35,6 +38,7 @@ def tile_moe_shf_mlp_relu2_kernel(
     nc = tc.nc
     with ExitStack() as ctx:
         keep = ctx.enter_context(tc.tile_pool(name="keep", bufs=1))
+        late = ctx.enter_context(tc.tile_pool(name="late", bufs=1))
         psum = ctx.enter_context(tc.psum_pool(name="psum", bufs=1))
 
         def held(shape, dtype, name):
@@ -55,10 +59,10 @@ def tile_moe_shf_mlp_relu2_kernel(
         nc.vector.memset(w1ssc[:].bitcast(I32), 0)
 
         w1w = held([P, E, 2 * H], U8, "w1w")
-        w2w = held([P, E, 2 * N], U8, "w2w")
+        w2w = late.tile([P, E, 2 * N], U8, name="w2w", offset=16 * T, align_bytes=64)
         w1sw = held([P, HS], I32, "w1sw")
         w2sw = held([P, G, N], I32, "w2sw")
-        gates = held([P, T], F32, "gates")
+        gates = late.tile([P, T], F32, name="gates", offset=40 * T)
 
         def load_words(tile, words):
             nc.sync.dma_start(out=tile[:].bitcast(I32), in_=words[:, 0].rearrange("e p b -> p e b").bitcast(I32))
@@ -70,8 +74,8 @@ def tile_moe_shf_mlp_relu2_kernel(
                 out=xs[32 * q : 32 * q + 4, :].bitcast(I32),
                 in_=x_scales[0, 4 * q : 4 * q + 4, :].bitcast(I32),
             )
-        load_words(w1w, w1_words)
         nc.sync.dma_start(out=w1sw[:], in_=w1s_words[0].rearrange("p l d -> p (l d)").bitcast(I32))
+        load_words(w1w, w1_words)
         for q in range(4):
             nc.sync.dma_start(
                 out=w1sc[32 * q : 32 * q + 4, :].bitcast(I32).rearrange("r (e n) -> r e n", e=E),
@@ -89,6 +93,7 @@ def tile_moe_shf_mlp_relu2_kernel(
             out=packed[64:96, :].bitcast(I32), in_=w2s_scales.rearrange("g b n -> b g n").bitcast(I32)
         )
         load_words(w2w, w2_words)
+        nc.sync.dma_start(out=w2sw[:], in_=w2s_words.rearrange("g p n d -> p g (n d)").bitcast(I32))
         nc.sync.dma_start(out=gates[:], in_=gate)
         make_identity(nc, ident[:])
 
@@ -98,22 +103,22 @@ def tile_moe_shf_mlp_relu2_kernel(
         w2scp = held([P, E * N], U8, "w2scp")
         w2sscp = held([P, G * N], U8, "w2sscp")
         sorted_rows = held([P, PASS], U8, "sorted_rows")
-        hb = held([P, E * C, 4], BF16, "hb")
-        hq = held([P, E * C], U32, "hq")
+        hb = [held([P, 2 * C, 4], BF16, "hb%d" % a) for a in range(2)]
+        hq = late.tile([P, E * C], U32, name="hq", offset=16 * T, align_bytes=64)
         hsc = held([P, E * C], U8, "hsc")
         w1sp = held([P, HS], I32, "w1sp")
         w2sp = held([P, HS], I32, "w2sp")
         w1sscp = held([P, PASS], U8, "w1sscp")
-        relu_s = [held([P, T, 4], F32, "relu_s%d" % g) for g in range(G)]
-        hsb = [held([P, T, 4], BF16, "hsb%d" % g) for g in range(G)]
-        hsq = [held([P, T], U32, "hsq%d" % g) for g in range(G)]
+        relu_a = late.tile([P, HALF, 4], F32, name="relu_a", offset=20 * T)
+        relu_b = held([P, 4, HALF], F32, "relu_b")
+        relu_c = late.tile([P, 4, T], F32, name="relu_c", offset=0)
         hssc = [held([P, T], U8, "hssc%d" % g) for g in range(G)]
 
         def slots(first, count):
             return offsets[:, first * (C // 16) : (first + count) * (C // 16)]
 
-        def deal(out, in_, run):
-            nc.vector.tensor_copy(
+        def deal(out, in_, run, copy=nc.vector.tensor_copy):
+            copy(
                 out=out.rearrange("p (g t c i) -> p g c t i", t=4, c=P // run, i=run),
                 in_=in_.rearrange("p (g c i t) -> p g c t i", t=4, c=P // run, i=run),
             )
@@ -148,70 +153,96 @@ def tile_moe_shf_mlp_relu2_kernel(
 
         def routed_relu(e):
             sorted_relu = held([P, 4, P], F32, "relu_r%d" % e)
-            relu(e % 2, sorted_relu[:].rearrange("s t p -> s p t"), pre_r[e][:].rearrange("s (p t) -> s p t", t=4))
+            relu(e % 2 == 0, sorted_relu[:].rearrange("s t p -> s p t"), pre_r[e][:].rearrange("s (p t) -> s p t", t=4))
             turned[e] = bank(4 + e, [P, 4, C])
             for t in range(4):
                 nc.tensor.transpose(turned[e][:, t, :], sorted_relu[:, t, :], ident[:])
 
         def routed_square(e):
             nc.scalar.activation(
-                hb[:, C * e : C * (e + 1), :], turned[e][:].rearrange("p t s -> p s t"), ACT.Square
+                hb[e // 2][:, C * (e % 2) : C * (e % 2 + 1), :], turned[e][:].rearrange("p t s -> p s t"), ACT.Square
+            )
+
+        def shared_pass(out, g, t, first, count):
+            nc.tensor.matmul_mx(
+                out=out,
+                lhsT=w1sp[:, PASS * g + P * t : PASS * g + P * (t + 1)].bitcast(FP8X4),
+                lhsT_scale=w1sscp[4 * g : P, P * t : P * (t + 1)],
+                rhs=xw[:, first : first + count].bitcast(FP8X4), rhs_scale=xs[:, first : first + count],
+                start=True, stop=True,
             )
 
         def shared_first(step):
-            g, u = divmod(step, 4)
-            pre_s[step] = bank(step, [P, 4, P])
-            for t in range(4):
-                nc.tensor.matmul_mx(
-                    out=pre_s[step][:, t, :],
-                    lhsT=w1sp[:, PASS * g + P * t : PASS * g + P * (t + 1)].bitcast(FP8X4),
-                    lhsT_scale=w1sscp[4 * g : P, P * t : P * (t + 1)],
-                    rhs=xw[:, P * u : P * (u + 1)].bitcast(FP8X4), rhs_scale=xs[:, P * u : P * (u + 1)],
-                    start=True, stop=True,
-                )
+            pre_s[step] = bank(SHARED_BANKS[step], [P, T])
+            if step < 2:
+                for t in range(4):
+                    shared_pass(pre_s[step][:, P * t : P * (t + 1)], 0, t, P * step, P)
+            elif step < 4:
+                for place in range(2):
+                    shared_pass(pre_s[step][:, HALF * place : HALF * (place + 1)], 0, 2 * (step - 2) + place, HALF, HALF)
+            else:
+                shared_pass(pre_s[step][:], 1, step - 4, 0, T)
 
         def shared_relu(step):
-            g, u = divmod(step, 4)
-            relu(step in VECTOR_RELUS, relu_s[g][:, P * u : P * (u + 1), :], pre_s[step][:].rearrange("p t s -> p s t"))
+            if step < 2:
+                relu(True, relu_a[:, P * step : P * (step + 1), :], pre_s[step][:].rearrange("p (t s) -> p s t", t=4))
+            elif step < 4:
+                out = relu_b[:, 2 * (step - 2) : 2 * (step - 1), :].rearrange("p t s -> p (t s)")
+                relu(step == 3, out, pre_s[step][:])
+            else:
+                relu(False, relu_c[:, step - 4, :], pre_s[step][:])
+
+        def square(out, values):
+            nc.scalar.activation(
+                out.rearrange("p (c i) t -> p c t i", i=4), values.rearrange("p t (c i) -> p c t i", i=4), ACT.Square
+            )
 
         def quantize(codes, scales, values):
             nc.vector.quantize_mx(out=codes.bitcast(FP8X4), scales=scales, in_=values.rearrange("p s t -> p (s t)"))
 
+        warm_scales = held([P, T], U8, "warm_scales")
+        nc.vector.tensor_copy(warm_scales[:].bitcast(I32), xs[:].bitcast(I32))
         warm = bank(7, [P, T])
         for repeat in range(WARM_PASSES):
             nc.tensor.matmul_mx(
-                out=warm[:], lhsT=xw[:, 0:P].bitcast(FP8X4), lhsT_scale=xs[:, 0:P],
-                rhs=xw[:].bitcast(FP8X4), rhs_scale=xs[:], start=True, stop=True,
+                out=warm[:], lhsT=w1sw[:, 0:P].bitcast(FP8X4), lhsT_scale=warm_scales[:, 0:P],
+                rhs=w1sw[:, 0:T].bitcast(FP8X4), rhs_scale=warm_scales[:], start=True, stop=True,
             )
 
         gather(0, 0, 1)
         gather(1, 1, 3)
         for e in range(E):
             routed_first(e)
-        deal(w1sp[:], w1sw[:], 4)
+        deal(w1sp[:].bitcast(U32), w1sw[:].bitcast(U32), 4, nc.scalar.copy)
         deal(w1sscp[:], w1ssc[:], 16)
         for e in range(E):
             routed_relu(e)
         deal(sorted_rows[:], packed[:], 16)
         place_planes(w2scp, 0, E)
-        nc.sync.dma_start(out=w2sw[:], in_=w2s_words.rearrange("g p n d -> p g (n d)").bitcast(I32))
         place_planes(w2sscp, 64, G)
         for e in range(E):
             routed_square(e)
-        for step in range(4):
+        for step in (0, 2, 4, 1, 5):
             shared_first(step)
         for a in range(2):
             deal(w2p[:, 2 * a : 2 * a + 2, :].rearrange("p e b -> p (e b)").bitcast(U16),
                  w2w[:, 2 * a : 2 * a + 2, :].rearrange("p e b -> p (e b)").bitcast(U16), 8)
-        quantize(hq[:], hsc[:], hb[:])
-        for step in range(4):
+        quantize(hq[:, 0:HALF], hsc[:, 0:HALF], hb[0][:])
+        deal(w2sp[:], w2sw[:].rearrange("p g n -> p (g n)"), 4)
+        shared_relu(0)
+        quantize(hq[:, HALF:T], hsc[:, HALF:T], hb[1][:])
+        hsb = [held([P, T, 4], BF16, name) for name in ("hb1", "hsb1")]
+        shared_first(3)
+        for step in (1, 2, 4, 5, 3):
             shared_relu(step)
-        for step in range(4, 8):
-            shared_first(step)
+        for u in range(2):
+            values = relu_a[:, P * u : P * (u + 1), :]
+            nc.gpsimd.tensor_tensor(hsb[0][:, P * u : P * (u + 1), :], values, values, ALU.mult)
+        square(hsb[0][:, HALF:T, :], relu_b[:])
 
         y = {}
         for place, t in enumerate(ROW_ORDER):
-            sums = bank(place, [P, T])
+            sums = bank(RESULT_BANKS[place], [P, T])
             for e in range(E):
                 cols = slice(C * e, C * (e + 1))
                 nc.tensor.matmul_mx(
@@ -224,32 +255,35 @@ def tile_moe_shf_mlp_relu2_kernel(
             y[t] = held([P, T], F32, "y%d" % t)
             nc.vector.tensor_tensor(y[t][:], sums[:], gates[:], ALU.mult)
 
-        for step in range(4, 8):
+        for step in range(6, 8):
+            shared_first(step)
             shared_relu(step)
-        for g in range(G):
-            nc.scalar.activation(hsb[g][:], relu_s[g][:], ACT.Square)
-        deal(w2sp[:], w2sw[:].rearrange("p g n -> p (g n)"), 4)
+        square(hsb[1][:], relu_c[:])
 
-        def scatter(on_vector, window, values):
-            for a in range(2):
-                out, in_ = window[:].indirect(slots(2 * a, 2)), values[:, HALF * a : HALF * (a + 1)]
-                if on_vector:
-                    nc.vector.tensor_copy(out, in_)
-                else:
-                    nc.scalar.activation(out, in_, ACT.Copy)
+        def scatter(on_vector, t, first, last):
+            out, in_ = win[t][:].indirect(offsets[:, first // 16 : last // 16]), y[t][:, first:last]
+            if on_vector:
+                nc.vector.tensor_copy(out, in_)
+            else:
+                nc.scalar.activation(out, in_, ACT.Copy)
 
-        win = {}
+        win = {t: late.tile([P, T], F32, name="win%d" % t, offset=4 * T * t) for t in (2, 3)}
         win[0] = held([P, T], F32, "win0")
-        scatter(True, win[0], y[0])
+        scatter(True, 0, 0, HALF)
+        scatter(True, 0, HALF, T)
+        hsq = [late.tile([P, T], U32, name="hsq0", offset=38 * T, align_bytes=64), held([P, T], U32, "hsq1")]
         for g in range(G):
             quantize(hsq[g][:], hssc[g][:], hsb[g][:])
         win[1] = held([P, T], F32, "hsb1")
-        scatter(True, win[1], y[1])
-        for t in (2, 3):
-            win[t] = held([P, T], F32, "win%d" % t)
-            scatter(False, win[t], y[t])
+        scatter(True, 3, 0, EXTRA_SLOTS)
+        scatter(True, 1, 0, HALF)
+        scatter(True, 1, HALF, T)
+        scatter(False, 2, 0, HALF)
+        scatter(False, 2, HALF, T)
+        scatter(False, 3, EXTRA_SLOTS, HALF)
+        scatter(False, 3, HALF, T)
 
-        ys = {t: bank(4 + place, [P, T]) for place, t in enumerate(SUM_ORDER)}
+        ys = {t: bank(SUM_BANKS[place], [P, T]) for place, t in enumerate(SUM_ORDER)}
         for g in range(G):
             for t in SUM_ORDER:
                 nc.tensor.matmul_mx(

@@ -22,13 +22,15 @@ PASS = 512
 G = HS // PASS
 HALF = T // 2
 WARM_PASSES = 2
-EXTRA_SLOTS = 64
 SCALAR_TOKENS = 192
 ROW_ORDER = (2, 3, 1, 0)
-SUM_ORDER = (0, 2, 1, 3)
-SHARED_BANKS = (0, 7, 1, 0, 3, 4, 2, 1)
-RESULT_BANKS = (2, 1, 7, 0)
-SUM_BANKS = (5, 6, 3, 4)
+SUM_ORDER = (2, 3, 0, 1)
+SCALAR_SLOTS = 288
+POOL_TOKENS = 448
+WIDE_WINDOW = 704
+SHARED_BANKS = (0, 7, 7, 0, 3, 4, 5, 0)
+RESULT_BANKS = (1, 2, 3, 4)
+SUM_BANKS = (5, 6, 0, 7)
 
 
 def tile_moe_shf_mlp_relu2_kernel(
@@ -109,8 +111,7 @@ def tile_moe_shf_mlp_relu2_kernel(
         w1sp = held([P, HS], I32, "w1sp")
         w2sp = held([P, HS], I32, "w2sp")
         w1sscp = held([P, PASS], U8, "w1sscp")
-        relu_a = late.tile([P, HALF, 4], F32, name="relu_a", offset=20 * T)
-        relu_b = held([P, 4, HALF], F32, "relu_b")
+        relu_a = late.tile([P, T, 4], F32, name="relu_a", offset=20 * T)
         relu_c = late.tile([P, 4, T], F32, name="relu_c", offset=0)
         hssc = [held([P, T], U8, "hssc%d" % g) for g in range(G)]
 
@@ -174,23 +175,18 @@ def tile_moe_shf_mlp_relu2_kernel(
 
         def shared_first(step):
             pre_s[step] = bank(SHARED_BANKS[step], [P, T])
-            if step < 2:
+            if step < 4:
                 for t in range(4):
                     shared_pass(pre_s[step][:, P * t : P * (t + 1)], 0, t, P * step, P)
-            elif step < 4:
-                for place in range(2):
-                    shared_pass(pre_s[step][:, HALF * place : HALF * (place + 1)], 0, 2 * (step - 2) + place, HALF, HALF)
             else:
                 shared_pass(pre_s[step][:], 1, step - 4, 0, T)
 
         def shared_relu(step):
-            if step < 2:
-                relu(True, relu_a[:, P * step : P * (step + 1), :], pre_s[step][:].rearrange("p (t s) -> p s t", t=4))
-            elif step < 4:
-                out = relu_b[:, 2 * (step - 2) : 2 * (step - 1), :].rearrange("p t s -> p (t s)")
-                relu(step == 3, out, pre_s[step][:])
+            if step < 4:
+                out = relu_a[:, P * step : P * (step + 1), :]
+                relu(True, out, pre_s[step][:].rearrange("p (t s) -> p s t", t=4))
             else:
-                relu(False, relu_c[:, step - 4, :], pre_s[step][:])
+                relu(step == 7, relu_c[:, step - 4, :], pre_s[step][:])
 
         def square(out, values):
             nc.scalar.activation(
@@ -222,23 +218,25 @@ def tile_moe_shf_mlp_relu2_kernel(
         place_planes(w2sscp, 64, G)
         for e in range(E):
             routed_square(e)
-        for step in (0, 2, 4, 1, 5):
+        for step in (0, 4, 5, 6, 1):
             shared_first(step)
-        for a in range(2):
-            deal(w2p[:, 2 * a : 2 * a + 2, :].rearrange("p e b -> p (e b)").bitcast(U16),
-                 w2w[:, 2 * a : 2 * a + 2, :].rearrange("p e b -> p (e b)").bitcast(U16), 8)
+        deal(w2p[:].rearrange("p e b -> p (e b)").bitcast(U16), w2w[:].rearrange("p e b -> p (e b)").bitcast(U16), 8)
         quantize(hq[:, 0:HALF], hsc[:, 0:HALF], hb[0][:])
         deal(w2sp[:], w2sw[:].rearrange("p g n -> p (g n)"), 4)
         shared_relu(0)
         quantize(hq[:, HALF:T], hsc[:, HALF:T], hb[1][:])
         hsb = [held([P, T, 4], BF16, name) for name in ("hb1", "hsb1")]
-        shared_first(3)
-        for step in (1, 2, 4, 5, 3):
+        shared_relu(1)
+        for step in range(4, 7):
             shared_relu(step)
-        for u in range(2):
-            values = relu_a[:, P * u : P * (u + 1), :]
-            nc.gpsimd.tensor_tensor(hsb[0][:, P * u : P * (u + 1), :], values, values, ALU.mult)
-        square(hsb[0][:, HALF:T, :], relu_b[:])
+        for step in (7, 2, 3):
+            shared_first(step)
+            shared_relu(step)
+        square(hsb[1][:], relu_c[:])
+        for first in range(0, POOL_TOKENS, P):
+            cols = slice(first, min(first + P, POOL_TOKENS))
+            nc.gpsimd.tensor_tensor(hsb[0][:, cols, :], relu_a[:, cols, :], relu_a[:, cols, :], ALU.mult)
+        nc.scalar.activation(hsb[0][:, POOL_TOKENS:T, :], relu_a[:, POOL_TOKENS:T, :], ACT.Square)
 
         y = {}
         for place, t in enumerate(ROW_ORDER):
@@ -253,12 +251,8 @@ def tile_moe_shf_mlp_relu2_kernel(
                     start=True, stop=True,
                 )
             y[t] = held([P, T], F32, "y%d" % t)
-            nc.vector.tensor_tensor(y[t][:], sums[:], gates[:], ALU.mult)
+            nc.vector.tensor_tensor(y[t][:], gates[:], sums[:], ALU.mult)
 
-        for step in range(6, 8):
-            shared_first(step)
-            shared_relu(step)
-        square(hsb[1][:], relu_c[:])
 
         def scatter(on_vector, t, first, last):
             out, in_ = win[t][:].indirect(offsets[:, first // 16 : last // 16]), y[t][:, first:last]
@@ -268,36 +262,34 @@ def tile_moe_shf_mlp_relu2_kernel(
                 nc.scalar.activation(out, in_, ACT.Copy)
 
         win = {t: late.tile([P, T], F32, name="win%d" % t, offset=4 * T * t) for t in (2, 3)}
-        win[0] = held([P, T], F32, "win0")
-        scatter(True, 0, 0, HALF)
-        scatter(True, 0, HALF, T)
-        hsq = [late.tile([P, T], U32, name="hsq0", offset=38 * T, align_bytes=64), held([P, T], U32, "hsq1")]
-        for g in range(G):
+        hsq = [late.tile([P, T], U32, name="hsq%d" % g, offset=(38 + 4 * g) * T, align_bytes=64) for g in range(G)]
+        for g in (1, 0):
             quantize(hsq[g][:], hssc[g][:], hsb[g][:])
+        win[0] = held([P, WIDE_WINDOW], F32, "hb1")
         win[1] = held([P, T], F32, "hsb1")
-        scatter(True, 3, 0, EXTRA_SLOTS)
-        scatter(True, 1, 0, HALF)
-        scatter(True, 1, HALF, T)
+        scatter(True, 1, SCALAR_SLOTS, T)
+        scatter(True, 0, 0, T)
         scatter(False, 2, 0, HALF)
         scatter(False, 2, HALF, T)
-        scatter(False, 3, EXTRA_SLOTS, HALF)
+        scatter(False, 3, 0, HALF)
         scatter(False, 3, HALF, T)
+        scatter(False, 1, 0, SCALAR_SLOTS)
 
         ys = {t: bank(SUM_BANKS[place], [P, T]) for place, t in enumerate(SUM_ORDER)}
-        for g in range(G):
+        for g in (1, 0):
             for t in SUM_ORDER:
                 nc.tensor.matmul_mx(
                     out=ys[t][:],
                     lhsT=w2sp[:, PASS * g + P * t : PASS * g + P * (t + 1)].bitcast(FP8X4),
                     lhsT_scale=w2sscp[:, N * g + P * t : N * g + P * (t + 1)],
                     rhs=hsq[g][:].bitcast(FP8X4), rhs_scale=hssc[g][:],
-                    start=(g == 0), stop=(g == G - 1),
+                    start=(g == 1), stop=(g == 0),
                 )
 
         total = held([P, 4, T], F32, "total")
         rows = out_0.rearrange("(p t) c -> p t c", t=4)
         for t in SUM_ORDER:
-            nc.vector.tensor_tensor(total[:, t, :], ys[t][:], win[t][:], ALU.add)
+            nc.vector.tensor_tensor(total[:, t, :], ys[t][:], win[t][:, 0:T], ALU.add)
             nc.sync.dma_start(out=rows[:, t, :], in_=total[:, t, :])
 
         oq = held([P, T], U32, "oq")

@@ -21,7 +21,6 @@ P = 128
 PASS = 512
 G = HS // PASS
 HALF = T // 2
-WARM_PASSES = 2
 SCALAR_TOKENS = 192
 ROW_ORDER = (2, 3, 1, 0)
 SUM_ORDER = (2, 3, 0, 1)
@@ -60,10 +59,10 @@ def tile_moe_shf_mlp_relu2_kernel(
         nc.vector.memset(packed[:].bitcast(I32), 0)
         nc.vector.memset(w1ssc[:].bitcast(I32), 0)
 
-        w1w = held([P, E, 2 * H], U8, "w1w")
-        w2w = late.tile([P, E, 2 * N], U8, name="w2w", offset=16 * T, align_bytes=64)
+        w1w = [held([P, 2, 2 * H], U8, "w1w%d" % a) for a in range(2)]
+        w2w = held([P, E, 2 * N], U8, "w2w")
         w1sw = held([P, HS], I32, "w1sw")
-        w2sw = held([P, G, N], I32, "w2sw")
+        w2sw = late.tile([P, G, N], I32, name="w2sw", offset=16 * T, align_bytes=64)
         gates = late.tile([P, T], F32, name="gates", offset=40 * T)
 
         def load_words(tile, words):
@@ -77,12 +76,14 @@ def tile_moe_shf_mlp_relu2_kernel(
                 in_=x_scales[0, 4 * q : 4 * q + 4, :].bitcast(I32),
             )
         nc.sync.dma_start(out=w1sw[:], in_=w1s_words[0].rearrange("p l d -> p (l d)").bitcast(I32))
-        load_words(w1w, w1_words)
+        load_words(w1w[0], w1_words[0:2])
         for q in range(4):
             nc.sync.dma_start(
                 out=w1sc[32 * q : 32 * q + 4, :].bitcast(I32).rearrange("r (e n) -> r e n", e=E),
                 in_=w1_scales[:, 0, 4 * q : 4 * q + 4, :].rearrange("e r n -> r e n").bitcast(I32),
             )
+        load_words(w1w[1], w1_words[2:4])
+        load_words(w2w, w2_words)
         for q in range(4):
             nc.sync.dma_start(
                 out=w1ssc[32 * q : 32 * q + 4 * G, :].bitcast(I32),
@@ -94,7 +95,6 @@ def tile_moe_shf_mlp_relu2_kernel(
         nc.sync.dma_start(
             out=packed[64:96, :].bitcast(I32), in_=w2s_scales.rearrange("g b n -> b g n").bitcast(I32)
         )
-        load_words(w2w, w2_words)
         nc.sync.dma_start(out=w2sw[:], in_=w2s_words.rearrange("g p n d -> p g (n d)").bitcast(I32))
         nc.sync.dma_start(out=gates[:], in_=gate)
         make_identity(nc, ident[:])
@@ -148,13 +148,13 @@ def tile_moe_shf_mlp_relu2_kernel(
             pre_r[e] = bank(e, [P, H])
             nc.tensor.matmul_mx(
                 out=pre_r[e][:], lhsT=xg[a][:, cols].bitcast(FP8X4), lhsT_scale=xgs[a][:, cols],
-                rhs=w1w[:, e, :].bitcast(FP4X4), rhs_scale=w1sc[:, H * e : H * (e + 1)],
+                rhs=w1w[e // 2][:, e % 2, :].bitcast(FP4X4), rhs_scale=w1sc[:, H * e : H * (e + 1)],
                 start=True, stop=True,
             )
 
         def routed_relu(e):
             sorted_relu = held([P, 4, P], F32, "relu_r%d" % e)
-            relu(e % 2 == 0, sorted_relu[:].rearrange("s t p -> s p t"), pre_r[e][:].rearrange("s (p t) -> s p t", t=4))
+            relu(e == 0, sorted_relu[:].rearrange("s t p -> s p t"), pre_r[e][:].rearrange("s (p t) -> s p t", t=4))
             turned[e] = bank(4 + e, [P, 4, C])
             for t in range(4):
                 nc.tensor.transpose(turned[e][:, t, :], sorted_relu[:, t, :], ident[:])
@@ -196,23 +196,15 @@ def tile_moe_shf_mlp_relu2_kernel(
         def quantize(codes, scales, values):
             nc.vector.quantize_mx(out=codes.bitcast(FP8X4), scales=scales, in_=values.rearrange("p s t -> p (s t)"))
 
-        warm_scales = held([P, T], U8, "warm_scales")
-        nc.vector.tensor_copy(warm_scales[:].bitcast(I32), xs[:].bitcast(I32))
-        warm = bank(7, [P, T])
-        for repeat in range(WARM_PASSES):
-            nc.tensor.matmul_mx(
-                out=warm[:], lhsT=w1sw[:, 0:P].bitcast(FP8X4), lhsT_scale=warm_scales[:, 0:P],
-                rhs=w1sw[:, 0:T].bitcast(FP8X4), rhs_scale=warm_scales[:], start=True, stop=True,
-            )
-
         gather(0, 0, 1)
         gather(1, 1, 3)
         for e in range(E):
             routed_first(e)
         deal(w1sp[:].bitcast(U32), w1sw[:].bitcast(U32), 4, nc.scalar.copy)
-        deal(w1sscp[:], w1ssc[:], 16)
+        deal(w2p[:].rearrange("p e b -> p (e b)").bitcast(U16), w2w[:].rearrange("p e b -> p (e b)").bitcast(U16), 8)
         for e in range(E):
             routed_relu(e)
+        deal(w1sscp[:], w1ssc[:], 16)
         deal(sorted_rows[:], packed[:], 16)
         place_planes(w2scp, 0, E)
         place_planes(w2sscp, 64, G)
@@ -220,16 +212,15 @@ def tile_moe_shf_mlp_relu2_kernel(
             routed_square(e)
         for step in (0, 4, 5, 6, 1):
             shared_first(step)
-        deal(w2p[:].rearrange("p e b -> p (e b)").bitcast(U16), w2w[:].rearrange("p e b -> p (e b)").bitcast(U16), 8)
-        quantize(hq[:, 0:HALF], hsc[:, 0:HALF], hb[0][:])
         deal(w2sp[:], w2sw[:].rearrange("p g n -> p (g n)"), 4)
+        quantize(hq[:, 0:HALF], hsc[:, 0:HALF], hb[0][:])
         shared_relu(0)
         quantize(hq[:, HALF:T], hsc[:, HALF:T], hb[1][:])
         hsb = [held([P, T, 4], BF16, name) for name in ("hb1", "hsb1")]
-        shared_relu(1)
-        for step in range(4, 7):
+        shared_first(7)
+        for step in (7, 1, 4, 5, 6):
             shared_relu(step)
-        for step in (7, 2, 3):
+        for step in (2, 3):
             shared_first(step)
             shared_relu(step)
         square(hsb[1][:], relu_c[:])

@@ -25,7 +25,7 @@ SCALAR_TOKENS = 192
 ROW_ORDER = (2, 3, 1, 0)
 SUM_ORDER = (2, 3, 0, 1)
 SCALAR_SLOTS = 288
-POOL_TOKENS = 448
+SCALAR_SQUARES = 64
 WIDE_WINDOW = 704
 SHARED_BANKS = (0, 7, 7, 0, 3, 4, 5, 0)
 RESULT_BANKS = (1, 2, 3, 4)
@@ -217,17 +217,16 @@ def tile_moe_shf_mlp_relu2_kernel(
         shared_relu(0)
         quantize(hq[:, HALF:T], hsc[:, HALF:T], hb[1][:])
         hsb = [held([P, T, 4], BF16, name) for name in ("hb1", "hsb1")]
-        shared_first(7)
-        for step in (7, 1, 4, 5, 6):
+        for step in (1, 4, 5, 6):
             shared_relu(step)
-        for step in (2, 3):
+        for step in (7, 2, 3):
             shared_first(step)
             shared_relu(step)
+        nc.scalar.activation(hsb[0][:, 0:SCALAR_SQUARES, :], relu_a[:, 0:SCALAR_SQUARES, :], ACT.Square)
         square(hsb[1][:], relu_c[:])
-        for first in range(0, POOL_TOKENS, P):
-            cols = slice(first, min(first + P, POOL_TOKENS))
+        for u in range(4):
+            cols = slice(max(P * u, SCALAR_SQUARES), P * (u + 1))
             nc.gpsimd.tensor_tensor(hsb[0][:, cols, :], relu_a[:, cols, :], relu_a[:, cols, :], ALU.mult)
-        nc.scalar.activation(hsb[0][:, POOL_TOKENS:T, :], relu_a[:, POOL_TOKENS:T, :], ACT.Square)
 
         y = {}
         for place, t in enumerate(ROW_ORDER):

@@ -21,15 +21,23 @@ P = 128
 PASS = 512
 G = HS // PASS
 HALF = T // 2
-SCALAR_TOKENS = 192
-ROW_ORDER = (2, 3, 1, 0)
-SUM_ORDER = (2, 3, 0, 1)
+
 SCALAR_SLOTS = 288
 SCALAR_SQUARES = 64
+SCALAR_TOKENS = 192
 WIDE_WINDOW = 704
+
+GATE_ORDER = (2, 3, 1, 0)
+SUM_ORDER = (2, 3, 0, 1)
+VECTOR_STEP_OF_PASS_1 = 7
 SHARED_BANKS = (0, 7, 7, 0, 3, 4, 5, 0)
 RESULT_BANKS = (1, 2, 3, 4)
 SUM_BANKS = (5, 6, 0, 7)
+
+ROW = 4 * T
+RELU_1_AT = 0
+W2S_WORDS_AT = 4 * ROW
+GATES_AT = 10 * ROW
 
 
 def tile_moe_shf_mlp_relu2_kernel(
@@ -62,8 +70,8 @@ def tile_moe_shf_mlp_relu2_kernel(
         w1w = [held([P, 2, 2 * H], U8, "w1w%d" % a) for a in range(2)]
         w2w = held([P, E, 2 * N], U8, "w2w")
         w1sw = held([P, HS], I32, "w1sw")
-        w2sw = late.tile([P, G, N], I32, name="w2sw", offset=16 * T, align_bytes=64)
-        gates = late.tile([P, T], F32, name="gates", offset=40 * T)
+        w2sw = late.tile([P, G, N], I32, name="w2sw", offset=W2S_WORDS_AT, align_bytes=64)
+        gates = late.tile([P, T], F32, name="gates", offset=GATES_AT)
 
         def load_words(tile, words):
             nc.sync.dma_start(out=tile[:].bitcast(I32), in_=words[:, 0].rearrange("e p b -> p e b").bitcast(I32))
@@ -104,19 +112,19 @@ def tile_moe_shf_mlp_relu2_kernel(
         w2p = held([P, E, 2 * N], U8, "w2p")
         w2scp = held([P, E * N], U8, "w2scp")
         w2sscp = held([P, G * N], U8, "w2sscp")
-        sorted_rows = held([P, PASS], U8, "sorted_rows")
+        dealt_rows = held([P, PASS], U8, "dealt_rows")
         hb = [held([P, 2 * C, 4], BF16, "hb%d" % a) for a in range(2)]
-        hq = late.tile([P, E * C], U32, name="hq", offset=16 * T, align_bytes=64)
+        hq = late.tile([P, E * C], U32, name="hq", offset=W2S_WORDS_AT, align_bytes=64)
         hsc = held([P, E * C], U8, "hsc")
         w1sp = held([P, HS], I32, "w1sp")
         w2sp = held([P, HS], I32, "w2sp")
         w1sscp = held([P, PASS], U8, "w1sscp")
-        relu_a = late.tile([P, T, 4], F32, name="relu_a", offset=20 * T)
-        relu_c = late.tile([P, 4, T], F32, name="relu_c", offset=0)
+        relu_0 = late.tile([P, T, 4], F32, name="relu_0", offset=W2S_WORDS_AT + ROW)
+        relu_1 = late.tile([P, 4, T], F32, name="relu_1", offset=RELU_1_AT)
         hssc = [held([P, T], U8, "hssc%d" % g) for g in range(G)]
 
-        def slots(first, count):
-            return offsets[:, first * (C // 16) : (first + count) * (C // 16)]
+        def slots(first, last):
+            return offsets[:, first // 16 : last // 16]
 
         def deal(out, in_, run, copy=nc.vector.tensor_copy):
             copy(
@@ -124,15 +132,15 @@ def tile_moe_shf_mlp_relu2_kernel(
                 in_=in_.rearrange("p (g c i t) -> p g c t i", t=4, c=P // run, i=run),
             )
 
-        def gather(a, first, count):
-            nc.vector.tensor_copy(xg[a][:], xw[:].bitcast(U32).indirect(slots(first, count)))
-            nc.vector.tensor_copy(xgs[a][:], xs[:].indirect(slots(first, count)))
+        def gather(a, first, last):
+            nc.vector.tensor_copy(xg[a][:], xw[:].bitcast(U32).indirect(slots(first, last)))
+            nc.vector.tensor_copy(xgs[a][:], xs[:].indirect(slots(first, last)))
 
         def place_planes(tile, first, count):
             for q in range(4):
                 nc.sync.dma_start(
                     out=tile[32 * q : 32 * q + 4, :].bitcast(I32).rearrange("r (a n) -> r a n", a=count),
-                    in_=sorted_rows[first + 4 * count * q : first + 4 * count * (q + 1), :].bitcast(I32),
+                    in_=dealt_rows[first + 4 * count * q : first + 4 * count * (q + 1), :].bitcast(I32),
                 )
 
         def relu(on_vector, dst, src):
@@ -141,20 +149,26 @@ def tile_moe_shf_mlp_relu2_kernel(
             else:
                 nc.scalar.activation(dst, src, ACT.Relu)
 
+        def interleaved(dst, src):
+            return dst.rearrange("p (c i) t -> p c t i", i=4), src.rearrange("p t (c i) -> p c t i", i=4)
+
+        def quantize(codes, scales, values):
+            nc.vector.quantize_mx(out=codes.bitcast(FP8X4), scales=scales, in_=values.rearrange("p s t -> p (s t)"))
+
         pre_r, turned, pre_s = {}, {}, {}
 
         def routed_first(e):
-            a, cols = min(e, 1), slice(C * max(e - 1, 0), C * (max(e - 1, 0) + 1))
+            a, at = (0, 0) if e == 0 else (1, C * (e - 1))
             pre_r[e] = bank(e, [P, H])
             nc.tensor.matmul_mx(
-                out=pre_r[e][:], lhsT=xg[a][:, cols].bitcast(FP8X4), lhsT_scale=xgs[a][:, cols],
+                out=pre_r[e][:], lhsT=xg[a][:, at : at + C].bitcast(FP8X4), lhsT_scale=xgs[a][:, at : at + C],
                 rhs=w1w[e // 2][:, e % 2, :].bitcast(FP4X4), rhs_scale=w1sc[:, H * e : H * (e + 1)],
                 start=True, stop=True,
             )
 
         def routed_relu(e):
             sorted_relu = held([P, 4, P], F32, "relu_r%d" % e)
-            relu(e == 0, sorted_relu[:].rearrange("s t p -> s p t"), pre_r[e][:].rearrange("s (p t) -> s p t", t=4))
+            relu(e == 0, sorted_relu[:], pre_r[e][:].rearrange("s (p t) -> s t p", t=4))
             turned[e] = bank(4 + e, [P, 4, C])
             for t in range(4):
                 nc.tensor.transpose(turned[e][:, t, :], sorted_relu[:, t, :], ident[:])
@@ -183,21 +197,13 @@ def tile_moe_shf_mlp_relu2_kernel(
 
         def shared_relu(step):
             if step < 4:
-                out = relu_a[:, P * step : P * (step + 1), :]
+                out = relu_0[:, P * step : P * (step + 1), :]
                 relu(True, out, pre_s[step][:].rearrange("p (t s) -> p s t", t=4))
             else:
-                relu(step == 7, relu_c[:, step - 4, :], pre_s[step][:])
+                relu(step == VECTOR_STEP_OF_PASS_1, relu_1[:, step - 4, :], pre_s[step][:])
 
-        def square(out, values):
-            nc.scalar.activation(
-                out.rearrange("p (c i) t -> p c t i", i=4), values.rearrange("p t (c i) -> p c t i", i=4), ACT.Square
-            )
-
-        def quantize(codes, scales, values):
-            nc.vector.quantize_mx(out=codes.bitcast(FP8X4), scales=scales, in_=values.rearrange("p s t -> p (s t)"))
-
-        gather(0, 0, 1)
-        gather(1, 1, 3)
+        gather(0, 0, C)
+        gather(1, C, T)
         for e in range(E):
             routed_first(e)
         deal(w1sp[:].bitcast(U32), w1sw[:].bitcast(U32), 4, nc.scalar.copy)
@@ -205,11 +211,12 @@ def tile_moe_shf_mlp_relu2_kernel(
         for e in range(E):
             routed_relu(e)
         deal(w1sscp[:], w1ssc[:], 16)
-        deal(sorted_rows[:], packed[:], 16)
+        deal(dealt_rows[:], packed[:], 16)
         place_planes(w2scp, 0, E)
         place_planes(w2sscp, 64, G)
         for e in range(E):
             routed_square(e)
+
         for step in (0, 4, 5, 6, 1):
             shared_first(step)
         deal(w2sp[:], w2sw[:].rearrange("p g n -> p (g n)"), 4)
@@ -219,18 +226,18 @@ def tile_moe_shf_mlp_relu2_kernel(
         hsb = [held([P, T, 4], BF16, name) for name in ("hb1", "hsb1")]
         for step in (1, 4, 5, 6):
             shared_relu(step)
-        for step in (7, 2, 3):
+        for step in (VECTOR_STEP_OF_PASS_1, 2, 3):
             shared_first(step)
             shared_relu(step)
-        nc.scalar.activation(hsb[0][:, 0:SCALAR_SQUARES, :], relu_a[:, 0:SCALAR_SQUARES, :], ACT.Square)
-        square(hsb[1][:], relu_c[:])
+        nc.scalar.activation(hsb[0][:, 0:SCALAR_SQUARES, :], relu_0[:, 0:SCALAR_SQUARES, :], ACT.Square)
+        nc.scalar.activation(*interleaved(hsb[1][:], relu_1[:]), ACT.Square)
         for u in range(4):
             cols = slice(max(P * u, SCALAR_SQUARES), P * (u + 1))
-            nc.gpsimd.tensor_tensor(hsb[0][:, cols, :], relu_a[:, cols, :], relu_a[:, cols, :], ALU.mult)
+            nc.gpsimd.tensor_tensor(hsb[0][:, cols, :], relu_0[:, cols, :], relu_0[:, cols, :], ALU.mult)
 
         y = {}
-        for place, t in enumerate(ROW_ORDER):
-            sums = bank(RESULT_BANKS[place], [P, T])
+        for t, number in zip(GATE_ORDER, RESULT_BANKS):
+            sums = bank(number, [P, T])
             for e in range(E):
                 cols = slice(C * e, C * (e + 1))
                 nc.tensor.matmul_mx(
@@ -243,29 +250,30 @@ def tile_moe_shf_mlp_relu2_kernel(
             y[t] = held([P, T], F32, "y%d" % t)
             nc.vector.tensor_tensor(y[t][:], gates[:], sums[:], ALU.mult)
 
-
         def scatter(on_vector, t, first, last):
-            out, in_ = win[t][:].indirect(offsets[:, first // 16 : last // 16]), y[t][:, first:last]
+            out, in_ = win[t][:].indirect(slots(first, last)), y[t][:, first:last]
             if on_vector:
                 nc.vector.tensor_copy(out, in_)
             else:
                 nc.scalar.activation(out, in_, ACT.Copy)
 
-        win = {t: late.tile([P, T], F32, name="win%d" % t, offset=4 * T * t) for t in (2, 3)}
-        hsq = [late.tile([P, T], U32, name="hsq%d" % g, offset=(38 + 4 * g) * T, align_bytes=64) for g in range(G)]
+        win = {t: late.tile([P, T], F32, name="win%d" % t, offset=RELU_1_AT + ROW * t) for t in (2, 3)}
+        hsq = [
+            late.tile([P, T], U32, name="hsq%d" % g, offset=GATES_AT - ROW // 2 + ROW * g, align_bytes=64)
+            for g in range(G)
+        ]
         for g in (1, 0):
             quantize(hsq[g][:], hssc[g][:], hsb[g][:])
         win[0] = held([P, WIDE_WINDOW], F32, "hb1")
         win[1] = held([P, T], F32, "hsb1")
         scatter(True, 1, SCALAR_SLOTS, T)
         scatter(True, 0, 0, T)
-        scatter(False, 2, 0, HALF)
-        scatter(False, 2, HALF, T)
-        scatter(False, 3, 0, HALF)
-        scatter(False, 3, HALF, T)
+        for t in (2, 3):
+            scatter(False, t, 0, HALF)
+            scatter(False, t, HALF, T)
         scatter(False, 1, 0, SCALAR_SLOTS)
 
-        ys = {t: bank(SUM_BANKS[place], [P, T]) for place, t in enumerate(SUM_ORDER)}
+        ys = {t: bank(number, [P, T]) for t, number in zip(SUM_ORDER, SUM_BANKS)}
         for g in (1, 0):
             for t in SUM_ORDER:
                 nc.tensor.matmul_mx(
@@ -287,10 +295,8 @@ def tile_moe_shf_mlp_relu2_kernel(
         words_out = out_1[0].rearrange("p t d -> p (t d)").bitcast(I32)
         ob = [held([P, HALF, 4], BF16, "ob%d" % a) for a in range(2)]
 
-        def rounded(a, lo, hi):
-            dst = ob[a][:, lo:hi, :].rearrange("p (c i) t -> p c t i", i=4)
-            src = total[:, :, HALF * a + lo : HALF * a + hi].rearrange("p t (c i) -> p c t i", i=4)
-            return dst, src
+        def rounded(a, first, last):
+            return interleaved(ob[a][:, first:last, :], total[:, :, HALF * a + first : HALF * a + last])
 
         nc.scalar.copy(*rounded(1, 0, SCALAR_TOKENS))
         nc.vector.tensor_copy(*rounded(0, 0, HALF))

@@ -21,23 +21,19 @@ P = 128
 PASS = 512
 G = HS // PASS
 HALF = T // 2
-
-SCALAR_SLOTS = 288
-SCALAR_SQUARES = 64
-SCALAR_TOKENS = 192
-WIDE_WINDOW = 704
-
-GATE_ORDER = (2, 3, 1, 0)
-SUM_ORDER = (2, 3, 0, 1)
-VECTOR_STEP_OF_PASS_1 = 7
-SHARED_BANKS = (0, 7, 7, 0, 3, 4, 5, 0)
-RESULT_BANKS = (1, 2, 3, 4)
-SUM_BANKS = (5, 6, 0, 7)
-
 ROW = 4 * T
-RELU_1_AT = 0
-W2S_WORDS_AT = 4 * ROW
-GATES_AT = 10 * ROW
+PLANES = E + 2 * G
+
+SCALAR_SLOTS = 224
+SCALAR_TOKENS = 192
+UNITS = (((0, 0), (1, 0)), ((2, 0), (0, 1)), ((1, 1), (2, 1)), ((3, 0), (3, 1)))
+
+RELU_23_AT = 0
+PACKED_AT = 2 * ROW - PASS // 2
+W2S_WORDS_AT = 2 * ROW
+W2S_DEALT_AT = 4 * ROW
+GATES_AT = W2S_DEALT_AT + 2 * ROW - ROW // 2
+HS0_CODES_AT = GATES_AT + ROW // 2
 
 
 def tile_moe_shf_mlp_relu2_kernel(
@@ -53,6 +49,9 @@ def tile_moe_shf_mlp_relu2_kernel(
         def held(shape, dtype, name):
             return keep.tile(shape, dtype, name=name, align_bytes=64)
 
+        def placed(shape, dtype, name, offset):
+            return late.tile(shape, dtype, name=name, offset=offset, align_bytes=64)
+
         def bank(number, shape):
             return psum.tile(shape, F32, name="bank%d" % number)
 
@@ -60,18 +59,14 @@ def tile_moe_shf_mlp_relu2_kernel(
         xw = held([P, T], I32, "xw")
         xs = held([P, T], U8, "xs")
         w1sc = held([P, E * H], U8, "w1sc")
-        packed = held([P, PASS], U8, "packed")
         ident = held([P, P], F32, "ident")
-        w1ssc = held([P, PASS], U8, "w1ssc")
+        packed = placed([P, PASS], U8, "packed", PACKED_AT)
         nc.gpsimd.memset(xs[:].bitcast(I32), 0)
-        nc.vector.memset(packed[:].bitcast(I32), 0)
-        nc.vector.memset(w1ssc[:].bitcast(I32), 0)
 
         w1w = [held([P, 2, 2 * H], U8, "w1w%d" % a) for a in range(2)]
         w2w = held([P, E, 2 * N], U8, "w2w")
         w1sw = held([P, HS], I32, "w1sw")
-        w2sw = late.tile([P, G, N], I32, name="w2sw", offset=W2S_WORDS_AT, align_bytes=64)
-        gates = late.tile([P, T], F32, name="gates", offset=GATES_AT)
+        gates = placed([P, T], F32, "gates", GATES_AT)
 
         def load_words(tile, words):
             nc.sync.dma_start(out=tile[:].bitcast(I32), in_=words[:, 0].rearrange("e p b -> p e b").bitcast(I32))
@@ -91,36 +86,28 @@ def tile_moe_shf_mlp_relu2_kernel(
                 in_=w1_scales[:, 0, 4 * q : 4 * q + 4, :].rearrange("e r n -> r e n").bitcast(I32),
             )
         load_words(w1w[1], w1_words[2:4])
+        nc.sync.dma_start(
+            out=packed[0:P:2, :].bitcast(I32), in_=w2_scales[:, 0].rearrange("e b n -> b e n").bitcast(I32)
+        )
+        nc.sync.dma_start(
+            out=packed[1:P:4, :].bitcast(I32), in_=w1s_scales[0].rearrange("b (g l) -> (b g) l", g=G).bitcast(I32)
+        )
+        nc.sync.dma_start(
+            out=packed[3:P:4, :].bitcast(I32), in_=w2s_scales.rearrange("g b n -> b g n").bitcast(I32)
+        )
         load_words(w2w, w2_words)
-        for q in range(4):
-            nc.sync.dma_start(
-                out=w1ssc[32 * q : 32 * q + 4 * G, :].bitcast(I32),
-                in_=w1s_scales[0, 4 * q : 4 * q + 4, :].rearrange("r (g l) -> g r l", g=G).bitcast(I32),
-            )
-        nc.sync.dma_start(
-            out=packed[0:64, :].bitcast(I32), in_=w2_scales[:, 0].rearrange("e b n -> b e n").bitcast(I32)
-        )
-        nc.sync.dma_start(
-            out=packed[64:96, :].bitcast(I32), in_=w2s_scales.rearrange("g b n -> b g n").bitcast(I32)
-        )
-        nc.sync.dma_start(out=w2sw[:], in_=w2s_words.rearrange("g p n d -> p g (n d)").bitcast(I32))
         nc.sync.dma_start(out=gates[:], in_=gate)
         make_identity(nc, ident[:])
 
         xg = [held([P, C], U32, "xg0"), held([P, 3 * C], U32, "xg1")]
         xgs = [held([P, C], U8, "xgs0"), held([P, 3 * C], U8, "xgs1")]
         w2p = held([P, E, 2 * N], U8, "w2p")
-        w2scp = held([P, E * N], U8, "w2scp")
-        w2sscp = held([P, G * N], U8, "w2sscp")
+        planes = held([P, PLANES * PASS], U8, "planes")
         dealt_rows = held([P, PASS], U8, "dealt_rows")
         hb = [held([P, 2 * C, 4], BF16, "hb%d" % a) for a in range(2)]
-        hq = late.tile([P, E * C], U32, name="hq", offset=W2S_WORDS_AT, align_bytes=64)
         hsc = held([P, E * C], U8, "hsc")
         w1sp = held([P, HS], I32, "w1sp")
-        w2sp = held([P, HS], I32, "w2sp")
-        w1sscp = held([P, PASS], U8, "w1sscp")
-        relu_0 = late.tile([P, T, 4], F32, name="relu_0", offset=W2S_WORDS_AT + ROW)
-        relu_1 = late.tile([P, 4, T], F32, name="relu_1", offset=RELU_1_AT)
+        relu_s = [held([P, T, 4], F32, "relu_s%d" % g) for g in range(G)]
         hssc = [held([P, T], U8, "hssc%d" % g) for g in range(G)]
 
         def slots(first, last):
@@ -136,12 +123,8 @@ def tile_moe_shf_mlp_relu2_kernel(
             nc.vector.tensor_copy(xg[a][:], xw[:].bitcast(U32).indirect(slots(first, last)))
             nc.vector.tensor_copy(xgs[a][:], xs[:].indirect(slots(first, last)))
 
-        def place_planes(tile, first, count):
-            for q in range(4):
-                nc.sync.dma_start(
-                    out=tile[32 * q : 32 * q + 4, :].bitcast(I32).rearrange("r (a n) -> r a n", a=count),
-                    in_=dealt_rows[first + 4 * count * q : first + 4 * count * (q + 1), :].bitcast(I32),
-                )
+        def plane(index, t):
+            return planes[:, PASS * index + P * t : PASS * index + P * (t + 1)]
 
         def relu(on_vector, dst, src):
             if on_vector:
@@ -155,7 +138,7 @@ def tile_moe_shf_mlp_relu2_kernel(
         def quantize(codes, scales, values):
             nc.vector.quantize_mx(out=codes.bitcast(FP8X4), scales=scales, in_=values.rearrange("p s t -> p (s t)"))
 
-        pre_r, turned, pre_s = {}, {}, {}
+        pre_r, turned, pre_s, sums, y, whole = {}, {}, {}, {}, {}, {}
 
         def routed_first(e):
             a, at = (0, 0) if e == 0 else (1, C * (e - 1))
@@ -166,9 +149,8 @@ def tile_moe_shf_mlp_relu2_kernel(
                 start=True, stop=True,
             )
 
-        def routed_relu(e):
-            sorted_relu = held([P, 4, P], F32, "relu_r%d" % e)
-            relu(e == 0, sorted_relu[:], pre_r[e][:].rearrange("s (p t) -> s t p", t=4))
+        def routed_relu(e, sorted_relu):
+            relu(e >= 2, sorted_relu, pre_r[e][:].rearrange("s (p t) -> s t p", t=4))
             turned[e] = bank(4 + e, [P, 4, C])
             for t in range(4):
                 nc.tensor.transpose(turned[e][:, t, :], sorted_relu[:, t, :], ident[:])
@@ -178,116 +160,143 @@ def tile_moe_shf_mlp_relu2_kernel(
                 hb[e // 2][:, C * (e % 2) : C * (e % 2 + 1), :], turned[e][:].rearrange("p t s -> p s t"), ACT.Square
             )
 
-        def shared_pass(out, g, t, first, count):
-            nc.tensor.matmul_mx(
-                out=out,
-                lhsT=w1sp[:, PASS * g + P * t : PASS * g + P * (t + 1)].bitcast(FP8X4),
-                lhsT_scale=w1sscp[4 * g : P, P * t : P * (t + 1)],
-                rhs=xw[:, first : first + count].bitcast(FP8X4), rhs_scale=xs[:, first : first + count],
-                start=True, stop=True,
+        def shared_first(step, number):
+            g, u = divmod(step, 4)
+            pre_s[step] = bank(number, [P, 4, P])
+            for t in range(4):
+                nc.tensor.matmul_mx(
+                    out=pre_s[step][:, t, :],
+                    lhsT=w1sp[:, PASS * g + P * t : PASS * g + P * (t + 1)].bitcast(FP8X4),
+                    lhsT_scale=plane(1 + 4 * g, t),
+                    rhs=xw[:, P * u : P * (u + 1)].bitcast(FP8X4), rhs_scale=xs[:, P * u : P * (u + 1)],
+                    start=True, stop=True,
+                )
+
+        def quarter(tiles, step):
+            g, u = divmod(step, 4)
+            return tiles[g][:, P * u : P * (u + 1), :]
+
+        def shared_relu(on_vector, step):
+            relu(on_vector, quarter(relu_s, step), pre_s[step][:].rearrange("p t s -> p s t"))
+
+        def vector_square(step):
+            nc.vector.scalar_tensor_tensor(
+                quarter(hsb, step), pre_s[step][:].rearrange("p t s -> p s t"), 0.0, quarter(relu_s, step),
+                ALU.max, ALU.mult,
             )
 
-        def shared_first(step):
-            pre_s[step] = bank(SHARED_BANKS[step], [P, T])
-            if step < 4:
-                for t in range(4):
-                    shared_pass(pre_s[step][:, P * t : P * (t + 1)], 0, t, P * step, P)
-            else:
-                shared_pass(pre_s[step][:], 1, step - 4, 0, T)
+        def routed_second(unit, number):
+            sums[unit] = bank(number, [P, 2, HALF])
+            for j, (t, a) in enumerate(UNITS[unit]):
+                for e in (2 * a, 2 * a + 1):
+                    cols = slice(C * (e % 2), C * (e % 2 + 1))
+                    nc.tensor.matmul_mx(
+                        out=sums[unit][:, j, cols],
+                        lhsT=w2p[:, e, 2 * P * t : 2 * P * (t + 1)].bitcast(FP4X4), lhsT_scale=plane(2 * e, t),
+                        rhs=hq[a][:, cols].bitcast(FP8X4), rhs_scale=hsc[:, C * e : C * (e + 1)],
+                        start=True, stop=True,
+                    )
 
-        def shared_relu(step):
-            if step < 4:
-                out = relu_0[:, P * step : P * (step + 1), :]
-                relu(True, out, pre_s[step][:].rearrange("p (t s) -> p s t", t=4))
-            else:
-                relu(step == VECTOR_STEP_OF_PASS_1, relu_1[:, step - 4, :], pre_s[step][:])
+        def gated(unit):
+            (t0, a0), (t1, a1) = UNITS[unit]
+            weights = gates[:].rearrange("p (a s) -> p a s", a=2)
+            if a0 == a1:
+                weights = weights[:, a0 : a0 + 1, :].to_broadcast([P, 2, HALF])
+            both = held([P, 2, HALF], F32, "y%d" % unit)
+            nc.vector.tensor_tensor(both[:], weights, sums[unit][:], ALU.mult)
+            y[t0, a0], y[t1, a1] = both[:, 0, :], both[:, 1, :]
+            whole[unit] = both
 
         gather(0, 0, C)
         gather(1, C, T)
-        for e in range(E):
+        for e in range(3):
             routed_first(e)
         deal(w1sp[:].bitcast(U32), w1sw[:].bitcast(U32), 4, nc.scalar.copy)
-        deal(w2p[:].rearrange("p e b -> p (e b)").bitcast(U16), w2w[:].rearrange("p e b -> p (e b)").bitcast(U16), 8)
-        for e in range(E):
-            routed_relu(e)
-        deal(w1sscp[:], w1ssc[:], 16)
+        relu_01 = [held([P, 4, P], F32, "relu_r%d" % e) for e in range(2)]
+        routed_relu(0, relu_01[0][:])
+        routed_first(3)
+        routed_relu(1, relu_01[1][:])
         deal(dealt_rows[:], packed[:], 16)
-        place_planes(w2scp, 0, E)
-        place_planes(w2sscp, 64, G)
+        for q in range(4):
+            nc.sync.dma_start(
+                out=planes[32 * q : 32 * q + 4, :].bitcast(I32).rearrange("r (a n) -> r a n", a=PLANES),
+                in_=dealt_rows[32 * q : 32 * (q + 1), :].bitcast(I32),
+            )
+        w2sw = placed([P, G, N], I32, "w2sw", W2S_WORDS_AT)
+        nc.sync.dma_start(out=w2sw[:], in_=w2s_words.rearrange("g p n d -> p g (n d)").bitcast(I32))
+        relu_23 = placed([P, 2, 4, P], F32, "relu_23", RELU_23_AT)
+        for e in (2, 3):
+            routed_relu(e, relu_23[:, e - 2])
         for e in range(E):
             routed_square(e)
+        deal(w2p[:].rearrange("p e b -> p (e b)").bitcast(U16), w2w[:].rearrange("p e b -> p (e b)").bitcast(U16), 8)
+        hq = [held([P, HALF], U32, name) for name in ("w2w", "hq1")]
+        for a in range(2):
+            quantize(hq[a][:], hsc[:, HALF * a : HALF * (a + 1)], hb[a][:])
 
-        for step in (0, 4, 5, 6, 1):
-            shared_first(step)
-        deal(w2sp[:], w2sw[:].rearrange("p g n -> p (g n)"), 4)
-        quantize(hq[:, 0:HALF], hsc[:, 0:HALF], hb[0][:])
-        shared_relu(0)
-        quantize(hq[:, HALF:T], hsc[:, HALF:T], hb[1][:])
         hsb = [held([P, T, 4], BF16, name) for name in ("hb1", "hsb1")]
-        for step in (1, 4, 5, 6):
-            shared_relu(step)
-        for step in (VECTOR_STEP_OF_PASS_1, 2, 3):
-            shared_first(step)
-            shared_relu(step)
-        nc.scalar.activation(hsb[0][:, 0:SCALAR_SQUARES, :], relu_0[:, 0:SCALAR_SQUARES, :], ACT.Square)
-        nc.scalar.activation(*interleaved(hsb[1][:], relu_1[:]), ACT.Square)
-        for u in range(4):
-            cols = slice(max(P * u, SCALAR_SQUARES), P * (u + 1))
-            nc.gpsimd.tensor_tensor(hsb[0][:, cols, :], relu_0[:, cols, :], relu_0[:, cols, :], ALU.mult)
+        for step, number in ((0, 0), (1, 1), (2, 2), (5, 3)):
+            shared_first(step, number)
+        routed_second(0, 4)
+        shared_first(3, 5)
+        shared_first(6, 6)
+        routed_second(1, 7)
+        for step in range(3):
+            shared_relu(False, step)
+        shared_relu(True, 5)
+        gated(0)
+        shared_first(4, 0)
+        shared_first(7, 1)
+        routed_second(2, 2)
+        routed_second(3, 4)
+        shared_relu(True, 3)
+        shared_relu(True, 6)
+        vector_square(5)
+        gated(1)
+        shared_relu(True, 4)
+        vector_square(6)
+        shared_relu(True, 7)
+        gated(2)
+        vector_square(7)
+        gated(3)
+        for step in range(5):
+            nc.gpsimd.tensor_tensor(quarter(hsb, step), quarter(relu_s, step), quarter(relu_s, step), ALU.mult)
 
-        y = {}
-        for t, number in zip(GATE_ORDER, RESULT_BANKS):
-            sums = bank(number, [P, T])
-            for e in range(E):
-                cols = slice(C * e, C * (e + 1))
-                nc.tensor.matmul_mx(
-                    out=sums[:, cols],
-                    lhsT=w2p[:, e, 2 * P * t : 2 * P * (t + 1)].bitcast(FP4X4),
-                    lhsT_scale=w2scp[:, N * e + P * t : N * e + P * (t + 1)],
-                    rhs=hq[:, cols].bitcast(FP8X4), rhs_scale=hsc[:, cols],
-                    start=True, stop=True,
-                )
-            y[t] = held([P, T], F32, "y%d" % t)
-            nc.vector.tensor_tensor(y[t][:], gates[:], sums[:], ALU.mult)
-
-        def scatter(on_vector, t, first, last):
-            out, in_ = win[t][:].indirect(slots(first, last)), y[t][:, first:last]
+        def scatter(on_vector, t, first, last, values):
+            out = win[t][:].indirect(slots(first, last))
             if on_vector:
-                nc.vector.tensor_copy(out, in_)
+                nc.vector.tensor_copy(out, values)
             else:
-                nc.scalar.activation(out, in_, ACT.Copy)
+                nc.scalar.activation(out, values, ACT.Copy)
 
-        win = {t: late.tile([P, T], F32, name="win%d" % t, offset=RELU_1_AT + ROW * t) for t in (2, 3)}
-        hsq = [
-            late.tile([P, T], U32, name="hsq%d" % g, offset=GATES_AT - ROW // 2 + ROW * g, align_bytes=64)
-            for g in range(G)
-        ]
-        for g in (1, 0):
+        w2sp = placed([P, HS], I32, "w2sp", W2S_DEALT_AT)
+        deal(w2sp[:], w2sw[:].rearrange("p g n -> p (g n)"), 4)
+        hsq = [placed([P, T], U32, "hsq0", HS0_CODES_AT), placed([P, T], U32, "hsq1", W2S_WORDS_AT + ROW)]
+        for g in range(G):
             quantize(hsq[g][:], hssc[g][:], hsb[g][:])
-        win[0] = held([P, WIDE_WINDOW], F32, "hb1")
-        win[1] = held([P, T], F32, "hsb1")
-        scatter(True, 1, SCALAR_SLOTS, T)
-        scatter(True, 0, 0, T)
-        for t in (2, 3):
-            scatter(False, t, 0, HALF)
-            scatter(False, t, HALF, T)
-        scatter(False, 1, 0, SCALAR_SLOTS)
+        win = [held([P, T], F32, name) for name in ("win0", "win1", "win2", "hsb1")]
+        last_rows = whole[3][:].rearrange("p a s -> p (a s)")
+        scatter(True, 3, SCALAR_SLOTS, T, last_rows[:, SCALAR_SLOTS:T])
+        for unit in UNITS[:3]:
+            for t, a in unit:
+                scatter(False, t, HALF * a, HALF * (a + 1), y[t, a])
+        scatter(False, 3, 0, SCALAR_SLOTS, last_rows[:, 0:SCALAR_SLOTS])
 
-        ys = {t: bank(number, [P, T]) for t, number in zip(SUM_ORDER, SUM_BANKS)}
-        for g in (1, 0):
-            for t in SUM_ORDER:
+        ys = [bank(number, [P, T]) for number in (5, 7, 0, 3)]
+        for t, g in ((0, 0), (1, 0), (0, 1), (1, 1), (2, 0), (2, 1), (3, 0), (3, 1)):
+            if True:
                 nc.tensor.matmul_mx(
                     out=ys[t][:],
                     lhsT=w2sp[:, PASS * g + P * t : PASS * g + P * (t + 1)].bitcast(FP8X4),
-                    lhsT_scale=w2sscp[:, N * g + P * t : N * g + P * (t + 1)],
+                    lhsT_scale=plane(3 + 4 * g, t),
                     rhs=hsq[g][:].bitcast(FP8X4), rhs_scale=hssc[g][:],
-                    start=(g == 1), stop=(g == 0),
+                    start=(g == 0), stop=(g == G - 1),
                 )
 
         total = held([P, 4, T], F32, "total")
         rows = out_0.rearrange("(p t) c -> p t c", t=4)
-        for t in SUM_ORDER:
-            nc.vector.tensor_tensor(total[:, t, :], ys[t][:], win[t][:, 0:T], ALU.add)
+        for t in range(4):
+            nc.vector.tensor_tensor(total[:, t, :], ys[t][:], win[t][:], ALU.add)
             nc.sync.dma_start(out=rows[:, t, :], in_=total[:, t, :])
 
         oq = held([P, T], U32, "oq")

@@ -22,18 +22,16 @@ PASS = 512
 G = HS // PASS
 HALF = T // 2
 ROW = 4 * T
-PLANES = E + 2 * G
 
-SCALAR_SLOTS = 224
+SCALAR_SLOTS = 128
 SCALAR_TOKENS = 192
 UNITS = (((0, 0), (1, 0)), ((2, 0), (0, 1)), ((1, 1), (2, 1)), ((3, 0), (3, 1)))
 
-RELU_23_AT = 0
-PACKED_AT = 2 * ROW - PASS // 2
-W2S_WORDS_AT = 2 * ROW
-W2S_DEALT_AT = 4 * ROW
-GATES_AT = W2S_DEALT_AT + 2 * ROW - ROW // 2
-HS0_CODES_AT = GATES_AT + ROW // 2
+W2S_WORDS_AT = 0
+RELU_0_AT = ROW
+DEALT_ROWS_AT = 5 * ROW
+RELU_1_AT = DEALT_ROWS_AT + PASS // 2
+GATES_AT = 11 * ROW
 
 
 def tile_moe_shf_mlp_relu2_kernel(
@@ -60,12 +58,16 @@ def tile_moe_shf_mlp_relu2_kernel(
         xs = held([P, T], U8, "xs")
         w1sc = held([P, E * H], U8, "w1sc")
         ident = held([P, P], F32, "ident")
-        packed = placed([P, PASS], U8, "packed", PACKED_AT)
+        packed = held([P, PASS], U8, "packed")
+        shared_rows = held([P, PASS], U8, "shared_rows")
         nc.gpsimd.memset(xs[:].bitcast(I32), 0)
+        nc.vector.memset(packed[:].bitcast(I32), 0)
+        nc.vector.memset(shared_rows[:].bitcast(I32), 0)
 
         w1w = [held([P, 2, 2 * H], U8, "w1w%d" % a) for a in range(2)]
         w2w = held([P, E, 2 * N], U8, "w2w")
         w1sw = held([P, HS], I32, "w1sw")
+        w2sw = placed([P, G, N], I32, "w2sw", W2S_WORDS_AT)
         gates = placed([P, T], F32, "gates", GATES_AT)
 
         def load_words(tile, words):
@@ -86,28 +88,33 @@ def tile_moe_shf_mlp_relu2_kernel(
                 in_=w1_scales[:, 0, 4 * q : 4 * q + 4, :].rearrange("e r n -> r e n").bitcast(I32),
             )
         load_words(w1w[1], w1_words[2:4])
-        nc.sync.dma_start(
-            out=packed[0:P:2, :].bitcast(I32), in_=w2_scales[:, 0].rearrange("e b n -> b e n").bitcast(I32)
-        )
-        nc.sync.dma_start(
-            out=packed[1:P:4, :].bitcast(I32), in_=w1s_scales[0].rearrange("b (g l) -> (b g) l", g=G).bitcast(I32)
-        )
-        nc.sync.dma_start(
-            out=packed[3:P:4, :].bitcast(I32), in_=w2s_scales.rearrange("g b n -> b g n").bitcast(I32)
-        )
         load_words(w2w, w2_words)
+        nc.sync.dma_start(
+            out=packed[0:64, :].bitcast(I32), in_=w2_scales[:, 0].rearrange("e b n -> b e n").bitcast(I32)
+        )
+        for q in range(4):
+            nc.sync.dma_start(
+                out=shared_rows[32 * q : 32 * q + 8, :].bitcast(I32),
+                in_=w1s_scales[0, 4 * q : 4 * q + 4, :].rearrange("r (g l) -> g r l", g=G).bitcast(I32),
+            )
+        for q in range(4):
+            nc.sync.dma_start(
+                out=shared_rows[32 * q + 8 : 32 * q + 16, :].bitcast(I32),
+                in_=w2s_scales[:, 4 * q : 4 * q + 4, :].bitcast(I32),
+            )
+        nc.sync.dma_start(out=w2sw[:], in_=w2s_words.rearrange("g p n d -> p g (n d)").bitcast(I32))
         nc.sync.dma_start(out=gates[:], in_=gate)
         make_identity(nc, ident[:])
 
         xg = [held([P, C], U32, "xg0"), held([P, 3 * C], U32, "xg1")]
         xgs = [held([P, C], U8, "xgs0"), held([P, 3 * C], U8, "xgs1")]
         w2p = held([P, E, 2 * N], U8, "w2p")
-        planes = held([P, PLANES * PASS], U8, "planes")
-        dealt_rows = held([P, PASS], U8, "dealt_rows")
+        w2scp = held([P, E * N], U8, "w2scp")
+        shared_planes = held([P, PASS], U8, "shared_planes")
+        dealt_rows = placed([P, PASS], U8, "dealt_rows", DEALT_ROWS_AT)
         hb = [held([P, 2 * C, 4], BF16, "hb%d" % a) for a in range(2)]
         hsc = held([P, E * C], U8, "hsc")
         w1sp = held([P, HS], I32, "w1sp")
-        relu_s = [held([P, T, 4], F32, "relu_s%d" % g) for g in range(G)]
         hssc = [held([P, T], U8, "hssc%d" % g) for g in range(G)]
 
         def slots(first, last):
@@ -123,8 +130,12 @@ def tile_moe_shf_mlp_relu2_kernel(
             nc.vector.tensor_copy(xg[a][:], xw[:].bitcast(U32).indirect(slots(first, last)))
             nc.vector.tensor_copy(xgs[a][:], xs[:].indirect(slots(first, last)))
 
-        def plane(index, t):
-            return planes[:, PASS * index + P * t : PASS * index + P * (t + 1)]
+        def place_planes(tile, first, count):
+            for q in range(4):
+                nc.sync.dma_start(
+                    out=tile[32 * q : 32 * q + 4, :].bitcast(I32).rearrange("r (a n) -> r a n", a=count),
+                    in_=dealt_rows[first + 4 * count * q : first + 4 * count * (q + 1), :].bitcast(I32),
+                )
 
         def relu(on_vector, dst, src):
             if on_vector:
@@ -150,7 +161,7 @@ def tile_moe_shf_mlp_relu2_kernel(
             )
 
         def routed_relu(e, sorted_relu):
-            relu(e >= 2, sorted_relu, pre_r[e][:].rearrange("s (p t) -> s t p", t=4))
+            relu(e % 2 == 0, sorted_relu, pre_r[e][:].rearrange("s (p t) -> s t p", t=4))
             turned[e] = bank(4 + e, [P, 4, C])
             for t in range(4):
                 nc.tensor.transpose(turned[e][:, t, :], sorted_relu[:, t, :], ident[:])
@@ -167,7 +178,7 @@ def tile_moe_shf_mlp_relu2_kernel(
                 nc.tensor.matmul_mx(
                     out=pre_s[step][:, t, :],
                     lhsT=w1sp[:, PASS * g + P * t : PASS * g + P * (t + 1)].bitcast(FP8X4),
-                    lhsT_scale=plane(1 + 4 * g, t),
+                    lhsT_scale=shared_planes[4 * g : P, P * t : P * (t + 1)],
                     rhs=xw[:, P * u : P * (u + 1)].bitcast(FP8X4), rhs_scale=xs[:, P * u : P * (u + 1)],
                     start=True, stop=True,
                 )
@@ -177,11 +188,11 @@ def tile_moe_shf_mlp_relu2_kernel(
             return tiles[g][:, P * u : P * (u + 1), :]
 
         def shared_relu(on_vector, step):
-            relu(on_vector, quarter(relu_s, step), pre_s[step][:].rearrange("p t s -> p s t"))
+            relu(on_vector, relu_s[step], pre_s[step][:].rearrange("p t s -> p s t"))
 
         def vector_square(step):
             nc.vector.scalar_tensor_tensor(
-                quarter(hsb, step), pre_s[step][:].rearrange("p t s -> p s t"), 0.0, quarter(relu_s, step),
+                quarter(hsb, step), pre_s[step][:].rearrange("p t s -> p s t"), 0.0, relu_s[step],
                 ALU.max, ALU.mult,
             )
 
@@ -192,7 +203,8 @@ def tile_moe_shf_mlp_relu2_kernel(
                     cols = slice(C * (e % 2), C * (e % 2 + 1))
                     nc.tensor.matmul_mx(
                         out=sums[unit][:, j, cols],
-                        lhsT=w2p[:, e, 2 * P * t : 2 * P * (t + 1)].bitcast(FP4X4), lhsT_scale=plane(2 * e, t),
+                        lhsT=w2p[:, e, 2 * P * t : 2 * P * (t + 1)].bitcast(FP4X4),
+                        lhsT_scale=w2scp[:, N * e + P * t : N * e + P * (t + 1)],
                         rhs=hq[a][:, cols].bitcast(FP8X4), rhs_scale=hsc[:, C * e : C * (e + 1)],
                         start=True, stop=True,
                     )
@@ -209,58 +221,48 @@ def tile_moe_shf_mlp_relu2_kernel(
 
         gather(0, 0, C)
         gather(1, C, T)
-        for e in range(3):
+        for e in range(E):
             routed_first(e)
         deal(w1sp[:].bitcast(U32), w1sw[:].bitcast(U32), 4, nc.scalar.copy)
-        relu_01 = [held([P, 4, P], F32, "relu_r%d" % e) for e in range(2)]
-        routed_relu(0, relu_01[0][:])
-        routed_first(3)
-        routed_relu(1, relu_01[1][:])
+        deal(w2p[:].rearrange("p e b -> p (e b)").bitcast(U16), w2w[:].rearrange("p e b -> p (e b)").bitcast(U16), 8)
         deal(dealt_rows[:], packed[:], 16)
-        for q in range(4):
-            nc.sync.dma_start(
-                out=planes[32 * q : 32 * q + 4, :].bitcast(I32).rearrange("r (a n) -> r a n", a=PLANES),
-                in_=dealt_rows[32 * q : 32 * (q + 1), :].bitcast(I32),
-            )
-        w2sw = placed([P, G, N], I32, "w2sw", W2S_WORDS_AT)
-        nc.sync.dma_start(out=w2sw[:], in_=w2s_words.rearrange("g p n d -> p g (n d)").bitcast(I32))
-        relu_23 = placed([P, 2, 4, P], F32, "relu_23", RELU_23_AT)
-        for e in (2, 3):
-            routed_relu(e, relu_23[:, e - 2])
+        place_planes(w2scp, 0, E)
+        for e, name in enumerate(("relu_r0", "relu_r1", "w2w", "relu_r3")):
+            routed_relu(e, held([P, 4, P], F32, name)[:])
+        deal(shared_planes[:], shared_rows[:], 16)
         for e in range(E):
             routed_square(e)
-        deal(w2p[:].rearrange("p e b -> p (e b)").bitcast(U16), w2w[:].rearrange("p e b -> p (e b)").bitcast(U16), 8)
-        hq = [held([P, HALF], U32, name) for name in ("w2w", "hq1")]
-        for a in range(2):
-            quantize(hq[a][:], hsc[:, HALF * a : HALF * (a + 1)], hb[a][:])
 
-        hsb = [held([P, T, 4], BF16, name) for name in ("hb1", "hsb1")]
-        for step, number in ((0, 0), (1, 1), (2, 2), (5, 3)):
+        for step, number in ((0, 0), (1, 1), (5, 4), (2, 2), (3, 3)):
             shared_first(step, number)
-        routed_second(0, 4)
-        shared_first(3, 5)
-        shared_first(6, 6)
-        routed_second(1, 7)
-        for step in range(3):
+        w2sp = held([P, HS], I32, "w2sp")
+        deal(w2sp[:], w2sw[:].rearrange("p g n -> p (g n)"), 4)
+        hq = [placed([P, HALF], U32, "hq%d" % a, W2S_WORDS_AT + ROW // 2 * a) for a in range(2)]
+        relus = [placed([P, T, 4], F32, "relu_s%d" % g, at) for g, at in enumerate((RELU_0_AT, RELU_1_AT))]
+        relu_s = [quarter(relus, step) for step in range(8)]
+        quantize(hq[0][:], hsc[:, 0:HALF], hb[0][:])
+        shared_relu(True, 0)
+        quantize(hq[1][:], hsc[:, HALF:T], hb[1][:])
+        hsb = [held([P, T, 4], BF16, name) for name in ("hb1", "hsb1")]
+        for step in (1, 2, 3):
             shared_relu(False, step)
+        for unit, number in enumerate((5, 6, 0, 1)):
+            routed_second(unit, number)
         shared_relu(True, 5)
         gated(0)
-        shared_first(4, 0)
-        shared_first(7, 1)
-        routed_second(2, 2)
-        routed_second(3, 4)
-        shared_relu(True, 3)
-        shared_relu(True, 6)
         vector_square(5)
         gated(1)
+        for step, number in ((4, 5), (6, 4), (7, 6)):
+            shared_first(step, number)
         shared_relu(True, 4)
-        vector_square(6)
-        shared_relu(True, 7)
+        shared_relu(True, 6)
         gated(2)
-        vector_square(7)
+        shared_relu(True, 7)
+        vector_square(6)
         gated(3)
+        vector_square(7)
         for step in range(5):
-            nc.gpsimd.tensor_tensor(quarter(hsb, step), quarter(relu_s, step), quarter(relu_s, step), ALU.mult)
+            nc.gpsimd.tensor_tensor(quarter(hsb, step), relu_s[step], relu_s[step], ALU.mult)
 
         def scatter(on_vector, t, first, last, values):
             out = win[t][:].indirect(slots(first, last))
@@ -269,9 +271,7 @@ def tile_moe_shf_mlp_relu2_kernel(
             else:
                 nc.scalar.activation(out, values, ACT.Copy)
 
-        w2sp = placed([P, HS], I32, "w2sp", W2S_DEALT_AT)
-        deal(w2sp[:], w2sw[:].rearrange("p g n -> p (g n)"), 4)
-        hsq = [placed([P, T], U32, "hsq0", HS0_CODES_AT), placed([P, T], U32, "hsq1", W2S_WORDS_AT + ROW)]
+        hsq = [placed([P, T], U32, "hsq%d" % g, GATES_AT - ROW // 2 + ROW * g) for g in range(G)]
         for g in range(G):
             quantize(hsq[g][:], hssc[g][:], hsb[g][:])
         win = [held([P, T], F32, name) for name in ("win0", "win1", "win2", "hsb1")]
@@ -282,13 +282,13 @@ def tile_moe_shf_mlp_relu2_kernel(
                 scatter(False, t, HALF * a, HALF * (a + 1), y[t, a])
         scatter(False, 3, 0, SCALAR_SLOTS, last_rows[:, 0:SCALAR_SLOTS])
 
-        ys = [bank(number, [P, T]) for number in (5, 7, 0, 3)]
+        ys = [bank(number, [P, T]) for number in (7, 2, 3, 5)]
         for t, g in ((0, 0), (1, 0), (0, 1), (1, 1), (2, 0), (2, 1), (3, 0), (3, 1)):
             if True:
                 nc.tensor.matmul_mx(
                     out=ys[t][:],
                     lhsT=w2sp[:, PASS * g + P * t : PASS * g + P * (t + 1)].bitcast(FP8X4),
-                    lhsT_scale=plane(3 + 4 * g, t),
+                    lhsT_scale=shared_planes[8 + 4 * g : P, P * t : P * (t + 1)],
                     rhs=hsq[g][:].bitcast(FP8X4), rhs_scale=hssc[g][:],
                     start=(g == 0), stop=(g == G - 1),
                 )

@@ -27,11 +27,14 @@ SCALAR_SLOTS = 128
 SCALAR_TOKENS = 192
 UNITS = (((0, 0), (1, 0)), ((2, 0), (0, 1)), ((1, 1), (2, 1)), ((3, 0), (3, 1)))
 
-W2S_WORDS_AT = 0
+W2_WORDS_AT = 0
 RELU_0_AT = ROW
-DEALT_ROWS_AT = 5 * ROW
-RELU_1_AT = DEALT_ROWS_AT + PASS // 2
-GATES_AT = 11 * ROW
+HS_0_AT = 5 * ROW
+H_1_AT = HS_0_AT + 2 * ROW - ROW // 2
+RELU_1_AT = HS_0_AT + 2 * ROW
+W2S_DEALT_AT = 11 * ROW
+GATES_AT = W2S_DEALT_AT + 2 * ROW - ROW // 2
+HS_0_CODES_AT = W2S_DEALT_AT + 2 * ROW
 
 
 def tile_moe_shf_mlp_relu2_kernel(
@@ -59,15 +62,15 @@ def tile_moe_shf_mlp_relu2_kernel(
         w1sc = held([P, E * H], U8, "w1sc")
         ident = held([P, P], F32, "ident")
         packed = held([P, PASS], U8, "packed")
-        shared_rows = held([P, PASS], U8, "shared_rows")
+        w1ssc = held([P, PASS], U8, "w1ssc")
         nc.gpsimd.memset(xs[:].bitcast(I32), 0)
         nc.vector.memset(packed[:].bitcast(I32), 0)
-        nc.vector.memset(shared_rows[:].bitcast(I32), 0)
+        nc.vector.memset(w1ssc[:].bitcast(I32), 0)
 
         w1w = [held([P, 2, 2 * H], U8, "w1w%d" % a) for a in range(2)]
-        w2w = held([P, E, 2 * N], U8, "w2w")
+        w2w = placed([P, E, 2 * N], U8, "w2w", W2_WORDS_AT)
         w1sw = held([P, HS], I32, "w1sw")
-        w2sw = placed([P, G, N], I32, "w2sw", W2S_WORDS_AT)
+        w2sw = held([P, G, N], I32, "w2sw")
         gates = placed([P, T], F32, "gates", GATES_AT)
 
         def load_words(tile, words):
@@ -88,31 +91,28 @@ def tile_moe_shf_mlp_relu2_kernel(
                 in_=w1_scales[:, 0, 4 * q : 4 * q + 4, :].rearrange("e r n -> r e n").bitcast(I32),
             )
         load_words(w1w[1], w1_words[2:4])
-        load_words(w2w, w2_words)
         nc.sync.dma_start(
             out=packed[0:64, :].bitcast(I32), in_=w2_scales[:, 0].rearrange("e b n -> b e n").bitcast(I32)
         )
+        nc.sync.dma_start(
+            out=packed[64:96, :].bitcast(I32), in_=w2s_scales.rearrange("g b n -> b g n").bitcast(I32)
+        )
         for q in range(4):
             nc.sync.dma_start(
-                out=shared_rows[32 * q : 32 * q + 8, :].bitcast(I32),
+                out=w1ssc[32 * q : 32 * q + 4 * G, :].bitcast(I32),
                 in_=w1s_scales[0, 4 * q : 4 * q + 4, :].rearrange("r (g l) -> g r l", g=G).bitcast(I32),
             )
-        for q in range(4):
-            nc.sync.dma_start(
-                out=shared_rows[32 * q + 8 : 32 * q + 16, :].bitcast(I32),
-                in_=w2s_scales[:, 4 * q : 4 * q + 4, :].bitcast(I32),
-            )
-        nc.sync.dma_start(out=w2sw[:], in_=w2s_words.rearrange("g p n d -> p g (n d)").bitcast(I32))
-        nc.sync.dma_start(out=gates[:], in_=gate)
+        load_words(w2w, w2_words)
         make_identity(nc, ident[:])
 
         xg = [held([P, C], U32, "xg0"), held([P, 3 * C], U32, "xg1")]
         xgs = [held([P, C], U8, "xgs0"), held([P, 3 * C], U8, "xgs1")]
         w2p = held([P, E, 2 * N], U8, "w2p")
         w2scp = held([P, E * N], U8, "w2scp")
-        shared_planes = held([P, PASS], U8, "shared_planes")
-        dealt_rows = placed([P, PASS], U8, "dealt_rows", DEALT_ROWS_AT)
-        hb = [held([P, 2 * C, 4], BF16, "hb%d" % a) for a in range(2)]
+        w1sscp = held([P, PASS], U8, "w1sscp")
+        dealt_rows = held([P, PASS], U8, "dealt_rows")
+        w2sscp = held([P, G * N], U8, "w2sscp")
+        hb = [held([P, HALF, 4], BF16, "hb0"), placed([P, HALF, 4], BF16, "hb1", H_1_AT)]
         hsc = held([P, E * C], U8, "hsc")
         w1sp = held([P, HS], I32, "w1sp")
         hssc = [held([P, T], U8, "hssc%d" % g) for g in range(G)]
@@ -161,7 +161,7 @@ def tile_moe_shf_mlp_relu2_kernel(
             )
 
         def routed_relu(e, sorted_relu):
-            relu(e % 2 == 0, sorted_relu, pre_r[e][:].rearrange("s (p t) -> s t p", t=4))
+            relu(e % 3 == 0, sorted_relu, pre_r[e][:].rearrange("s (p t) -> s t p", t=4))
             turned[e] = bank(4 + e, [P, 4, C])
             for t in range(4):
                 nc.tensor.transpose(turned[e][:, t, :], sorted_relu[:, t, :], ident[:])
@@ -178,7 +178,7 @@ def tile_moe_shf_mlp_relu2_kernel(
                 nc.tensor.matmul_mx(
                     out=pre_s[step][:, t, :],
                     lhsT=w1sp[:, PASS * g + P * t : PASS * g + P * (t + 1)].bitcast(FP8X4),
-                    lhsT_scale=shared_planes[4 * g : P, P * t : P * (t + 1)],
+                    lhsT_scale=w1sscp[4 * g : P, P * t : P * (t + 1)],
                     rhs=xw[:, P * u : P * (u + 1)].bitcast(FP8X4), rhs_scale=xs[:, P * u : P * (u + 1)],
                     start=True, stop=True,
                 )
@@ -224,26 +224,27 @@ def tile_moe_shf_mlp_relu2_kernel(
         for e in range(E):
             routed_first(e)
         deal(w1sp[:].bitcast(U32), w1sw[:].bitcast(U32), 4, nc.scalar.copy)
-        deal(w2p[:].rearrange("p e b -> p (e b)").bitcast(U16), w2w[:].rearrange("p e b -> p (e b)").bitcast(U16), 8)
         deal(dealt_rows[:], packed[:], 16)
         place_planes(w2scp, 0, E)
-        for e, name in enumerate(("relu_r0", "relu_r1", "w2w", "relu_r3")):
+        nc.sync.dma_start(out=gates[:], in_=gate)
+        place_planes(w2sscp, 64, G)
+        nc.sync.dma_start(out=w2sw[:], in_=w2s_words.rearrange("g p n d -> p g (n d)").bitcast(I32))
+        for e, name in enumerate(("relu_r0", "relu_r1", "relu_r2", "packed")):
             routed_relu(e, held([P, 4, P], F32, name)[:])
-        deal(shared_planes[:], shared_rows[:], 16)
+        deal(w1sscp[:], w1ssc[:], 16)
         for e in range(E):
             routed_square(e)
+        deal(w2p[:].rearrange("p e b -> p (e b)").bitcast(U16), w2w[:].rearrange("p e b -> p (e b)").bitcast(U16), 8)
 
         for step, number in ((0, 0), (1, 1), (5, 4), (2, 2), (3, 3)):
             shared_first(step, number)
-        w2sp = held([P, HS], I32, "w2sp")
-        deal(w2sp[:], w2sw[:].rearrange("p g n -> p (g n)"), 4)
-        hq = [placed([P, HALF], U32, "hq%d" % a, W2S_WORDS_AT + ROW // 2 * a) for a in range(2)]
+        hq = [placed([P, HALF], U32, "hq%d" % a, W2_WORDS_AT + ROW // 2 * a) for a in range(2)]
         relus = [placed([P, T, 4], F32, "relu_s%d" % g, at) for g, at in enumerate((RELU_0_AT, RELU_1_AT))]
         relu_s = [quarter(relus, step) for step in range(8)]
         quantize(hq[0][:], hsc[:, 0:HALF], hb[0][:])
         shared_relu(True, 0)
         quantize(hq[1][:], hsc[:, HALF:T], hb[1][:])
-        hsb = [held([P, T, 4], BF16, name) for name in ("hb1", "hsb1")]
+        hsb = [placed([P, T, 4], BF16, "hsb0", HS_0_AT), held([P, T, 4], BF16, "hsb1")]
         for step in (1, 2, 3):
             shared_relu(False, step)
         for unit, number in enumerate((5, 6, 0, 1)):
@@ -271,7 +272,9 @@ def tile_moe_shf_mlp_relu2_kernel(
             else:
                 nc.scalar.activation(out, values, ACT.Copy)
 
-        hsq = [placed([P, T], U32, "hsq%d" % g, GATES_AT - ROW // 2 + ROW * g) for g in range(G)]
+        w2sp = placed([P, HS], I32, "w2sp", W2S_DEALT_AT)
+        deal(w2sp[:], w2sw[:].rearrange("p g n -> p (g n)"), 4)
+        hsq = [placed([P, T], U32, "hsq0", HS_0_CODES_AT), held([P, T], U32, "w2sw")]
         for g in range(G):
             quantize(hsq[g][:], hssc[g][:], hsb[g][:])
         win = [held([P, T], F32, name) for name in ("win0", "win1", "win2", "hsb1")]
@@ -288,7 +291,7 @@ def tile_moe_shf_mlp_relu2_kernel(
                 nc.tensor.matmul_mx(
                     out=ys[t][:],
                     lhsT=w2sp[:, PASS * g + P * t : PASS * g + P * (t + 1)].bitcast(FP8X4),
-                    lhsT_scale=shared_planes[8 + 4 * g : P, P * t : P * (t + 1)],
+                    lhsT_scale=w2sscp[:, N * g + P * t : N * g + P * (t + 1)],
                     rhs=hsq[g][:].bitcast(FP8X4), rhs_scale=hssc[g][:],
                     start=(g == 0), stop=(g == G - 1),
                 )

@@ -236,7 +236,7 @@ def tile_moe_shf_mlp_relu2_kernel(
             routed_square(e)
         deal(w2p[:].rearrange("p e b -> p (e b)").bitcast(U16), w2w[:].rearrange("p e b -> p (e b)").bitcast(U16), 8)
 
-        for step, number in ((0, 0), (1, 1), (5, 4), (2, 2), (3, 3)):
+        for step, number in ((0, 0), (1, 1), (2, 2)):
             shared_first(step, number)
         hq = [placed([P, HALF], U32, "hq%d" % a, W2_WORDS_AT + ROW // 2 * a) for a in range(2)]
         relus = [placed([P, T, 4], F32, "relu_s%d" % g, at) for g, at in enumerate((RELU_0_AT, RELU_1_AT))]
@@ -245,21 +245,17 @@ def tile_moe_shf_mlp_relu2_kernel(
         shared_relu(True, 0)
         quantize(hq[1][:], hsc[:, HALF:T], hb[1][:])
         hsb = [placed([P, T, 4], BF16, "hsb0", HS_0_AT), held([P, T, 4], BF16, "hsb1")]
-        for step in (1, 2, 3):
+        for step in (1, 2):
             shared_relu(False, step)
-        for unit, number in enumerate((5, 6, 0, 1)):
+        for unit, number in enumerate((3, 4, 5, 6)):
             routed_second(unit, number)
-        shared_relu(True, 5)
-        gated(0)
-        vector_square(5)
-        gated(1)
-        for step, number in ((4, 5), (6, 4), (7, 6)):
+        for unit in range(3):
+            gated(unit)
+        for step, number in ((3, 3), (4, 4), (5, 5), (6, 3), (7, 4)):
             shared_first(step, number)
-        shared_relu(True, 4)
-        shared_relu(True, 6)
-        gated(2)
-        shared_relu(True, 7)
-        vector_square(6)
+            shared_relu(True, step)
+            if step > 5:
+                vector_square(step - 1)
         gated(3)
         vector_square(7)
         for step in range(5):
@@ -285,7 +281,7 @@ def tile_moe_shf_mlp_relu2_kernel(
                 scatter(False, t, HALF * a, HALF * (a + 1), y[t, a])
         scatter(False, 3, 0, SCALAR_SLOTS, last_rows[:, 0:SCALAR_SLOTS])
 
-        ys = [bank(number, [P, T]) for number in (7, 2, 3, 5)]
+        ys = [bank(number, [P, T]) for number in (7, 0, 1, 2)]
         for t, g in ((0, 0), (1, 0), (0, 1), (1, 1), (2, 0), (2, 1), (3, 0), (3, 1)):
             if True:
                 nc.tensor.matmul_mx(

@@ -27,7 +27,8 @@ SCALAR_SLOTS = 128
 SCALAR_TOKENS = 192
 UNITS = (((0, 0), (1, 0)), ((2, 0), (0, 1)), ((1, 1), (2, 1)), ((3, 0), (3, 1)))
 
-W2_WORDS_AT = 0
+H_0_CODES_AT = 0
+W2_WORDS_AT = ROW // 4
 RELU_0_AT = ROW
 HS_0_AT = 5 * ROW
 H_1_AT = HS_0_AT + 2 * ROW - ROW // 2
@@ -68,7 +69,7 @@ def tile_moe_shf_mlp_relu2_kernel(
         nc.vector.memset(w1ssc[:].bitcast(I32), 0)
 
         w1w = [held([P, 2, 2 * H], U8, "w1w%d" % a) for a in range(2)]
-        w2w = placed([P, E, 2 * N], U8, "w2w", W2_WORDS_AT)
+        w2w = [placed([P, 2, 2 * N], U8, "w2w0", W2_WORDS_AT), held([P, 2, 2 * N], U8, "w2w1")]
         w1sw = held([P, HS], I32, "w1sw")
         w2sw = held([P, G, N], I32, "w2sw")
         gates = placed([P, T], F32, "gates", GATES_AT)
@@ -102,12 +103,13 @@ def tile_moe_shf_mlp_relu2_kernel(
                 out=w1ssc[32 * q : 32 * q + 4 * G, :].bitcast(I32),
                 in_=w1s_scales[0, 4 * q : 4 * q + 4, :].rearrange("r (g l) -> g r l", g=G).bitcast(I32),
             )
-        load_words(w2w, w2_words)
+        load_words(w2w[0], w2_words[0:2])
+        load_words(w2w[1], w2_words[2:4])
         make_identity(nc, ident[:])
 
         xg = [held([P, C], U32, "xg0"), held([P, 3 * C], U32, "xg1")]
         xgs = [held([P, C], U8, "xgs0"), held([P, 3 * C], U8, "xgs1")]
-        w2p = held([P, E, 2 * N], U8, "w2p")
+        w2p = [held([P, 2, 2 * N], U8, "w2p%d" % a) for a in range(2)]
         w2scp = held([P, E * N], U8, "w2scp")
         w1sscp = held([P, PASS], U8, "w1sscp")
         dealt_rows = held([P, PASS], U8, "dealt_rows")
@@ -125,6 +127,10 @@ def tile_moe_shf_mlp_relu2_kernel(
                 out=out.rearrange("p (g t c i) -> p g c t i", t=4, c=P // run, i=run),
                 in_=in_.rearrange("p (g c i t) -> p g c t i", t=4, c=P // run, i=run),
             )
+
+        def deal_w2(a):
+            flat = "p e b -> p (e b)"
+            deal(w2p[a][:].rearrange(flat).bitcast(U16), w2w[a][:].rearrange(flat).bitcast(U16), 8)
 
         def gather(a, first, last):
             nc.vector.tensor_copy(xg[a][:], xw[:].bitcast(U32).indirect(slots(first, last)))
@@ -161,7 +167,7 @@ def tile_moe_shf_mlp_relu2_kernel(
             )
 
         def routed_relu(e, sorted_relu):
-            relu(e % 3 == 0, sorted_relu, pre_r[e][:].rearrange("s (p t) -> s t p", t=4))
+            relu(e == 0, sorted_relu, pre_r[e][:].rearrange("s (p t) -> s t p", t=4))
             turned[e] = bank(4 + e, [P, 4, C])
             for t in range(4):
                 nc.tensor.transpose(turned[e][:, t, :], sorted_relu[:, t, :], ident[:])
@@ -203,7 +209,7 @@ def tile_moe_shf_mlp_relu2_kernel(
                     cols = slice(C * (e % 2), C * (e % 2 + 1))
                     nc.tensor.matmul_mx(
                         out=sums[unit][:, j, cols],
-                        lhsT=w2p[:, e, 2 * P * t : 2 * P * (t + 1)].bitcast(FP4X4),
+                        lhsT=w2p[a][:, e % 2, 2 * P * t : 2 * P * (t + 1)].bitcast(FP4X4),
                         lhsT_scale=w2scp[:, N * e + P * t : N * e + P * (t + 1)],
                         rhs=hq[a][:, cols].bitcast(FP8X4), rhs_scale=hsc[:, C * e : C * (e + 1)],
                         start=True, stop=True,
@@ -229,20 +235,22 @@ def tile_moe_shf_mlp_relu2_kernel(
         nc.sync.dma_start(out=gates[:], in_=gate)
         place_planes(w2sscp, 64, G)
         nc.sync.dma_start(out=w2sw[:], in_=w2s_words.rearrange("g p n d -> p g (n d)").bitcast(I32))
-        for e, name in enumerate(("relu_r0", "relu_r1", "relu_r2", "packed")):
-            routed_relu(e, held([P, 4, P], F32, name)[:])
+        for e in range(E):
+            routed_relu(e, held([P, 4, P], F32, "relu_r%d" % e)[:])
         deal(w1sscp[:], w1ssc[:], 16)
         for e in range(E):
             routed_square(e)
-        deal(w2p[:].rearrange("p e b -> p (e b)").bitcast(U16), w2w[:].rearrange("p e b -> p (e b)").bitcast(U16), 8)
+        deal_w2(0)
 
         for step, number in ((0, 0), (1, 1), (2, 2)):
             shared_first(step, number)
-        hq = [placed([P, HALF], U32, "hq%d" % a, W2_WORDS_AT + ROW // 2 * a) for a in range(2)]
+        hq = [placed([P, HALF], U32, "hq0", H_0_CODES_AT)]
         relus = [placed([P, T, 4], F32, "relu_s%d" % g, at) for g, at in enumerate((RELU_0_AT, RELU_1_AT))]
         relu_s = [quarter(relus, step) for step in range(8)]
         quantize(hq[0][:], hsc[:, 0:HALF], hb[0][:])
         shared_relu(True, 0)
+        deal_w2(1)
+        hq.append(held([P, HALF], U32, "w2w1"))
         quantize(hq[1][:], hsc[:, HALF:T], hb[1][:])
         hsb = [placed([P, T, 4], BF16, "hsb0", HS_0_AT), held([P, T, 4], BF16, "hsb1")]
         for step in (1, 2):
@@ -296,7 +304,9 @@ def tile_moe_shf_mlp_relu2_kernel(
         rows = out_0.rearrange("(p t) c -> p t c", t=4)
         for t in range(4):
             nc.vector.tensor_tensor(total[:, t, :], ys[t][:], win[t][:], ALU.add)
-            nc.sync.dma_start(out=rows[:, t, :], in_=total[:, t, :])
+            if t > 0:
+                first = 0 if t == 1 else t
+                nc.sync.dma_start(out=rows[:, first : t + 1, :], in_=total[:, first : t + 1, :])
 
         oq = held([P, T], U32, "oq")
         osc = held([P, T], U8, "osc")

@@ -1,3 +1,4 @@
+import itertools
 from contextlib import ExitStack
 
 import concourse.mybir as mybir
@@ -23,17 +24,16 @@ G = HS // PASS
 HALF = T // 2
 ROW = 4 * T
 
-SCALAR_SLOTS = 128
+SCALAR_SLOTS = 160
+GPSIMD_COLUMNS = (0, 128, 384, 640)
 SCALAR_TOKENS = 192
 UNITS = (((0, 0), (1, 0)), ((2, 0), (0, 1)), ((1, 1), (2, 1)), ((3, 0), (3, 1)))
 
 H_0_CODES_AT = 0
 W2_WORDS_AT = ROW // 4
-RELU_0_AT = ROW
-HS_0_AT = 5 * ROW
-H_1_AT = HS_0_AT + 2 * ROW - ROW // 2
-RELU_1_AT = HS_0_AT + 2 * ROW
-W2S_DEALT_AT = 11 * ROW
+RELUS_AT = ROW
+H_1_AT = 9 * ROW
+W2S_DEALT_AT = 13 * ROW
 GATES_AT = W2S_DEALT_AT + 2 * ROW - ROW // 2
 HS_0_CODES_AT = W2S_DEALT_AT + 2 * ROW
 
@@ -189,16 +189,13 @@ def tile_moe_shf_mlp_relu2_kernel(
                     start=True, stop=True,
                 )
 
-        def quarter(tiles, step):
-            g, u = divmod(step, 4)
-            return tiles[g][:, P * u : P * (u + 1), :]
-
         def shared_relu(on_vector, step):
-            relu(on_vector, relu_s[step], pre_s[step][:].rearrange("p t s -> p s t"))
+            relu(on_vector, relus[:, P * step : P * (step + 1), :], pre_s[step][:].rearrange("p t s -> p s t"))
 
         def vector_square(step):
+            cols = slice(P * step, P * (step + 1))
             nc.vector.scalar_tensor_tensor(
-                quarter(hsb, step), pre_s[step][:].rearrange("p t s -> p s t"), 0.0, relu_s[step],
+                hs[:, cols, :], pre_s[step][:].rearrange("p t s -> p s t"), 0.0, relus[:, cols, :],
                 ALU.max, ALU.mult,
             )
 
@@ -245,14 +242,13 @@ def tile_moe_shf_mlp_relu2_kernel(
         for step, number in ((0, 0), (1, 1), (2, 2)):
             shared_first(step, number)
         hq = [placed([P, HALF], U32, "hq0", H_0_CODES_AT)]
-        relus = [placed([P, T, 4], F32, "relu_s%d" % g, at) for g, at in enumerate((RELU_0_AT, RELU_1_AT))]
-        relu_s = [quarter(relus, step) for step in range(8)]
+        relus = placed([P, G * T, 4], F32, "relus", RELUS_AT)
         quantize(hq[0][:], hsc[:, 0:HALF], hb[0][:])
         shared_relu(True, 0)
         deal_w2(1)
         hq.append(held([P, HALF], U32, "w2w1"))
         quantize(hq[1][:], hsc[:, HALF:T], hb[1][:])
-        hsb = [placed([P, T, 4], BF16, "hsb0", HS_0_AT), held([P, T, 4], BF16, "hsb1")]
+        hs = placed([P, G * T, 4], BF16, "hs", H_1_AT)
         for step in (1, 2):
             shared_relu(False, step)
         for unit, number in enumerate((3, 4, 5, 6)):
@@ -266,8 +262,8 @@ def tile_moe_shf_mlp_relu2_kernel(
                 vector_square(step - 1)
         gated(3)
         vector_square(7)
-        for step in range(5):
-            nc.gpsimd.tensor_tensor(quarter(hsb, step), relu_s[step], relu_s[step], ALU.mult)
+        for first, last in zip(GPSIMD_COLUMNS, GPSIMD_COLUMNS[1:]):
+            nc.gpsimd.tensor_tensor(hs[:, first:last, :], relus[:, first:last, :], relus[:, first:last, :], ALU.mult)
 
         def scatter(on_vector, t, first, last, values):
             out = win[t][:].indirect(slots(first, last))
@@ -280,8 +276,8 @@ def tile_moe_shf_mlp_relu2_kernel(
         deal(w2sp[:], w2sw[:].rearrange("p g n -> p (g n)"), 4)
         hsq = [placed([P, T], U32, "hsq0", HS_0_CODES_AT), held([P, T], U32, "w2sw")]
         for g in range(G):
-            quantize(hsq[g][:], hssc[g][:], hsb[g][:])
-        win = [held([P, T], F32, name) for name in ("win0", "win1", "win2", "hsb1")]
+            quantize(hsq[g][:], hssc[g][:], hs[:, T * g : T * (g + 1), :])
+        win = [held([P, T], F32, "win%d" % t) for t in range(3)] + [placed([P, T], F32, "win3", H_1_AT)]
         last_rows = whole[3][:].rearrange("p a s -> p (a s)")
         scatter(True, 3, SCALAR_SLOTS, T, last_rows[:, SCALAR_SLOTS:T])
         for unit in UNITS[:3]:
@@ -290,8 +286,8 @@ def tile_moe_shf_mlp_relu2_kernel(
         scatter(False, 3, 0, SCALAR_SLOTS, last_rows[:, 0:SCALAR_SLOTS])
 
         ys = [bank(number, [P, T]) for number in (7, 0, 1, 2)]
-        for t, g in ((0, 0), (1, 0), (0, 1), (1, 1), (2, 0), (2, 1), (3, 0), (3, 1)):
-            if True:
+        for rows_at_once in ((0, 1), (2,), (3,)):
+            for g, t in itertools.product(range(G), rows_at_once):
                 nc.tensor.matmul_mx(
                     out=ys[t][:],
                     lhsT=w2sp[:, PASS * g + P * t : PASS * g + P * (t + 1)].bitcast(FP8X4),

@@ -24,7 +24,7 @@ G = HS // PASS
 HALF = T // 2
 ROW = 4 * T
 
-SCALAR_SLOTS = 160
+SCALAR_SLOTS = 128
 GPSIMD_COLUMNS = (0, 128, 384, 640)
 SCALAR_TOKENS = 192
 UNITS = (((0, 0), (1, 0)), ((2, 0), (0, 1)), ((1, 1), (2, 1)), ((3, 0), (3, 1)))
@@ -84,20 +84,20 @@ def tile_moe_shf_mlp_relu2_kernel(
                 out=xs[32 * q : 32 * q + 4, :].bitcast(I32),
                 in_=x_scales[0, 4 * q : 4 * q + 4, :].bitcast(I32),
             )
-        nc.sync.dma_start(out=w1sw[:], in_=w1s_words[0].rearrange("p l d -> p (l d)").bitcast(I32))
         load_words(w1w[0], w1_words[0:2])
-        for q in range(4):
-            nc.sync.dma_start(
-                out=w1sc[32 * q : 32 * q + 4, :].bitcast(I32).rearrange("r (e n) -> r e n", e=E),
-                in_=w1_scales[:, 0, 4 * q : 4 * q + 4, :].rearrange("e r n -> r e n").bitcast(I32),
-            )
-        load_words(w1w[1], w1_words[2:4])
+        nc.sync.dma_start(out=w1sw[:], in_=w1s_words[0].rearrange("p l d -> p (l d)").bitcast(I32))
         nc.sync.dma_start(
             out=packed[0:64, :].bitcast(I32), in_=w2_scales[:, 0].rearrange("e b n -> b e n").bitcast(I32)
         )
         nc.sync.dma_start(
             out=packed[64:96, :].bitcast(I32), in_=w2s_scales.rearrange("g b n -> b g n").bitcast(I32)
         )
+        for q in range(4):
+            nc.sync.dma_start(
+                out=w1sc[32 * q : 32 * q + 4, :].bitcast(I32).rearrange("r (e n) -> r e n", e=E),
+                in_=w1_scales[:, 0, 4 * q : 4 * q + 4, :].rearrange("e r n -> r e n").bitcast(I32),
+            )
+        load_words(w1w[1], w1_words[2:4])
         for q in range(4):
             nc.sync.dma_start(
                 out=w1ssc[32 * q : 32 * q + 4 * G, :].bitcast(I32),
@@ -167,7 +167,7 @@ def tile_moe_shf_mlp_relu2_kernel(
             )
 
         def routed_relu(e, sorted_relu):
-            relu(e == 0, sorted_relu, pre_r[e][:].rearrange("s (p t) -> s t p", t=4))
+            relu(e % 3 == 0, sorted_relu, pre_r[e][:].rearrange("s (p t) -> s t p", t=4))
             turned[e] = bank(4 + e, [P, 4, C])
             for t in range(4):
                 nc.tensor.transpose(turned[e][:, t, :], sorted_relu[:, t, :], ident[:])

@@ -23,19 +23,21 @@ PASS = 512
 G = HS // PASS
 HALF = T // 2
 ROW = 4 * T
+STEPS = 4 * G
 
-SCALAR_SLOTS = 128
-GPSIMD_COLUMNS = (0, 128, 384, 640)
-SCALAR_TOKENS = 192
 UNITS = (((0, 0), (1, 0)), ((2, 0), (0, 1)), ((1, 1), (2, 1)), ((3, 0), (3, 1)))
+GPSIMD_STEPS = (0, 1, 3, 5)
+SCALAR_STEPS = 2
+VECTOR_SLOTS = 192
+SCALAR_TOKENS = 192
 
-H_0_CODES_AT = 0
-W2_WORDS_AT = ROW // 4
-RELUS_AT = ROW
-H_1_AT = 9 * ROW
-W2S_DEALT_AT = 13 * ROW
-GATES_AT = W2S_DEALT_AT + 2 * ROW - ROW // 2
-HS_0_CODES_AT = W2S_DEALT_AT + 2 * ROW
+W2_ROWS_AT = 0
+W2_WORDS_AT = 2 * ROW
+H_1_AT = 3 * ROW
+LAST_RELUS_AT = 12 * ROW
+W2S_DEALT_AT = LAST_RELUS_AT - ROW // 2 + 64
+W2S_PLANE_AT = LAST_RELUS_AT + 64
+HS_0_CODES_AT = LAST_RELUS_AT + ROW // 2
 
 
 def tile_moe_shf_mlp_relu2_kernel(
@@ -60,67 +62,76 @@ def tile_moe_shf_mlp_relu2_kernel(
         offsets = keep.tile([P, T // 16], U16, name="offsets")
         xw = held([P, T], I32, "xw")
         xs = held([P, T], U8, "xs")
+        xs_rows = held([4, 4 * T], U8, "xs_rows")
         w1sc = held([P, E * H], U8, "w1sc")
-        ident = held([P, P], F32, "ident")
-        packed = held([P, PASS], U8, "packed")
+        w2sc = placed([P, E * N], U8, "w2sc", W2_ROWS_AT)
         w1ssc = held([P, PASS], U8, "w1ssc")
-        nc.gpsimd.memset(xs[:].bitcast(I32), 0)
-        nc.vector.memset(packed[:].bitcast(I32), 0)
+        w2ssc = held([P, N], U8, "w2ssc")
+        ident = held([P, P], F32, "ident")
+        nc.vector.memset(xs[:].bitcast(I32), 0)
+        nc.vector.memset(w2sc[:].bitcast(I32), 0)
         nc.vector.memset(w1ssc[:].bitcast(I32), 0)
+        nc.vector.memset(w2ssc[:].bitcast(I32), 0)
 
         w1w = [held([P, 2, 2 * H], U8, "w1w%d" % a) for a in range(2)]
-        w2w = [placed([P, 2, 2 * N], U8, "w2w0", W2_WORDS_AT), held([P, 2, 2 * N], U8, "w2w1")]
+        w2w = [held([P, 2, 2 * N], U8, "w2w0"), placed([P, 2, 2 * N], U8, "w2w1", W2_WORDS_AT)]
         w1sw = held([P, HS], I32, "w1sw")
         w2sw = held([P, G, N], I32, "w2sw")
-        gates = placed([P, T], F32, "gates", GATES_AT)
+        gates = held([P, T], F32, "gates")
 
         def load_words(tile, words):
             nc.sync.dma_start(out=tile[:].bitcast(I32), in_=words[:, 0].rearrange("e p b -> p e b").bitcast(I32))
 
-        nc.sync.dma_start(offsets[:], offs)
+        def load_expert_planes(tile, scales):
+            for r in range(4):
+                nc.sync.dma_start(
+                    out=tile[r:P:32, :].bitcast(I32).rearrange("q (e n) -> q e n", e=E),
+                    in_=scales[:, 0, r:16:4, :].rearrange("e q n -> q e n").bitcast(I32),
+                )
+
+        def load_pass_planes(tile, rows):
+            for q in range(4):
+                nc.sync.dma_start(out=tile[32 * q : 32 * q + 4 * G, :].bitcast(I32), in_=rows(q).bitcast(I32))
+
+        nc.sync.dma_start(
+            out=xs_rows[:].bitcast(I32).rearrange("r (q t) -> r q t", q=4),
+            in_=x_scales[0].rearrange("(q r) t -> r q t", r=4).bitcast(I32),
+        )
         nc.sync.dma_start(out=xw[:], in_=x_words[0].rearrange("p t d -> p (t d)").bitcast(I32))
-        for q in range(4):
-            nc.sync.dma_start(
-                out=xs[32 * q : 32 * q + 4, :].bitcast(I32),
-                in_=x_scales[0, 4 * q : 4 * q + 4, :].bitcast(I32),
-            )
+        nc.sync.dma_start(offsets[:], offs)
+        load_expert_planes(w1sc, w1_scales)
         load_words(w1w[0], w1_words[0:2])
-        nc.sync.dma_start(out=w1sw[:], in_=w1s_words[0].rearrange("p l d -> p (l d)").bitcast(I32))
-        nc.sync.dma_start(
-            out=packed[0:64, :].bitcast(I32), in_=w2_scales[:, 0].rearrange("e b n -> b e n").bitcast(I32)
-        )
-        nc.sync.dma_start(
-            out=packed[64:96, :].bitcast(I32), in_=w2s_scales.rearrange("g b n -> b g n").bitcast(I32)
-        )
-        for q in range(4):
-            nc.sync.dma_start(
-                out=w1sc[32 * q : 32 * q + 4, :].bitcast(I32).rearrange("r (e n) -> r e n", e=E),
-                in_=w1_scales[:, 0, 4 * q : 4 * q + 4, :].rearrange("e r n -> r e n").bitcast(I32),
-            )
         load_words(w1w[1], w1_words[2:4])
-        for q in range(4):
-            nc.sync.dma_start(
-                out=w1ssc[32 * q : 32 * q + 4 * G, :].bitcast(I32),
-                in_=w1s_scales[0, 4 * q : 4 * q + 4, :].rearrange("r (g l) -> g r l", g=G).bitcast(I32),
-            )
         load_words(w2w[0], w2_words[0:2])
+        load_expert_planes(w2sc, w2_scales)
+        nc.sync.dma_start(out=w1sw[:], in_=w1s_words[0].rearrange("p l d -> p (l d)").bitcast(I32))
+        load_pass_planes(w1ssc, lambda q: w1s_scales[0, 4 * q : 4 * q + 4, :].rearrange("r (g l) -> g r l", g=G))
         load_words(w2w[1], w2_words[2:4])
+        nc.sync.dma_start(out=gates[:], in_=gate)
+        nc.sync.dma_start(out=w2sw[:], in_=w2s_words.rearrange("g p n d -> p g (n d)").bitcast(I32))
+        load_pass_planes(w2ssc, lambda q: w2s_scales[:, 4 * q : 4 * q + 4, :])
         make_identity(nc, ident[:])
 
-        xg = [held([P, C], U32, "xg0"), held([P, 3 * C], U32, "xg1")]
-        xgs = [held([P, C], U8, "xgs0"), held([P, 3 * C], U8, "xgs1")]
+        for q in range(4):
+            nc.vector.tensor_copy(
+                xs[32 * q : 32 * q + 4, :].bitcast(I32), xs_rows[:, T * q : T * (q + 1)].bitcast(I32)
+            )
+
+        xg = held([P, T], U32, "xg")
+        xgs = held([P, T], U8, "xgs")
         w2p = [held([P, 2, 2 * N], U8, "w2p%d" % a) for a in range(2)]
         w2scp = held([P, E * N], U8, "w2scp")
         w1sscp = held([P, PASS], U8, "w1sscp")
-        dealt_rows = held([P, PASS], U8, "dealt_rows")
-        w2sscp = held([P, G * N], U8, "w2sscp")
         hb = [held([P, HALF, 4], BF16, "hb0"), placed([P, HALF, 4], BF16, "hb1", H_1_AT)]
         hsc = held([P, E * C], U8, "hsc")
         w1sp = held([P, HS], I32, "w1sp")
         hssc = [held([P, T], U8, "hssc%d" % g) for g in range(G)]
+        own = GPSIMD_STEPS[-1]
+        relus = held([P, own * P, 4], F32, "relus")
+        last_relus = placed([P, (STEPS - own) * P, 4], F32, "last_relus", LAST_RELUS_AT)
 
-        def slots(first, last):
-            return offsets[:, first // 16 : last // 16]
+        def slots(e):
+            return offsets[:, C * e // 16 : C * (e + 1) // 16]
 
         def deal(out, in_, run, copy=nc.vector.tensor_copy):
             copy(
@@ -128,20 +139,13 @@ def tile_moe_shf_mlp_relu2_kernel(
                 in_=in_.rearrange("p (g c i t) -> p g c t i", t=4, c=P // run, i=run),
             )
 
-        def deal_w2(a):
+        def deal_w2_words(a):
             flat = "p e b -> p (e b)"
             deal(w2p[a][:].rearrange(flat).bitcast(U16), w2w[a][:].rearrange(flat).bitcast(U16), 8)
 
-        def gather(a, first, last):
-            nc.vector.tensor_copy(xg[a][:], xw[:].bitcast(U32).indirect(slots(first, last)))
-            nc.vector.tensor_copy(xgs[a][:], xs[:].indirect(slots(first, last)))
-
-        def place_planes(tile, first, count):
-            for q in range(4):
-                nc.sync.dma_start(
-                    out=tile[32 * q : 32 * q + 4, :].bitcast(I32).rearrange("r (a n) -> r a n", a=count),
-                    in_=dealt_rows[first + 4 * count * q : first + 4 * count * (q + 1), :].bitcast(I32),
-                )
+        def deal_w2_plane(a):
+            cols = slice(2 * N * a, 2 * N * (a + 1))
+            deal(w2scp[:, cols], w2sc[:, cols], 16)
 
         def relu(on_vector, dst, src):
             if on_vector:
@@ -155,19 +159,22 @@ def tile_moe_shf_mlp_relu2_kernel(
         def quantize(codes, scales, values):
             nc.vector.quantize_mx(out=codes.bitcast(FP8X4), scales=scales, in_=values.rearrange("p s t -> p (s t)"))
 
-        pre_r, turned, pre_s, sums, y, whole = {}, {}, {}, {}, {}, {}
+        pre_r, turned, pre_s, sums, y = {}, {}, {}, {}, {}
 
-        def routed_first(e):
-            a, at = (0, 0) if e == 0 else (1, C * (e - 1))
-            pre_r[e] = bank(e, [P, H])
+        def routed_first(e, number):
+            cols = slice(C * e, C * (e + 1))
+            nc.vector.tensor_copy(xg[:, cols], xw[:].bitcast(U32).indirect(slots(e)))
+            nc.vector.tensor_copy(xgs[:, cols], xs[:].indirect(slots(e)))
+            pre_r[e] = bank(number, [P, H])
             nc.tensor.matmul_mx(
-                out=pre_r[e][:], lhsT=xg[a][:, at : at + C].bitcast(FP8X4), lhsT_scale=xgs[a][:, at : at + C],
+                out=pre_r[e][:], lhsT=xg[:, cols].bitcast(FP8X4), lhsT_scale=xgs[:, cols],
                 rhs=w1w[e // 2][:, e % 2, :].bitcast(FP4X4), rhs_scale=w1sc[:, H * e : H * (e + 1)],
                 start=True, stop=True,
             )
 
-        def routed_relu(e, sorted_relu):
-            relu(e % 3 == 0, sorted_relu, pre_r[e][:].rearrange("s (p t) -> s t p", t=4))
+        def routed_relu(e):
+            sorted_relu = held([P, 4, P], F32, "relu_r%d" % e)
+            relu(False, sorted_relu[:], pre_r[e][:].rearrange("s (p t) -> s t p", t=4))
             turned[e] = bank(4 + e, [P, 4, C])
             for t in range(4):
                 nc.tensor.transpose(turned[e][:, t, :], sorted_relu[:, t, :], ident[:])
@@ -175,28 +182,6 @@ def tile_moe_shf_mlp_relu2_kernel(
         def routed_square(e):
             nc.scalar.activation(
                 hb[e // 2][:, C * (e % 2) : C * (e % 2 + 1), :], turned[e][:].rearrange("p t s -> p s t"), ACT.Square
-            )
-
-        def shared_first(step, number):
-            g, u = divmod(step, 4)
-            pre_s[step] = bank(number, [P, 4, P])
-            for t in range(4):
-                nc.tensor.matmul_mx(
-                    out=pre_s[step][:, t, :],
-                    lhsT=w1sp[:, PASS * g + P * t : PASS * g + P * (t + 1)].bitcast(FP8X4),
-                    lhsT_scale=w1sscp[4 * g : P, P * t : P * (t + 1)],
-                    rhs=xw[:, P * u : P * (u + 1)].bitcast(FP8X4), rhs_scale=xs[:, P * u : P * (u + 1)],
-                    start=True, stop=True,
-                )
-
-        def shared_relu(on_vector, step):
-            relu(on_vector, relus[:, P * step : P * (step + 1), :], pre_s[step][:].rearrange("p t s -> p s t"))
-
-        def vector_square(step):
-            cols = slice(P * step, P * (step + 1))
-            nc.vector.scalar_tensor_tensor(
-                hs[:, cols, :], pre_s[step][:].rearrange("p t s -> p s t"), 0.0, relus[:, cols, :],
-                ALU.max, ALU.mult,
             )
 
         def routed_second(unit, number):
@@ -217,92 +202,117 @@ def tile_moe_shf_mlp_relu2_kernel(
             weights = gates[:].rearrange("p (a s) -> p a s", a=2)
             if a0 == a1:
                 weights = weights[:, a0 : a0 + 1, :].to_broadcast([P, 2, HALF])
-            both = held([P, 2, HALF], F32, "y%d" % unit)
-            nc.vector.tensor_tensor(both[:], weights, sums[unit][:], ALU.mult)
-            y[t0, a0], y[t1, a1] = both[:, 0, :], both[:, 1, :]
-            whole[unit] = both
-
-        gather(0, 0, C)
-        gather(1, C, T)
-        for e in range(E):
-            routed_first(e)
-        deal(w1sp[:].bitcast(U32), w1sw[:].bitcast(U32), 4, nc.scalar.copy)
-        deal(dealt_rows[:], packed[:], 16)
-        place_planes(w2scp, 0, E)
-        nc.sync.dma_start(out=gates[:], in_=gate)
-        place_planes(w2sscp, 64, G)
-        nc.sync.dma_start(out=w2sw[:], in_=w2s_words.rearrange("g p n d -> p g (n d)").bitcast(I32))
-        for e in range(E):
-            routed_relu(e, held([P, 4, P], F32, "relu_r%d" % e)[:])
-        deal(w1sscp[:], w1ssc[:], 16)
-        for e in range(E):
-            routed_square(e)
-        deal_w2(0)
-
-        for step, number in ((0, 0), (1, 1), (2, 2)):
-            shared_first(step, number)
-        hq = [placed([P, HALF], U32, "hq0", H_0_CODES_AT)]
-        relus = placed([P, G * T, 4], F32, "relus", RELUS_AT)
-        quantize(hq[0][:], hsc[:, 0:HALF], hb[0][:])
-        shared_relu(True, 0)
-        deal_w2(1)
-        hq.append(held([P, HALF], U32, "w2w1"))
-        quantize(hq[1][:], hsc[:, HALF:T], hb[1][:])
-        hs = placed([P, G * T, 4], BF16, "hs", H_1_AT)
-        for step in (1, 2):
-            shared_relu(False, step)
-        for unit, number in enumerate((3, 4, 5, 6)):
-            routed_second(unit, number)
-        for unit in range(3):
-            gated(unit)
-        for step, number in ((3, 3), (4, 4), (5, 5), (6, 3), (7, 4)):
-            shared_first(step, number)
-            shared_relu(True, step)
-            if step > 5:
-                vector_square(step - 1)
-        gated(3)
-        vector_square(7)
-        for first, last in zip(GPSIMD_COLUMNS, GPSIMD_COLUMNS[1:]):
-            nc.gpsimd.tensor_tensor(hs[:, first:last, :], relus[:, first:last, :], relus[:, first:last, :], ALU.mult)
+            y[unit] = held([P, 2, HALF], F32, "y%d" % unit)
+            nc.vector.tensor_tensor(y[unit][:], weights, sums[unit][:], ALU.mult)
 
         def scatter(on_vector, t, first, last, values):
-            out = win[t][:].indirect(slots(first, last))
+            out = win[t][:].indirect(offsets[:, first // 16 : last // 16])
             if on_vector:
                 nc.vector.tensor_copy(out, values)
             else:
                 nc.scalar.activation(out, values, ACT.Copy)
 
-        w2sp = placed([P, HS], I32, "w2sp", W2S_DEALT_AT)
-        deal(w2sp[:], w2sw[:].rearrange("p g n -> p (g n)"), 4)
-        hsq = [placed([P, T], U32, "hsq0", HS_0_CODES_AT), held([P, T], U32, "w2sw")]
+        def relu_of(step):
+            tile, at = (relus, step) if step < own else (last_relus, step - own)
+            return tile[:, P * at : P * (at + 1), :]
+
+        def shared_first(step):
+            g, u = divmod(step, 4)
+            pre_s[step] = bank(4 + u, [P, 4, P])
+            for t in range(4):
+                nc.tensor.matmul_mx(
+                    out=pre_s[step][:, t, :],
+                    lhsT=w1sp[:, PASS * g + P * t : PASS * g + P * (t + 1)].bitcast(FP8X4),
+                    lhsT_scale=w1sscp[4 * g : P, P * t : P * (t + 1)],
+                    rhs=xw[:, P * u : P * (u + 1)].bitcast(FP8X4), rhs_scale=xs[:, P * u : P * (u + 1)],
+                    start=True, stop=True,
+                )
+            relu(step >= SCALAR_STEPS, relu_of(step), pre_s[step][:].rearrange("p t s -> p s t"))
+
+        def vector_square(step):
+            nc.vector.scalar_tensor_tensor(
+                hs[:, P * step : P * (step + 1), :], pre_s[step][:].rearrange("p t s -> p s t"), 0.0, relu_of(step),
+                ALU.max, ALU.mult,
+            )
+
+        for e in range(3):
+            routed_first(e, e)
+        routed_relu(0)
+        routed_first(3, 0)
+        routed_relu(1)
+        routed_relu(2)
+        routed_square(0)
+        routed_square(1)
+        routed_relu(3)
+        routed_square(2)
+        routed_square(3)
+        deal_w2_words(0)
+        deal_w2_plane(0)
+        deal_w2_plane(1)
+        hq = [placed([P, HALF], U32, "hq0", W2_ROWS_AT)]
+        quantize(hq[0][:], hsc[:, 0:HALF], hb[0][:])
+        routed_second(0, 3)
+        deal(w1sp[:], w1sw[:], 4)
+        deal(w1sscp[:], w1ssc[:], 16)
+        deal_w2_words(1)
+        gated(0)
+        hq.append(placed([P, HALF], U32, "hq1", W2_WORDS_AT))
+        quantize(hq[1][:], hsc[:, HALF:T], hb[1][:])
+        hs = placed([P, G * T, 4], BF16, "hs", H_1_AT)
+        routed_second(1, 1)
+        routed_second(2, 2)
+        routed_second(3, 0)
+
+        for step in range(STEPS):
+            shared_first(step)
+            if step == 4:
+                gated(1)
+        gated(2)
+        for step in range(own, STEPS):
+            vector_square(step)
+        gated(3)
+        for first, last in zip(GPSIMD_STEPS, GPSIMD_STEPS[1:]):
+            cols = slice(P * first, P * last)
+            nc.gpsimd.tensor_tensor(hs[:, cols, :], relus[:, cols, :], relus[:, cols, :], ALU.mult)
+
+        def deal_w2s(tile, first, last):
+            nc.vector.tensor_copy(
+                out=tile[:].rearrange("p g t (c i) -> p g c t i", i=4),
+                in_=w2sw[:].rearrange("p g (c i t) -> p g c t i", i=4, t=4)[:, :, :, first:last, :],
+            )
+
+        w2sp = [placed([P, G, 1, P], I32, "w2sp0", W2S_DEALT_AT)]
+        deal_w2s(w2sp[0], 0, 1)
+        w2sscp = placed([P, N], U8, "w2sscp", W2S_PLANE_AT)
+        deal(w2sscp[:], w2ssc[:], 16)
+        hsq = [placed([P, T], U32, "hsq0", HS_0_CODES_AT), held([P, T], U32, "hsq1")]
         for g in range(G):
             quantize(hsq[g][:], hssc[g][:], hs[:, T * g : T * (g + 1), :])
+        w2sp.append(placed([P, G, 3, P], I32, "w2sp1", H_1_AT + ROW))
+        deal_w2s(w2sp[1], 1, 4)
         win = [held([P, T], F32, "win%d" % t) for t in range(3)] + [placed([P, T], F32, "win3", H_1_AT)]
-        last_rows = whole[3][:].rearrange("p a s -> p (a s)")
-        scatter(True, 3, SCALAR_SLOTS, T, last_rows[:, SCALAR_SLOTS:T])
-        for unit in UNITS[:3]:
-            for t, a in unit:
-                scatter(False, t, HALF * a, HALF * (a + 1), y[t, a])
-        scatter(False, 3, 0, SCALAR_SLOTS, last_rows[:, 0:SCALAR_SLOTS])
+        last_rows = y[3][:].rearrange("p a s -> p (a s)")
+        scatter(True, 3, T - VECTOR_SLOTS, T, last_rows[:, T - VECTOR_SLOTS : T])
+        for unit in range(3):
+            for j, (t, a) in enumerate(UNITS[unit]):
+                scatter(False, t, HALF * a, HALF * (a + 1), y[unit][:, j, :])
+        scatter(False, 3, 0, T - VECTOR_SLOTS, last_rows[:, 0 : T - VECTOR_SLOTS])
 
-        ys = [bank(number, [P, T]) for number in (7, 0, 1, 2)]
-        for rows_at_once in ((0, 1), (2,), (3,)):
-            for g, t in itertools.product(range(G), rows_at_once):
-                nc.tensor.matmul_mx(
-                    out=ys[t][:],
-                    lhsT=w2sp[:, PASS * g + P * t : PASS * g + P * (t + 1)].bitcast(FP8X4),
-                    lhsT_scale=w2sscp[:, N * g + P * t : N * g + P * (t + 1)],
-                    rhs=hsq[g][:].bitcast(FP8X4), rhs_scale=hssc[g][:],
-                    start=(g == 0), stop=(g == G - 1),
-                )
+        ys = [bank(number, [P, T]) for number in (3, 1, 2, 0)]
+        for t, g in itertools.product(range(4), range(G)):
+            nc.tensor.matmul_mx(
+                out=ys[t][:],
+                lhsT=(w2sp[0][:, g, 0, :] if t == 0 else w2sp[1][:, g, t - 1, :]).bitcast(FP8X4),
+                lhsT_scale=w2sscp[4 * g : P, P * t : P * (t + 1)],
+                rhs=hsq[g][:].bitcast(FP8X4), rhs_scale=hssc[g][:],
+                start=(g == 0), stop=(g == G - 1),
+            )
 
         total = held([P, 4, T], F32, "total")
         rows = out_0.rearrange("(p t) c -> p t c", t=4)
         for t in range(4):
             nc.vector.tensor_tensor(total[:, t, :], ys[t][:], win[t][:], ALU.add)
-            if t > 0:
-                first = 0 if t == 1 else t
-                nc.sync.dma_start(out=rows[:, first : t + 1, :], in_=total[:, first : t + 1, :])
+            nc.sync.dma_start(out=rows[:, t, :], in_=total[:, t, :])
 
         oq = held([P, T], U32, "oq")
         osc = held([P, T], U8, "osc")

@@ -61,7 +61,7 @@ def tile_moe_shf_mlp_relu2_kernel(
 
         offsets = keep.tile([P, T // 16], U16, name="offsets")
         xw = held([P, T], I32, "xw")
-        xs = held([P, T], U8, "xs")
+        xs = held([P, 2 * T], U8, "xs")
         xs_rows = held([4, 4 * T], U8, "xs_rows")
         w1sc = held([P, E * H], U8, "w1sc")
         w2sc = placed([P, E * N], U8, "w2sc", W2_ROWS_AT)
@@ -112,10 +112,10 @@ def tile_moe_shf_mlp_relu2_kernel(
         load_pass_planes(w2ssc, lambda q: w2s_scales[:, 4 * q : 4 * q + 4, :])
         make_identity(nc, ident[:])
 
-        for q in range(4):
-            nc.vector.tensor_copy(
-                xs[32 * q : 32 * q + 4, :].bitcast(I32), xs_rows[:, T * q : T * (q + 1)].bitcast(I32)
-            )
+        staged = xs_rows[:].bitcast(I32).rearrange("r (a b t) -> r b a t", a=2, b=2)
+        for b in range(2):
+            nc.vector.tensor_copy(xs[32 * b : 32 * b + 4, :].bitcast(I32).rearrange("r (a t) -> r a t", a=2), staged[:, b])
+        nc.vector.tensor_copy(xs[64:P, 0:T].bitcast(I32), xs[0:64, T : 2 * T].bitcast(I32))
 
         xg = held([P, T], U32, "xg")
         xgs = held([P, T], U8, "xgs")
@@ -164,7 +164,7 @@ def tile_moe_shf_mlp_relu2_kernel(
         def routed_first(e, number):
             cols = slice(C * e, C * (e + 1))
             nc.vector.tensor_copy(xg[:, cols], xw[:].bitcast(U32).indirect(slots(e)))
-            nc.vector.tensor_copy(xgs[:, cols], xs[:].indirect(slots(e)))
+            nc.vector.tensor_copy(xgs[:, cols], xs[:, 0:T].indirect(slots(e)))
             pre_r[e] = bank(number, [P, H])
             nc.tensor.matmul_mx(
                 out=pre_r[e][:], lhsT=xg[:, cols].bitcast(FP8X4), lhsT_scale=xgs[:, cols],

@@ -25,10 +25,10 @@ HALF = T // 2
 ROW = 4 * T
 STEPS = 4 * G
 
-UNITS = (((0, 0), (1, 0)), ((2, 0), (0, 1)), ((1, 1), (2, 1)), ((3, 0), (3, 1)))
-GPSIMD_STEPS = (0, 1, 3, 5)
+UNITS = (((0, 0), (1, 0)), ((2, 0), (3, 0)), ((0, 1), (1, 1)), ((2, 1), (3, 1)))
+GPSIMD_STEPS = (0, 1, 4, 5)
 SCALAR_STEPS = 2
-VECTOR_SLOTS = 192
+VECTOR_SLOTS = 160
 SCALAR_TOKENS = 192
 
 W2_ROWS_AT = 0
@@ -37,7 +37,7 @@ H_1_AT = 3 * ROW
 LAST_RELUS_AT = 12 * ROW
 W2S_DEALT_AT = LAST_RELUS_AT - ROW // 2 + 64
 W2S_PLANE_AT = LAST_RELUS_AT + 64
-HS_0_CODES_AT = LAST_RELUS_AT + ROW // 2
+RELUS_AT = 5 * ROW
 
 
 def tile_moe_shf_mlp_relu2_kernel(
@@ -127,7 +127,7 @@ def tile_moe_shf_mlp_relu2_kernel(
         w1sp = held([P, HS], I32, "w1sp")
         hssc = [held([P, T], U8, "hssc%d" % g) for g in range(G)]
         own = GPSIMD_STEPS[-1]
-        relus = held([P, own * P, 4], F32, "relus")
+        relus = placed([P, own * P, 4], F32, "relus", RELUS_AT)
         last_relus = placed([P, (STEPS - own) * P, 4], F32, "last_relus", LAST_RELUS_AT)
 
         def slots(e):
@@ -197,13 +197,12 @@ def tile_moe_shf_mlp_relu2_kernel(
                         start=True, stop=True,
                     )
 
-        def gated(unit):
-            (t0, a0), (t1, a1) = UNITS[unit]
-            weights = gates[:].rearrange("p (a s) -> p a s", a=2)
-            if a0 == a1:
-                weights = weights[:, a0 : a0 + 1, :].to_broadcast([P, 2, HALF])
-            y[unit] = held([P, 2, HALF], F32, "y%d" % unit)
-            nc.vector.tensor_tensor(y[unit][:], weights, sums[unit][:], ALU.mult)
+        def gated(unit, first, last, tile):
+            a = unit // 2
+            weights = gates[:, HALF * a : HALF * (a + 1)].unsqueeze(1).to_broadcast([P, last - first, HALF])
+            nc.vector.tensor_tensor(tile[:], weights, sums[unit][:, first:last, :], ALU.mult)
+            for j in range(first, last):
+                y[UNITS[unit][j]] = tile[:, j - first, :]
 
         def scatter(on_vector, t, first, last, values):
             out = win[t][:].indirect(offsets[:, first // 16 : last // 16])
@@ -231,7 +230,7 @@ def tile_moe_shf_mlp_relu2_kernel(
 
         def vector_square(step):
             nc.vector.scalar_tensor_tensor(
-                hs[:, P * step : P * (step + 1), :], pre_s[step][:].rearrange("p t s -> p s t"), 0.0, relu_of(step),
+                hs[1][:, P * (step - 4) : P * (step - 3), :], pre_s[step][:].rearrange("p t s -> p s t"), 0.0, relu_of(step),
                 ALU.max, ALU.mult,
             )
 
@@ -252,28 +251,28 @@ def tile_moe_shf_mlp_relu2_kernel(
         hq = [placed([P, HALF], U32, "hq0", W2_ROWS_AT)]
         quantize(hq[0][:], hsc[:, 0:HALF], hb[0][:])
         routed_second(0, 3)
+        routed_second(1, 1)
         deal(w1sp[:], w1sw[:], 4)
         deal(w1sscp[:], w1ssc[:], 16)
         deal_w2_words(1)
-        gated(0)
+        gated(0, 0, 2, held([P, 2, HALF], F32, "y0"))
         hq.append(placed([P, HALF], U32, "hq1", W2_WORDS_AT))
         quantize(hq[1][:], hsc[:, HALF:T], hb[1][:])
-        hs = placed([P, G * T, 4], BF16, "hs", H_1_AT)
-        routed_second(1, 1)
+        hs = [placed([P, T, 4], BF16, "hs0", H_1_AT), held([P, T, 4], BF16, "hs1")]
         routed_second(2, 2)
         routed_second(3, 0)
 
         for step in range(STEPS):
             shared_first(step)
             if step == 4:
-                gated(1)
-        gated(2)
+                gated(1, 0, 2, held([P, 2, HALF], F32, "y1"))
+        gated(2, 0, 2, held([P, 2, HALF], F32, "y2"))
         for step in range(own, STEPS):
             vector_square(step)
-        gated(3)
+        gated(3, 0, 1, held([P, 1, HALF], F32, "y3"))
         for first, last in zip(GPSIMD_STEPS, GPSIMD_STEPS[1:]):
-            cols = slice(P * first, P * last)
-            nc.gpsimd.tensor_tensor(hs[:, cols, :], relus[:, cols, :], relus[:, cols, :], ALU.mult)
+            values, at = relus[:, P * first : P * last, :], P * (first % 4)
+            nc.gpsimd.tensor_tensor(hs[first // 4][:, at : at + P * (last - first), :], values, values, ALU.mult)
 
         def deal_w2s(tile, first, last):
             nc.vector.tensor_copy(
@@ -285,18 +284,17 @@ def tile_moe_shf_mlp_relu2_kernel(
         deal_w2s(w2sp[0], 0, 1)
         w2sscp = placed([P, N], U8, "w2sscp", W2S_PLANE_AT)
         deal(w2sscp[:], w2ssc[:], 16)
-        hsq = [placed([P, T], U32, "hsq0", HS_0_CODES_AT), held([P, T], U32, "hsq1")]
+        hsq = [placed([P, T], U32, "hsq0", RELUS_AT), held([P, T], U32, "hsq1")]
         for g in range(G):
-            quantize(hsq[g][:], hssc[g][:], hs[:, T * g : T * (g + 1), :])
-        w2sp.append(placed([P, G, 3, P], I32, "w2sp1", H_1_AT + ROW))
+            quantize(hsq[g][:], hssc[g][:], hs[g][:])
+        gated(3, 1, 2, placed([P, 1, HALF], F32, "y4", H_1_AT))
+        w2sp.append(placed([P, G, 3, P], I32, "w2sp1", H_1_AT + ROW // 2))
         deal_w2s(w2sp[1], 1, 4)
-        win = [held([P, T], F32, "win%d" % t) for t in range(3)] + [placed([P, T], F32, "win3", H_1_AT)]
-        last_rows = y[3][:].rearrange("p a s -> p (a s)")
-        scatter(True, 3, T - VECTOR_SLOTS, T, last_rows[:, T - VECTOR_SLOTS : T])
-        for unit in range(3):
-            for j, (t, a) in enumerate(UNITS[unit]):
-                scatter(False, t, HALF * a, HALF * (a + 1), y[unit][:, j, :])
-        scatter(False, 3, 0, T - VECTOR_SLOTS, last_rows[:, 0 : T - VECTOR_SLOTS])
+        win = [held([P, T], F32, "win%d" % t) for t in range(4)]
+        for a, t in list(itertools.product(range(2), range(4)))[:-1]:
+            scatter(False, t, HALF * a, HALF * (a + 1), y[t, a])
+        scatter(True, 3, HALF, HALF + VECTOR_SLOTS, y[3, 1][:, 0:VECTOR_SLOTS])
+        scatter(False, 3, HALF + VECTOR_SLOTS, T, y[3, 1][:, VECTOR_SLOTS:HALF])
 
         ys = [bank(number, [P, T]) for number in (3, 1, 2, 0)]
         for t, g in itertools.product(range(4), range(G)):
@@ -310,9 +308,13 @@ def tile_moe_shf_mlp_relu2_kernel(
 
         total = held([P, 4, T], F32, "total")
         rows = out_0.rearrange("(p t) c -> p t c", t=4)
-        for t in range(4):
+        for t in range(3):
             nc.vector.tensor_tensor(total[:, t, :], ys[t][:], win[t][:], ALU.add)
             nc.sync.dma_start(out=rows[:, t, :], in_=total[:, t, :])
+        for a in range(2):
+            cols = slice(HALF * a, HALF * (a + 1))
+            nc.vector.tensor_tensor(total[:, 3, cols], ys[3][:, cols], win[3][:, cols], ALU.add)
+        nc.sync.dma_start(out=rows[:, 3, :], in_=total[:, 3, :])
 
         oq = held([P, T], U32, "oq")
         osc = held([P, T], U8, "osc")

@@ -31,7 +31,6 @@ SCALAR_STEPS = 2
 VECTOR_SLOTS = 160
 SCALAR_TOKENS = 192
 
-W2_ROWS_AT = 0
 W2_WORDS_AT = 2 * ROW
 H_1_AT = 3 * ROW
 LAST_RELUS_AT = 12 * ROW
@@ -64,7 +63,7 @@ def tile_moe_shf_mlp_relu2_kernel(
         xs = held([P, 2 * T], U8, "xs")
         xs_rows = held([4, 4 * T], U8, "xs_rows")
         w1sc = held([P, E * H], U8, "w1sc")
-        w2sc = placed([P, E * N], U8, "w2sc", W2_ROWS_AT)
+        w2sc = held([P, E * N], U8, "w2sc")
         w1ssc = held([P, PASS], U8, "w1ssc")
         w2ssc = held([P, N], U8, "w2ssc")
         ident = held([P, P], F32, "ident")
@@ -102,8 +101,8 @@ def tile_moe_shf_mlp_relu2_kernel(
         load_expert_planes(w1sc, w1_scales)
         load_words(w1w[0], w1_words[0:2])
         load_words(w1w[1], w1_words[2:4])
-        load_words(w2w[0], w2_words[0:2])
         load_expert_planes(w2sc, w2_scales)
+        load_words(w2w[0], w2_words[0:2])
         nc.sync.dma_start(out=w1sw[:], in_=w1s_words[0].rearrange("p l d -> p (l d)").bitcast(I32))
         load_pass_planes(w1ssc, lambda q: w1s_scales[0, 4 * q : 4 * q + 4, :].rearrange("r (g l) -> g r l", g=G))
         load_words(w2w[1], w2_words[2:4])
@@ -234,25 +233,20 @@ def tile_moe_shf_mlp_relu2_kernel(
                 ALU.max, ALU.mult,
             )
 
-        for e in range(3):
+        for e in range(E):
             routed_first(e, e)
-        routed_relu(0)
-        routed_first(3, 0)
-        routed_relu(1)
-        routed_relu(2)
-        routed_square(0)
-        routed_square(1)
-        routed_relu(3)
-        routed_square(2)
-        routed_square(3)
-        deal_w2_words(0)
+        for e in range(E):
+            routed_relu(e)
+        for e in range(E):
+            routed_square(e)
         deal_w2_plane(0)
         deal_w2_plane(1)
-        hq = [placed([P, HALF], U32, "hq0", W2_ROWS_AT)]
-        quantize(hq[0][:], hsc[:, 0:HALF], hb[0][:])
-        routed_second(0, 3)
-        routed_second(1, 1)
+        deal_w2_words(0)
         deal(w1sp[:], w1sw[:], 4)
+        hq = [held([P, HALF], U32, "w1sw")]
+        quantize(hq[0][:], hsc[:, 0:HALF], hb[0][:])
+        routed_second(0, 0)
+        routed_second(1, 1)
         deal(w1sscp[:], w1ssc[:], 16)
         deal_w2_words(1)
         gated(0, 0, 2, held([P, 2, HALF], F32, "y0"))
@@ -260,7 +254,7 @@ def tile_moe_shf_mlp_relu2_kernel(
         quantize(hq[1][:], hsc[:, HALF:T], hb[1][:])
         hs = [placed([P, T, 4], BF16, "hs0", H_1_AT), held([P, T, 4], BF16, "hs1")]
         routed_second(2, 2)
-        routed_second(3, 0)
+        routed_second(3, 3)
 
         for step in range(STEPS):
             shared_first(step)
@@ -296,7 +290,7 @@ def tile_moe_shf_mlp_relu2_kernel(
         scatter(True, 3, HALF, HALF + VECTOR_SLOTS, y[3, 1][:, 0:VECTOR_SLOTS])
         scatter(False, 3, HALF + VECTOR_SLOTS, T, y[3, 1][:, VECTOR_SLOTS:HALF])
 
-        ys = [bank(number, [P, T]) for number in (3, 1, 2, 0)]
+        ys = [bank(number, [P, T]) for number in range(4)]
         for t, g in itertools.product(range(4), range(G)):
             nc.tensor.matmul_mx(
                 out=ys[t][:],

@@ -26,9 +26,9 @@ ROW = 4 * T
 STEPS = 4 * G
 
 UNITS = (((0, 0), (1, 0)), ((2, 0), (3, 0)), ((0, 1), (1, 1)), ((2, 1), (3, 1)))
-GPSIMD_STEPS = (0, 1, 4, 5)
+GPSIMD_COLUMNS = (0, 128, 256, 512, 704)
 SCALAR_STEPS = 2
-VECTOR_SLOTS = 160
+SCALAR_SLOTS = 160
 SCALAR_TOKENS = 192
 
 W2_WORDS_AT = 2 * ROW
@@ -74,7 +74,7 @@ def tile_moe_shf_mlp_relu2_kernel(
 
         w1w = [held([P, 2, 2 * H], U8, "w1w%d" % a) for a in range(2)]
         w2w = [held([P, 2, 2 * N], U8, "w2w0"), placed([P, 2, 2 * N], U8, "w2w1", W2_WORDS_AT)]
-        w1sw = held([P, HS], I32, "w1sw")
+        w1sw = [held([P, PASS], I32, "w1sw0"), placed([P, PASS], I32, "w1sw1", H_1_AT + ROW)]
         w2sw = held([P, G, N], I32, "w2sw")
         gates = held([P, T], F32, "gates")
 
@@ -103,9 +103,11 @@ def tile_moe_shf_mlp_relu2_kernel(
         load_words(w1w[1], w1_words[2:4])
         load_expert_planes(w2sc, w2_scales)
         load_words(w2w[0], w2_words[0:2])
-        nc.sync.dma_start(out=w1sw[:], in_=w1s_words[0].rearrange("p l d -> p (l d)").bitcast(I32))
+        w1s_rows = w1s_words[0].rearrange("p l d -> p (l d)").bitcast(I32)
+        nc.sync.dma_start(out=w1sw[0][:], in_=w1s_rows[:, 0:PASS])
         load_pass_planes(w1ssc, lambda q: w1s_scales[0, 4 * q : 4 * q + 4, :].rearrange("r (g l) -> g r l", g=G))
         load_words(w2w[1], w2_words[2:4])
+        nc.sync.dma_start(out=w1sw[1][:], in_=w1s_rows[:, PASS:HS])
         nc.sync.dma_start(out=gates[:], in_=gate)
         nc.sync.dma_start(out=w2sw[:], in_=w2s_words.rearrange("g p n d -> p g (n d)").bitcast(I32))
         load_pass_planes(w2ssc, lambda q: w2s_scales[:, 4 * q : 4 * q + 4, :])
@@ -125,7 +127,7 @@ def tile_moe_shf_mlp_relu2_kernel(
         hsc = held([P, E * C], U8, "hsc")
         w1sp = held([P, HS], I32, "w1sp")
         hssc = [held([P, T], U8, "hssc%d" % g) for g in range(G)]
-        own = GPSIMD_STEPS[-1]
+        own = -(-GPSIMD_COLUMNS[-1] // P)
         relus = placed([P, own * P, 4], F32, "relus", RELUS_AT)
         last_relus = placed([P, (STEPS - own) * P, 4], F32, "last_relus", LAST_RELUS_AT)
 
@@ -158,7 +160,7 @@ def tile_moe_shf_mlp_relu2_kernel(
         def quantize(codes, scales, values):
             nc.vector.quantize_mx(out=codes.bitcast(FP8X4), scales=scales, in_=values.rearrange("p s t -> p (s t)"))
 
-        pre_r, turned, pre_s, sums, y = {}, {}, {}, {}, {}
+        pre_r, turned, pre_s, sums = {}, {}, {}, {}
 
         def routed_first(e, number):
             cols = slice(C * e, C * (e + 1))
@@ -197,11 +199,10 @@ def tile_moe_shf_mlp_relu2_kernel(
                     )
 
         def gated(unit, first, last, tile):
-            a = unit // 2
-            weights = gates[:, HALF * a : HALF * (a + 1)].unsqueeze(1).to_broadcast([P, last - first, HALF])
-            nc.vector.tensor_tensor(tile[:], weights, sums[unit][:, first:last, :], ALU.mult)
-            for j in range(first, last):
-                y[UNITS[unit][j]] = tile[:, j - first, :]
+            at = HALF * (unit // 2)
+            weights = gates[:, at + first : at + last].unsqueeze(1).to_broadcast([P, 2, last - first])
+            nc.vector.tensor_tensor(tile[:], weights, sums[unit][:, :, first:last], ALU.mult)
+            return tile
 
         def scatter(on_vector, t, first, last, values):
             out = win[t][:].indirect(offsets[:, first // 16 : last // 16])
@@ -227,9 +228,10 @@ def tile_moe_shf_mlp_relu2_kernel(
                 )
             relu(step >= SCALAR_STEPS, relu_of(step), pre_s[step][:].rearrange("p t s -> p s t"))
 
-        def vector_square(step):
+        def vector_square(step, first):
             nc.vector.scalar_tensor_tensor(
-                hs[1][:, P * (step - 4) : P * (step - 3), :], pre_s[step][:].rearrange("p t s -> p s t"), 0.0, relu_of(step),
+                hs[1][:, P * (step - 4) + first : P * (step - 3), :],
+                pre_s[step][:].rearrange("p t s -> p s t")[:, first:P, :], 0.0, relu_of(step)[:, first:P, :],
                 ALU.max, ALU.mult,
             )
 
@@ -242,16 +244,17 @@ def tile_moe_shf_mlp_relu2_kernel(
         deal_w2_plane(0)
         deal_w2_plane(1)
         deal_w2_words(0)
-        deal(w1sp[:], w1sw[:], 4)
-        hq = [held([P, HALF], U32, "w1sw")]
+        deal(w1sp[:, 0:PASS], w1sw[0][:], 4)
+        deal(w1sscp[:], w1ssc[:], 16)
+        hq = [held([P, HALF], U32, "w1ssc")]
         quantize(hq[0][:], hsc[:, 0:HALF], hb[0][:])
         routed_second(0, 0)
         routed_second(1, 1)
-        deal(w1sscp[:], w1ssc[:], 16)
         deal_w2_words(1)
-        gated(0, 0, 2, held([P, 2, HALF], F32, "y0"))
+        deal(w1sp[:, PASS:HS], w1sw[1][:], 4)
         hq.append(placed([P, HALF], U32, "hq1", W2_WORDS_AT))
         quantize(hq[1][:], hsc[:, HALF:T], hb[1][:])
+        y = [gated(0, 0, HALF, held([P, 2, HALF], F32, "y0"))]
         hs = [placed([P, T, 4], BF16, "hs0", H_1_AT), held([P, T, 4], BF16, "hs1")]
         routed_second(2, 2)
         routed_second(3, 3)
@@ -259,14 +262,15 @@ def tile_moe_shf_mlp_relu2_kernel(
         for step in range(STEPS):
             shared_first(step)
             if step == 4:
-                gated(1, 0, 2, held([P, 2, HALF], F32, "y1"))
-        gated(2, 0, 2, held([P, 2, HALF], F32, "y2"))
+                y.append(gated(1, 0, HALF, held([P, 2, HALF], F32, "y1")))
+        vector_square(own - 1, GPSIMD_COLUMNS[-1] % P)
+        y.append(gated(2, 0, HALF, held([P, 2, HALF], F32, "y2")))
         for step in range(own, STEPS):
-            vector_square(step)
-        gated(3, 0, 1, held([P, 1, HALF], F32, "y3"))
-        for first, last in zip(GPSIMD_STEPS, GPSIMD_STEPS[1:]):
-            values, at = relus[:, P * first : P * last, :], P * (first % 4)
-            nc.gpsimd.tensor_tensor(hs[first // 4][:, at : at + P * (last - first), :], values, values, ALU.mult)
+            vector_square(step, 0)
+        y.append(gated(3, 0, SCALAR_SLOTS, held([P, 2, SCALAR_SLOTS], F32, "y3")))
+        for first, last in zip(GPSIMD_COLUMNS, GPSIMD_COLUMNS[1:]):
+            values, at = relus[:, first:last, :], first % T
+            nc.gpsimd.tensor_tensor(hs[first // T][:, at : at + last - first, :], values, values, ALU.mult)
 
         def deal_w2s(tile, first, last):
             nc.vector.tensor_copy(
@@ -281,14 +285,17 @@ def tile_moe_shf_mlp_relu2_kernel(
         hsq = [placed([P, T], U32, "hsq0", RELUS_AT), held([P, T], U32, "hsq1")]
         for g in range(G):
             quantize(hsq[g][:], hssc[g][:], hs[g][:])
-        gated(3, 1, 2, placed([P, 1, HALF], F32, "y4", H_1_AT))
+        rest = gated(3, SCALAR_SLOTS, HALF, placed([P, 2, HALF - SCALAR_SLOTS], F32, "y4", H_1_AT))
         w2sp.append(placed([P, G, 3, P], I32, "w2sp1", H_1_AT + ROW // 2))
         deal_w2s(w2sp[1], 1, 4)
         win = [held([P, T], F32, "win%d" % t) for t in range(4)]
-        for a, t in list(itertools.product(range(2), range(4)))[:-1]:
-            scatter(False, t, HALF * a, HALF * (a + 1), y[t, a])
-        scatter(True, 3, HALF, HALF + VECTOR_SLOTS, y[3, 1][:, 0:VECTOR_SLOTS])
-        scatter(False, 3, HALF + VECTOR_SLOTS, T, y[3, 1][:, VECTOR_SLOTS:HALF])
+        for unit, j in itertools.product(range(3), range(2)):
+            t, a = UNITS[unit][j]
+            scatter(False, t, HALF * a, HALF * (a + 1), y[unit][:, j, :])
+        for j in range(2):
+            scatter(True, 2 + j, HALF + SCALAR_SLOTS, T, rest[:, j, :])
+        for j in range(2):
+            scatter(False, 2 + j, HALF, HALF + SCALAR_SLOTS, y[3][:, j, :])
 
         ys = [bank(number, [P, T]) for number in range(4)]
         for t, g in itertools.product(range(4), range(G)):

@@ -28,7 +28,7 @@ STEPS = 4 * G
 UNITS = (((0, 0), (1, 0)), ((2, 0), (3, 0)), ((0, 1), (1, 1)), ((2, 1), (3, 1)))
 GPSIMD_COLUMNS = (0, 128, 256, 512, 704)
 SCALAR_STEPS = 2
-SCALAR_SLOTS = 160
+SCALAR_SLOTS = 128
 SCALAR_TOKENS = 192
 
 W2_WORDS_AT = 2 * ROW

@@ -26,7 +26,7 @@ ROW = 4 * T
 STEPS = 4 * G
 
 UNITS = (((0, 0), (1, 0)), ((2, 0), (3, 0)), ((0, 1), (1, 1)), ((2, 1), (3, 1)))
-GPSIMD_COLUMNS = (0, 128, 256, 512, 704)
+GPSIMD_COLUMNS = (0, 128, 256, 512, 640)
 SCALAR_STEPS = 2
 SCALAR_SLOTS = 128
 SCALAR_TOKENS = 192
@@ -127,7 +127,7 @@ def tile_moe_shf_mlp_relu2_kernel(
         hsc = held([P, E * C], U8, "hsc")
         w1sp = held([P, HS], I32, "w1sp")
         hssc = [held([P, T], U8, "hssc%d" % g) for g in range(G)]
-        own = -(-GPSIMD_COLUMNS[-1] // P)
+        own = GPSIMD_COLUMNS[-1] // P
         relus = placed([P, own * P, 4], F32, "relus", RELUS_AT)
         last_relus = placed([P, (STEPS - own) * P, 4], F32, "last_relus", LAST_RELUS_AT)
 
@@ -228,10 +228,10 @@ def tile_moe_shf_mlp_relu2_kernel(
                 )
             relu(step >= SCALAR_STEPS, relu_of(step), pre_s[step][:].rearrange("p t s -> p s t"))
 
-        def vector_square(step, first):
+        def vector_square(step):
             nc.vector.scalar_tensor_tensor(
-                hs[1][:, P * (step - 4) + first : P * (step - 3), :],
-                pre_s[step][:].rearrange("p t s -> p s t")[:, first:P, :], 0.0, relu_of(step)[:, first:P, :],
+                hs[1][:, P * (step - 4) : P * (step - 3), :],
+                pre_s[step][:].rearrange("p t s -> p s t"), 0.0, relu_of(step),
                 ALU.max, ALU.mult,
             )
 
@@ -263,10 +263,9 @@ def tile_moe_shf_mlp_relu2_kernel(
             shared_first(step)
             if step == 4:
                 y.append(gated(1, 0, HALF, held([P, 2, HALF], F32, "y1")))
-        vector_square(own - 1, GPSIMD_COLUMNS[-1] % P)
         y.append(gated(2, 0, HALF, held([P, 2, HALF], F32, "y2")))
         for step in range(own, STEPS):
-            vector_square(step, 0)
+            vector_square(step)
         y.append(gated(3, 0, SCALAR_SLOTS, held([P, 2, SCALAR_SLOTS], F32, "y3")))
         for first, last in zip(GPSIMD_COLUMNS, GPSIMD_COLUMNS[1:]):
             values, at = relus[:, first:last, :], first % T

@@ -1,4 +1,3 @@
-import itertools
 from contextlib import ExitStack
 
 import concourse.mybir as mybir
@@ -25,18 +24,17 @@ HALF = T // 2
 ROW = 4 * T
 STEPS = 4 * G
 
-UNITS = (((0, 0), (1, 0)), ((2, 0), (3, 0)), ((0, 1), (1, 1)), ((2, 1), (3, 1)))
-GPSIMD_COLUMNS = (0, 128, 256, 512, 640)
+GPSIMD_TOKENS = (128, 128, 128, 128, 128, 64, 0, 0)
 SCALAR_STEPS = 2
 SCALAR_SLOTS = 128
 SCALAR_TOKENS = 192
 
-W2_WORDS_AT = 2 * ROW
-H_1_AT = 3 * ROW
+W1S_1_AT = ROW
+Y_0_AT = W1S_1_AT - ROW + 64
+HQ_1_AT = W1S_1_AT + 64
+RELUS_AT = W1S_1_AT + ROW - 64
+H_1_AT = 8 * ROW
 LAST_RELUS_AT = 12 * ROW
-W2S_DEALT_AT = LAST_RELUS_AT - ROW // 2 + 64
-W2S_PLANE_AT = LAST_RELUS_AT + 64
-RELUS_AT = 5 * ROW
 
 
 def tile_moe_shf_mlp_relu2_kernel(
@@ -73,9 +71,9 @@ def tile_moe_shf_mlp_relu2_kernel(
         nc.vector.memset(w2ssc[:].bitcast(I32), 0)
 
         w1w = [held([P, 2, 2 * H], U8, "w1w%d" % a) for a in range(2)]
-        w2w = [held([P, 2, 2 * N], U8, "w2w0"), placed([P, 2, 2 * N], U8, "w2w1", W2_WORDS_AT)]
-        w1sw = [held([P, PASS], I32, "w1sw0"), placed([P, PASS], I32, "w1sw1", H_1_AT + ROW)]
-        w2sw = held([P, G, N], I32, "w2sw")
+        w2w = [held([P, 2, 2 * N], U8, "w2w%d" % a) for a in range(2)]
+        w1sw = [held([P, PASS], I32, "w1sw0"), placed([P, PASS], I32, "w1sw1", W1S_1_AT)]
+        w2sw = held([P, G * N], I32, "w2sw")
         gates = held([P, T], F32, "gates")
 
         def load_words(tile, words):
@@ -106,10 +104,12 @@ def tile_moe_shf_mlp_relu2_kernel(
         w1s_rows = w1s_words[0].rearrange("p l d -> p (l d)").bitcast(I32)
         nc.sync.dma_start(out=w1sw[0][:], in_=w1s_rows[:, 0:PASS])
         load_pass_planes(w1ssc, lambda q: w1s_scales[0, 4 * q : 4 * q + 4, :].rearrange("r (g l) -> g r l", g=G))
-        load_words(w2w[1], w2_words[2:4])
+        nc.sync.dma_start(
+            out=w2sw[:].rearrange("p (g n) -> p g n", g=G), in_=w2s_words.rearrange("g p n d -> p g (n d)").bitcast(I32)
+        )
         nc.sync.dma_start(out=w1sw[1][:], in_=w1s_rows[:, PASS:HS])
         nc.sync.dma_start(out=gates[:], in_=gate)
-        nc.sync.dma_start(out=w2sw[:], in_=w2s_words.rearrange("g p n d -> p g (n d)").bitcast(I32))
+        load_words(w2w[1], w2_words[2:4])
         load_pass_planes(w2ssc, lambda q: w2s_scales[:, 4 * q : 4 * q + 4, :])
         make_identity(nc, ident[:])
 
@@ -120,39 +120,26 @@ def tile_moe_shf_mlp_relu2_kernel(
 
         xg = held([P, T], U32, "xg")
         xgs = held([P, T], U8, "xgs")
-        w2p = [held([P, 2, 2 * N], U8, "w2p%d" % a) for a in range(2)]
-        w2scp = held([P, E * N], U8, "w2scp")
+        w2p = held([P, 2, 2 * N], U8, "w2p")
+        w2scp = held([P, 2 * N], U8, "w2scp")
         w1sscp = held([P, PASS], U8, "w1sscp")
         hb = [held([P, HALF, 4], BF16, "hb0"), placed([P, HALF, 4], BF16, "hb1", H_1_AT)]
         hsc = held([P, E * C], U8, "hsc")
         w1sp = held([P, HS], I32, "w1sp")
         hssc = [held([P, T], U8, "hssc%d" % g) for g in range(G)]
-        own = GPSIMD_COLUMNS[-1] // P
-        relus = placed([P, own * P, 4], F32, "relus", RELUS_AT)
+        own = 6
+        first_relus = held([P, 2 * P, 4], F32, "first_relus")
+        relus = placed([P, (own - 2) * P, 4], F32, "relus", RELUS_AT)
         last_relus = placed([P, (STEPS - own) * P, 4], F32, "last_relus", LAST_RELUS_AT)
 
-        def slots(e):
-            return offsets[:, C * e // 16 : C * (e + 1) // 16]
+        def slots(first, last):
+            return offsets[:, first // 16 : last // 16]
 
-        def deal(out, in_, run, copy=nc.vector.tensor_copy):
-            copy(
+        def deal(out, in_, run):
+            nc.vector.tensor_copy(
                 out=out.rearrange("p (g t c i) -> p g c t i", t=4, c=P // run, i=run),
                 in_=in_.rearrange("p (g c i t) -> p g c t i", t=4, c=P // run, i=run),
             )
-
-        def deal_w2_words(a):
-            flat = "p e b -> p (e b)"
-            deal(w2p[a][:].rearrange(flat).bitcast(U16), w2w[a][:].rearrange(flat).bitcast(U16), 8)
-
-        def deal_w2_plane(a):
-            cols = slice(2 * N * a, 2 * N * (a + 1))
-            deal(w2scp[:, cols], w2sc[:, cols], 16)
-
-        def relu(on_vector, dst, src):
-            if on_vector:
-                nc.vector.tensor_scalar_max(dst, src, 0.0)
-            else:
-                nc.scalar.activation(dst, src, ACT.Relu)
 
         def interleaved(dst, src):
             return dst.rearrange("p (c i) t -> p c t i", i=4), src.rearrange("p t (c i) -> p c t i", i=4)
@@ -160,22 +147,22 @@ def tile_moe_shf_mlp_relu2_kernel(
         def quantize(codes, scales, values):
             nc.vector.quantize_mx(out=codes.bitcast(FP8X4), scales=scales, in_=values.rearrange("p s t -> p (s t)"))
 
-        pre_r, turned, pre_s, sums = {}, {}, {}, {}
+        pre_r, turned, pre_s = {}, {}, {}
 
-        def routed_first(e, number):
+        def routed_first(e):
             cols = slice(C * e, C * (e + 1))
-            nc.vector.tensor_copy(xg[:, cols], xw[:].bitcast(U32).indirect(slots(e)))
-            nc.vector.tensor_copy(xgs[:, cols], xs[:, 0:T].indirect(slots(e)))
-            pre_r[e] = bank(number, [P, H])
+            nc.vector.tensor_copy(xg[:, cols], xw[:].bitcast(U32).indirect(slots(C * e, C * (e + 1))))
+            nc.vector.tensor_copy(xgs[:, cols], xs[:, 0:T].indirect(slots(C * e, C * (e + 1))))
+            pre_r[e] = bank(e, [P, H])
             nc.tensor.matmul_mx(
                 out=pre_r[e][:], lhsT=xg[:, cols].bitcast(FP8X4), lhsT_scale=xgs[:, cols],
                 rhs=w1w[e // 2][:, e % 2, :].bitcast(FP4X4), rhs_scale=w1sc[:, H * e : H * (e + 1)],
                 start=True, stop=True,
             )
 
-        def routed_relu(e):
-            sorted_relu = held([P, 4, P], F32, "relu_r%d" % e)
-            relu(False, sorted_relu[:], pre_r[e][:].rearrange("s (p t) -> s t p", t=4))
+        def routed_relu(e, buffer):
+            sorted_relu = held([P, 4, P], F32, "relu_r%d" % buffer)
+            nc.scalar.activation(sorted_relu[:], pre_r[e][:].rearrange("s (p t) -> s t p", t=4), ACT.Relu)
             turned[e] = bank(4 + e, [P, 4, C])
             for t in range(4):
                 nc.tensor.transpose(turned[e][:, t, :], sorted_relu[:, t, :], ident[:])
@@ -185,34 +172,27 @@ def tile_moe_shf_mlp_relu2_kernel(
                 hb[e // 2][:, C * (e % 2) : C * (e % 2 + 1), :], turned[e][:].rearrange("p t s -> p s t"), ACT.Square
             )
 
-        def routed_second(unit, number):
-            sums[unit] = bank(number, [P, 2, HALF])
-            for j, (t, a) in enumerate(UNITS[unit]):
-                for e in (2 * a, 2 * a + 1):
-                    cols = slice(C * (e % 2), C * (e % 2 + 1))
+        def routed_second(number, a, blocks, words, plane):
+            sums = bank(number, [P, 2, HALF])
+            for j, t in enumerate(blocks):
+                for i in range(2):
+                    cols = slice(C * i, C * (i + 1))
                     nc.tensor.matmul_mx(
-                        out=sums[unit][:, j, cols],
-                        lhsT=w2p[a][:, e % 2, 2 * P * t : 2 * P * (t + 1)].bitcast(FP4X4),
-                        lhsT_scale=w2scp[:, N * e + P * t : N * e + P * (t + 1)],
-                        rhs=hq[a][:, cols].bitcast(FP8X4), rhs_scale=hsc[:, C * e : C * (e + 1)],
+                        out=sums[:, j, cols],
+                        lhsT=words[:, i, 2 * P * t : 2 * P * (t + 1)].bitcast(FP4X4),
+                        lhsT_scale=plane[:, N * i + P * t : N * i + P * (t + 1)],
+                        rhs=hq[a][:, cols].bitcast(FP8X4), rhs_scale=hsc[:, HALF * a + C * i : HALF * a + C * (i + 1)],
                         start=True, stop=True,
                     )
+            return sums
 
-        def gated(unit, first, last, tile):
-            at = HALF * (unit // 2)
-            weights = gates[:, at + first : at + last].unsqueeze(1).to_broadcast([P, 2, last - first])
-            nc.vector.tensor_tensor(tile[:], weights, sums[unit][:, :, first:last], ALU.mult)
+        def gated(tile, a, sums):
+            weights = gates[:, HALF * a : HALF * (a + 1)].unsqueeze(1).to_broadcast([P, 2, HALF])
+            nc.vector.tensor_tensor(tile[:], weights, sums[:], ALU.mult)
             return tile
 
-        def scatter(on_vector, t, first, last, values):
-            out = win[t][:].indirect(offsets[:, first // 16 : last // 16])
-            if on_vector:
-                nc.vector.tensor_copy(out, values)
-            else:
-                nc.scalar.activation(out, values, ACT.Copy)
-
         def relu_of(step):
-            tile, at = (relus, step) if step < own else (last_relus, step - own)
+            tile, at = (first_relus, step) if step < 2 else (relus, step - 2) if step < own else (last_relus, step - own)
             return tile[:, P * at : P * (at + 1), :]
 
         def shared_first(step):
@@ -226,91 +206,99 @@ def tile_moe_shf_mlp_relu2_kernel(
                     rhs=xw[:, P * u : P * (u + 1)].bitcast(FP8X4), rhs_scale=xs[:, P * u : P * (u + 1)],
                     start=True, stop=True,
                 )
-            relu(step >= SCALAR_STEPS, relu_of(step), pre_s[step][:].rearrange("p t s -> p s t"))
+            sums = pre_s[step][:].rearrange("p t s -> p s t")
+            if step < SCALAR_STEPS:
+                nc.scalar.activation(relu_of(step), sums, ACT.Relu)
+            else:
+                nc.vector.tensor_scalar_max(relu_of(step), sums, 0.0)
 
-        def vector_square(step):
-            nc.vector.scalar_tensor_tensor(
-                hs[1][:, P * (step - 4) : P * (step - 3), :],
-                pre_s[step][:].rearrange("p t s -> p s t"), 0.0, relu_of(step),
-                ALU.max, ALU.mult,
-            )
+        def square(step):
+            g, u = divmod(step, 4)
+            out, values, cut = hs[g][:, P * u : P * (u + 1), :], relu_of(step), GPSIMD_TOKENS[step]
+            if cut > 0:
+                nc.gpsimd.tensor_tensor(out[:, 0:cut], values[:, 0:cut], values[:, 0:cut], ALU.mult)
+            if cut < P:
+                sums = pre_s[step][:].rearrange("p t s -> p s t")
+                nc.vector.scalar_tensor_tensor(out[:, cut:P], sums[:, cut:P], 0.0, values[:, cut:P], ALU.max, ALU.mult)
 
         for e in range(E):
-            routed_first(e, e)
+            routed_first(e)
         for e in range(E):
-            routed_relu(e)
+            routed_relu(e, e)
         for e in range(E):
             routed_square(e)
-        deal_w2_plane(0)
-        deal_w2_plane(1)
-        deal_w2_words(0)
+        deal(w2scp[:], w2sc[:, 0 : 2 * N], 16)
+        flat = "p e b -> p (e b)"
+        deal(w2p[:].rearrange(flat).bitcast(U16), w2w[0][:].rearrange(flat).bitcast(U16), 8)
         deal(w1sp[:, 0:PASS], w1sw[0][:], 4)
         deal(w1sscp[:], w1ssc[:], 16)
         hq = [held([P, HALF], U32, "w1ssc")]
         quantize(hq[0][:], hsc[:, 0:HALF], hb[0][:])
-        routed_second(0, 0)
-        routed_second(1, 1)
-        deal_w2_words(1)
+        w2sp = held([P, G * N], I32, "w2sp")
+        deal(w2sp[:], w2sw[:], 4)
         deal(w1sp[:, PASS:HS], w1sw[1][:], 4)
-        hq.append(placed([P, HALF], U32, "hq1", W2_WORDS_AT))
+        near = [routed_second(u, 0, (2 * u, 2 * u + 1), w2p, w2scp) for u in range(2)]
+        y = [gated(placed([P, 2, HALF], F32, "y0", Y_0_AT), 0, near[0])]
+        hq.append(placed([P, HALF], U32, "hq1", HQ_1_AT))
         quantize(hq[1][:], hsc[:, HALF:T], hb[1][:])
-        y = [gated(0, 0, HALF, held([P, 2, HALF], F32, "y0"))]
-        hs = [placed([P, T, 4], BF16, "hs0", H_1_AT), held([P, T, 4], BF16, "hs1")]
-        routed_second(2, 2)
-        routed_second(3, 3)
-
-        for step in range(STEPS):
+        for step in range(SCALAR_STEPS):
             shared_first(step)
-            if step == 4:
-                y.append(gated(1, 0, HALF, held([P, 2, HALF], F32, "y1")))
-        y.append(gated(2, 0, HALF, held([P, 2, HALF], F32, "y2")))
-        for step in range(own, STEPS):
-            vector_square(step)
-        y.append(gated(3, 0, SCALAR_SLOTS, held([P, 2, SCALAR_SLOTS], F32, "y3")))
-        for first, last in zip(GPSIMD_COLUMNS, GPSIMD_COLUMNS[1:]):
-            values, at = relus[:, first:last, :], first % T
-            nc.gpsimd.tensor_tensor(hs[first // T][:, at : at + last - first, :], values, values, ALU.mult)
+        moved = held([P, 4, HALF], F32, "moved")
+        for u in range(2):
+            shared_first(SCALAR_STEPS + u)
+            far = routed_second(2 + u, 1, (u, u + 2), w2w[1], w2sc[:, 2 * N : 4 * N])
+            plain = gated(held([P, 2, HALF], F32, "plain%d" % u), 1, far)
+            for j in range(2):
+                block = u + 2 * j
+                nc.sync.dma_start(out=moved[32 * block : 32 * (block + 1), :, :], in_=plain[:, j, :])
+        y.append(gated(held([P, 2, HALF], F32, "y1"), 0, near[1]))
+        hs = [placed([P, T, 4], BF16, "hs0", H_1_AT), held([P, T, 4], BF16, "hs1")]
+        for step in range(SCALAR_STEPS + 2, STEPS):
+            shared_first(step)
+        for step in range(STEPS):
+            square(step)
 
-        def deal_w2s(tile, first, last):
+        def deal_w2s_plane(tile, first, last):
             nc.vector.tensor_copy(
-                out=tile[:].rearrange("p g t (c i) -> p g c t i", i=4),
-                in_=w2sw[:].rearrange("p g (c i t) -> p g c t i", i=4, t=4)[:, :, :, first:last, :],
+                out=tile[:].rearrange("p t (c i) -> p c t i", i=16),
+                in_=w2ssc[:].rearrange("p (c i t) -> p c t i", i=16, t=4)[:, :, first:last, :],
             )
 
-        w2sp = [placed([P, G, 1, P], I32, "w2sp0", W2S_DEALT_AT)]
-        deal_w2s(w2sp[0], 0, 1)
-        w2sscp = placed([P, N], U8, "w2sscp", W2S_PLANE_AT)
-        deal(w2sscp[:], w2ssc[:], 16)
-        hsq = [placed([P, T], U32, "hsq0", RELUS_AT), held([P, T], U32, "hsq1")]
+        w2sscp = [placed([P, 1, P], U8, "w2sscp0", LAST_RELUS_AT)]
+        deal_w2s_plane(w2sscp[0], 0, 1)
+        hsq = [placed([P, T], U32, "hsq0", RELUS_AT + ROW), held([P, T], U32, "hsq1")]
         for g in range(G):
             quantize(hsq[g][:], hssc[g][:], hs[g][:])
-        rest = gated(3, SCALAR_SLOTS, HALF, placed([P, 2, HALF - SCALAR_SLOTS], F32, "y4", H_1_AT))
-        w2sp.append(placed([P, G, 3, P], I32, "w2sp1", H_1_AT + ROW // 2))
-        deal_w2s(w2sp[1], 1, 4)
+        w2sscp.append(placed([P, 3, P], U8, "w2sscp1", H_1_AT + ROW))
+        deal_w2s_plane(w2sscp[1], 1, 4)
         win = [held([P, T], F32, "win%d" % t) for t in range(4)]
-        for unit, j in itertools.product(range(3), range(2)):
-            t, a = UNITS[unit][j]
-            scatter(False, t, HALF * a, HALF * (a + 1), y[unit][:, j, :])
-        for j in range(2):
-            scatter(True, 2 + j, HALF + SCALAR_SLOTS, T, rest[:, j, :])
-        for j in range(2):
-            scatter(False, 2 + j, HALF, HALF + SCALAR_SLOTS, y[3][:, j, :])
+        for t in range(4):
+            nc.scalar.activation(win[t][:].indirect(slots(0, HALF)), y[t // 2][:, t % 2, :], ACT.Copy)
+        for t in range(2):
+            nc.scalar.activation(win[t][:].indirect(slots(HALF, T)), moved[:, t, :], ACT.Copy)
+        for t in range(2, 4):
+            nc.vector.tensor_copy(win[t][:].indirect(slots(HALF + SCALAR_SLOTS, T)), moved[:, t, SCALAR_SLOTS:HALF])
+        for t in range(2, 4):
+            nc.scalar.activation(win[t][:].indirect(slots(HALF, HALF + SCALAR_SLOTS)), moved[:, t, 0:SCALAR_SLOTS], ACT.Copy)
 
         ys = [bank(number, [P, T]) for number in range(4)]
-        for t, g in itertools.product(range(4), range(G)):
-            nc.tensor.matmul_mx(
-                out=ys[t][:],
-                lhsT=(w2sp[0][:, g, 0, :] if t == 0 else w2sp[1][:, g, t - 1, :]).bitcast(FP8X4),
-                lhsT_scale=w2sscp[4 * g : P, P * t : P * (t + 1)],
-                rhs=hsq[g][:].bitcast(FP8X4), rhs_scale=hssc[g][:],
-                start=(g == 0), stop=(g == G - 1),
-            )
+        for t in range(4):
+            for g in range(G):
+                nc.tensor.matmul_mx(
+                    out=ys[t][:],
+                    lhsT=w2sp[:, N * g + P * t : N * g + P * (t + 1)].bitcast(FP8X4),
+                    lhsT_scale=w2sscp[0][4 * g : P, 0, :] if t == 0 else w2sscp[1][4 * g : P, t - 1, :],
+                    rhs=hsq[g][:].bitcast(FP8X4), rhs_scale=hssc[g][:],
+                    start=(g == 0), stop=(g == G - 1),
+                )
 
         total = held([P, 4, T], F32, "total")
         rows = out_0.rearrange("(p t) c -> p t c", t=4)
         for t in range(3):
             nc.vector.tensor_tensor(total[:, t, :], ys[t][:], win[t][:], ALU.add)
-            nc.sync.dma_start(out=rows[:, t, :], in_=total[:, t, :])
+            if t > 0:
+                first = 0 if t == 1 else t
+                nc.sync.dma_start(out=rows[:, first : t + 1, :], in_=total[:, first : t + 1, :])
         for a in range(2):
             cols = slice(HALF * a, HALF * (a + 1))
             nc.vector.tensor_tensor(total[:, 3, cols], ys[3][:, cols], win[3][:, cols], ALU.add)

@@ -24,15 +24,15 @@ HALF = T // 2
 ROW = 4 * T
 STEPS = 4 * G
 
-GPSIMD_TOKENS = (128, 128, 128, 128, 128, 64, 0, 0)
+GPSIMD_COLUMNS = (0, 128, 256, 512, 704)
 SCALAR_STEPS = 2
-SCALAR_SLOTS = 128
+SCALAR_SLOTS = {2: 128, 3: 96}
 SCALAR_TOKENS = 192
 
-W1S_1_AT = ROW
-Y_0_AT = W1S_1_AT - ROW + 64
-HQ_1_AT = W1S_1_AT + 64
-RELUS_AT = W1S_1_AT + ROW - 64
+W2S_AT = ROW
+Y_0_AT = W2S_AT - ROW + 64
+HQ_1_AT = W2S_AT + 64
+RELUS_AT = W2S_AT + ROW - 64
 H_1_AT = 8 * ROW
 LAST_RELUS_AT = 12 * ROW
 
@@ -72,8 +72,8 @@ def tile_moe_shf_mlp_relu2_kernel(
 
         w1w = [held([P, 2, 2 * H], U8, "w1w%d" % a) for a in range(2)]
         w2w = [held([P, 2, 2 * N], U8, "w2w%d" % a) for a in range(2)]
-        w1sw = [held([P, PASS], I32, "w1sw0"), placed([P, PASS], I32, "w1sw1", W1S_1_AT)]
-        w2sw = held([P, G * N], I32, "w2sw")
+        w1sw = held([P, HS], I32, "w1sw")
+        w2sw = [held([P, N], I32, "w2sw0"), placed([P, N], I32, "w2sw1", W2S_AT)]
         gates = held([P, T], F32, "gates")
 
         def load_words(tile, words):
@@ -101,13 +101,10 @@ def tile_moe_shf_mlp_relu2_kernel(
         load_words(w1w[1], w1_words[2:4])
         load_expert_planes(w2sc, w2_scales)
         load_words(w2w[0], w2_words[0:2])
-        w1s_rows = w1s_words[0].rearrange("p l d -> p (l d)").bitcast(I32)
-        nc.sync.dma_start(out=w1sw[0][:], in_=w1s_rows[:, 0:PASS])
+        nc.sync.dma_start(out=w1sw[:], in_=w1s_words[0].rearrange("p l d -> p (l d)").bitcast(I32))
         load_pass_planes(w1ssc, lambda q: w1s_scales[0, 4 * q : 4 * q + 4, :].rearrange("r (g l) -> g r l", g=G))
-        nc.sync.dma_start(
-            out=w2sw[:].rearrange("p (g n) -> p g n", g=G), in_=w2s_words.rearrange("g p n d -> p g (n d)").bitcast(I32)
-        )
-        nc.sync.dma_start(out=w1sw[1][:], in_=w1s_rows[:, PASS:HS])
+        for g in range(G):
+            nc.sync.dma_start(out=w2sw[g][:], in_=w2s_words[g].rearrange("p n d -> p (n d)").bitcast(I32))
         nc.sync.dma_start(out=gates[:], in_=gate)
         load_words(w2w[1], w2_words[2:4])
         load_pass_planes(w2ssc, lambda q: w2s_scales[:, 4 * q : 4 * q + 4, :])
@@ -212,14 +209,13 @@ def tile_moe_shf_mlp_relu2_kernel(
             else:
                 nc.vector.tensor_scalar_max(relu_of(step), sums, 0.0)
 
-        def square(step):
-            g, u = divmod(step, 4)
-            out, values, cut = hs[g][:, P * u : P * (u + 1), :], relu_of(step), GPSIMD_TOKENS[step]
-            if cut > 0:
-                nc.gpsimd.tensor_tensor(out[:, 0:cut], values[:, 0:cut], values[:, 0:cut], ALU.mult)
-            if cut < P:
-                sums = pre_s[step][:].rearrange("p t s -> p s t")
-                nc.vector.scalar_tensor_tensor(out[:, cut:P], sums[:, cut:P], 0.0, values[:, cut:P], ALU.max, ALU.mult)
+        def vector_square(step):
+            cut = max(GPSIMD_COLUMNS[-1] - P * step, 0)
+            nc.vector.scalar_tensor_tensor(
+                hs[1][:, P * (step - 4) + cut : P * (step - 3), :],
+                pre_s[step][:].rearrange("p t s -> p s t")[:, cut:P], 0.0, relu_of(step)[:, cut:P],
+                ALU.max, ALU.mult,
+            )
 
         for e in range(E):
             routed_first(e)
@@ -230,17 +226,17 @@ def tile_moe_shf_mlp_relu2_kernel(
         deal(w2scp[:], w2sc[:, 0 : 2 * N], 16)
         flat = "p e b -> p (e b)"
         deal(w2p[:].rearrange(flat).bitcast(U16), w2w[0][:].rearrange(flat).bitcast(U16), 8)
-        deal(w1sp[:, 0:PASS], w1sw[0][:], 4)
+        deal(w1sp[:], w1sw[:], 4)
         deal(w1sscp[:], w1ssc[:], 16)
         hq = [held([P, HALF], U32, "w1ssc")]
         quantize(hq[0][:], hsc[:, 0:HALF], hb[0][:])
         w2sp = held([P, G * N], I32, "w2sp")
-        deal(w2sp[:], w2sw[:], 4)
-        deal(w1sp[:, PASS:HS], w1sw[1][:], 4)
+        for g in range(G):
+            deal(w2sp[:, N * g : N * (g + 1)], w2sw[g][:], 4)
         near = [routed_second(u, 0, (2 * u, 2 * u + 1), w2p, w2scp) for u in range(2)]
-        y = [gated(placed([P, 2, HALF], F32, "y0", Y_0_AT), 0, near[0])]
         hq.append(placed([P, HALF], U32, "hq1", HQ_1_AT))
         quantize(hq[1][:], hsc[:, HALF:T], hb[1][:])
+        y = [gated(placed([P, 2, HALF], F32, "y0", Y_0_AT), 0, near[0])]
         for step in range(SCALAR_STEPS):
             shared_first(step)
         moved = held([P, 4, HALF], F32, "moved")
@@ -255,8 +251,12 @@ def tile_moe_shf_mlp_relu2_kernel(
         hs = [placed([P, T, 4], BF16, "hs0", H_1_AT), held([P, T, 4], BF16, "hs1")]
         for step in range(SCALAR_STEPS + 2, STEPS):
             shared_first(step)
-        for step in range(STEPS):
-            square(step)
+        for step in range(GPSIMD_COLUMNS[-1] // P, STEPS):
+            vector_square(step)
+        for first, last in zip(GPSIMD_COLUMNS, GPSIMD_COLUMNS[1:]):
+            values = first_relus[:, first:last, :] if last <= 2 * P else relus[:, first - 2 * P : last - 2 * P, :]
+            at = first % T
+            nc.gpsimd.tensor_tensor(hs[first // T][:, at : at + last - first, :], values, values, ALU.mult)
 
         def deal_w2s_plane(tile, first, last):
             nc.vector.tensor_copy(
@@ -277,9 +277,11 @@ def tile_moe_shf_mlp_relu2_kernel(
         for t in range(2):
             nc.scalar.activation(win[t][:].indirect(slots(HALF, T)), moved[:, t, :], ACT.Copy)
         for t in range(2, 4):
-            nc.vector.tensor_copy(win[t][:].indirect(slots(HALF + SCALAR_SLOTS, T)), moved[:, t, SCALAR_SLOTS:HALF])
+            cut = SCALAR_SLOTS[t]
+            nc.vector.tensor_copy(win[t][:].indirect(slots(HALF + cut, T)), moved[:, t, cut:HALF])
         for t in range(2, 4):
-            nc.scalar.activation(win[t][:].indirect(slots(HALF, HALF + SCALAR_SLOTS)), moved[:, t, 0:SCALAR_SLOTS], ACT.Copy)
+            cut = SCALAR_SLOTS[t]
+            nc.scalar.activation(win[t][:].indirect(slots(HALF, HALF + cut)), moved[:, t, 0:cut], ACT.Copy)
 
         ys = [bank(number, [P, T]) for number in range(4)]
         for t in range(4):

@@ -24,9 +24,9 @@ HALF = T // 2
 ROW = 4 * T
 STEPS = 4 * G
 
-GPSIMD_COLUMNS = (0, 128, 256, 512, 704)
+GPSIMD_COLUMNS = (0, 128, 256, 512, 672)
 SCALAR_STEPS = 2
-SCALAR_SLOTS = {2: 128, 3: 96}
+SCALAR_SLOTS = {2: 96, 3: 96}
 SCALAR_TOKENS = 192
 
 W2S_AT = ROW
@@ -34,7 +34,6 @@ Y_0_AT = W2S_AT - ROW + 64
 HQ_1_AT = W2S_AT + 64
 RELUS_AT = W2S_AT + ROW - 64
 H_1_AT = 8 * ROW
-LAST_RELUS_AT = 12 * ROW
 
 
 def tile_moe_shf_mlp_relu2_kernel(
@@ -127,7 +126,7 @@ def tile_moe_shf_mlp_relu2_kernel(
         own = 6
         first_relus = held([P, 2 * P, 4], F32, "first_relus")
         relus = placed([P, (own - 2) * P, 4], F32, "relus", RELUS_AT)
-        last_relus = placed([P, (STEPS - own) * P, 4], F32, "last_relus", LAST_RELUS_AT)
+        last_relus = held([P, (STEPS - own) * P, 4], F32, "last_relus")
 
         def slots(first, last):
             return offsets[:, first // 16 : last // 16]
@@ -264,7 +263,7 @@ def tile_moe_shf_mlp_relu2_kernel(
                 in_=w2ssc[:].rearrange("p (c i t) -> p c t i", i=16, t=4)[:, :, first:last, :],
             )
 
-        w2sscp = [placed([P, 1, P], U8, "w2sscp0", LAST_RELUS_AT)]
+        w2sscp = [placed([P, 1, P], U8, "w2sscp0", RELUS_AT + 2 * ROW)]
         deal_w2s_plane(w2sscp[0], 0, 1)
         hsq = [placed([P, T], U32, "hsq0", RELUS_AT + ROW), held([P, T], U32, "hsq1")]
         for g in range(G):

@@ -26,7 +26,7 @@ STEPS = 4 * G
 
 GPSIMD_COLUMNS = (0, 128, 256, 512, 672)
 SCALAR_STEPS = 2
-SCALAR_SLOTS = {2: 96, 3: 96}
+SCALAR_SLOTS = {2: 96, 3: 64}
 SCALAR_TOKENS = 192
 
 W2S_AT = ROW
@@ -263,13 +263,13 @@ def tile_moe_shf_mlp_relu2_kernel(
                 in_=w2ssc[:].rearrange("p (c i t) -> p c t i", i=16, t=4)[:, :, first:last, :],
             )
 
-        w2sscp = [placed([P, 1, P], U8, "w2sscp0", RELUS_AT + 2 * ROW)]
-        deal_w2s_plane(w2sscp[0], 0, 1)
+        w2sscp = [placed([P, 2, P], U8, "w2sscp0", RELUS_AT + 2 * ROW)]
+        deal_w2s_plane(w2sscp[0], 0, 2)
         hsq = [placed([P, T], U32, "hsq0", RELUS_AT + ROW), held([P, T], U32, "hsq1")]
         for g in range(G):
             quantize(hsq[g][:], hssc[g][:], hs[g][:])
-        w2sscp.append(placed([P, 3, P], U8, "w2sscp1", H_1_AT + ROW))
-        deal_w2s_plane(w2sscp[1], 1, 4)
+        w2sscp.append(placed([P, 2, P], U8, "w2sscp1", H_1_AT + ROW))
+        deal_w2s_plane(w2sscp[1], 2, 4)
         win = [held([P, T], F32, "win%d" % t) for t in range(4)]
         for t in range(4):
             nc.scalar.activation(win[t][:].indirect(slots(0, HALF)), y[t // 2][:, t % 2, :], ACT.Copy)
@@ -288,7 +288,7 @@ def tile_moe_shf_mlp_relu2_kernel(
                 nc.tensor.matmul_mx(
                     out=ys[t][:],
                     lhsT=w2sp[:, N * g + P * t : N * g + P * (t + 1)].bitcast(FP8X4),
-                    lhsT_scale=w2sscp[0][4 * g : P, 0, :] if t == 0 else w2sscp[1][4 * g : P, t - 1, :],
+                    lhsT_scale=w2sscp[t // 2][4 * g : P, t % 2, :],
                     rhs=hsq[g][:].bitcast(FP8X4), rhs_scale=hssc[g][:],
                     start=(g == 0), stop=(g == G - 1),
                 )

@@ -34,6 +34,7 @@ Y_0_AT = W2S_AT - ROW + 64
 HQ_1_AT = W2S_AT + 64
 RELUS_AT = W2S_AT + ROW - 64
 H_1_AT = 8 * ROW
+HS_1_AT = 10 * ROW
 
 
 def tile_moe_shf_mlp_relu2_kernel(
@@ -247,7 +248,7 @@ def tile_moe_shf_mlp_relu2_kernel(
                 block = u + 2 * j
                 nc.sync.dma_start(out=moved[32 * block : 32 * (block + 1), :, :], in_=plain[:, j, :])
         y.append(gated(held([P, 2, HALF], F32, "y1"), 0, near[1]))
-        hs = [placed([P, T, 4], BF16, "hs0", H_1_AT), held([P, T, 4], BF16, "hs1")]
+        hs = [placed([P, T, 4], BF16, "hs0", H_1_AT), placed([P, T, 4], BF16, "hs1", HS_1_AT)]
         for step in range(SCALAR_STEPS + 2, STEPS):
             shared_first(step)
         for step in range(GPSIMD_COLUMNS[-1] // P, STEPS):
@@ -257,19 +258,19 @@ def tile_moe_shf_mlp_relu2_kernel(
             at = first % T
             nc.gpsimd.tensor_tensor(hs[first // T][:, at : at + last - first, :], values, values, ALU.mult)
 
-        def deal_w2s_plane(tile, first, last):
-            nc.vector.tensor_copy(
+        def deal_w2s_plane(engine, tile, first, last):
+            engine.tensor_copy(
                 out=tile[:].rearrange("p t (c i) -> p c t i", i=16),
                 in_=w2ssc[:].rearrange("p (c i t) -> p c t i", i=16, t=4)[:, :, first:last, :],
             )
 
         w2sscp = [placed([P, 2, P], U8, "w2sscp0", RELUS_AT + 2 * ROW)]
-        deal_w2s_plane(w2sscp[0], 0, 2)
+        deal_w2s_plane(nc.vector, w2sscp[0], 0, 2)
         hsq = [placed([P, T], U32, "hsq0", RELUS_AT + ROW), held([P, T], U32, "hsq1")]
         for g in range(G):
             quantize(hsq[g][:], hssc[g][:], hs[g][:])
-        w2sscp.append(placed([P, 2, P], U8, "w2sscp1", H_1_AT + ROW))
-        deal_w2s_plane(w2sscp[1], 2, 4)
+        w2sscp.append(placed([P, 2, P], U8, "w2sscp1", HS_1_AT))
+        deal_w2s_plane(nc.gpsimd, w2sscp[1], 2, 4)
         win = [held([P, T], F32, "win%d" % t) for t in range(4)]
         for t in range(4):
             nc.scalar.activation(win[t][:].indirect(slots(0, HALF)), y[t // 2][:, t % 2, :], ACT.Copy)

from contextlib import ExitStack

import concourse.mybir as mybir
from concourse.masks import make_identity

K, T, E, C, H, HS, N = 512, 512, 4, 128, 512, 1024, 512
FLOPS = 2 * T * (K * HS + HS * N + K * H + H * N)

F32 = mybir.dt.float32
BF16 = mybir.dt.bfloat16
I32 = mybir.dt.int32
U32 = mybir.dt.uint32
U16 = mybir.dt.uint16
U8 = mybir.dt.uint8
FP8X4 = mybir.dt.float8_e4m3fn_x4
FP4X4 = mybir.dt.float4_e2m1fn_x4
ACT = mybir.ActivationFunctionType
ALU = mybir.AluOpType

P = 128
PASS = 512
G = HS // PASS
HALF = T // 2
ROW = 4 * T
STEPS = 4 * G

GPSIMD_COLUMNS = (0, 128, 256, 512, 672)
SCALAR_STEPS = 2
SCALAR_SLOTS = {2: 96, 3: 64}
SCALAR_TOKENS = 192

W2S_AT = ROW
Y_0_AT = W2S_AT - ROW + 64
HQ_1_AT = W2S_AT + 64
RELUS_AT = W2S_AT + ROW - 64
H_1_AT = 8 * ROW
HS_1_AT = 10 * ROW


def tile_moe_shf_mlp_relu2_kernel(
    tc, x_words, x_scales, w1_words, w1_scales, w2_words, w2_scales, w1s_words, w1s_scales,
    w2s_words, w2s_scales, gate, offs, out_0, out_1, out_2,
):
    nc = tc.nc
    with ExitStack() as ctx:
        keep = ctx.enter_context(tc.tile_pool(name="keep", bufs=1))
        late = ctx.enter_context(tc.tile_pool(name="late", bufs=1))
        psum = ctx.enter_context(tc.psum_pool(name="psum", bufs=1))

        def held(shape, dtype, name):
            return keep.tile(shape, dtype, name=name, align_bytes=64)

        def placed(shape, dtype, name, offset):
            return late.tile(shape, dtype, name=name, offset=offset, align_bytes=64)

        def bank(number, shape):
            return psum.tile(shape, F32, name="bank%d" % number)

        offsets = keep.tile([P, T // 16], U16, name="offsets")
        xw = held([P, T], I32, "xw")
        xs = held([P, 2 * T], U8, "xs")
        xs_rows = held([4, 4 * T], U8, "xs_rows")
        w1sc = held([P, E * H], U8, "w1sc")
        w2sc = held([P, E * N], U8, "w2sc")
        w1ssc = held([P, PASS], U8, "w1ssc")
        w2ssc = held([P, N], U8, "w2ssc")
        ident = held([P, P], F32, "ident")
        nc.vector.memset(xs[:].bitcast(I32), 0)
        nc.vector.memset(w2sc[:].bitcast(I32), 0)
        nc.vector.memset(w1ssc[:].bitcast(I32), 0)
        nc.vector.memset(w2ssc[:].bitcast(I32), 0)

        w1w = [held([P, 2, 2 * H], U8, "w1w%d" % a) for a in range(2)]
        w2w = [held([P, 2, 2 * N], U8, "w2w%d" % a) for a in range(2)]
        w1sw = held([P, HS], I32, "w1sw")
        w2sw = [held([P, N], I32, "w2sw0"), placed([P, N], I32, "w2sw1", W2S_AT)]
        gates = held([P, T], F32, "gates")

        def load_words(tile, words):
            nc.sync.dma_start(out=tile[:].bitcast(I32), in_=words[:, 0].rearrange("e p b -> p e b").bitcast(I32))

        def load_expert_planes(tile, scales):
            for r in range(4):
                nc.sync.dma_start(
                    out=tile[r:P:32, :].bitcast(I32).rearrange("q (e n) -> q e n", e=E),
                    in_=scales[:, 0, r:16:4, :].rearrange("e q n -> q e n").bitcast(I32),
                )

        def load_pass_planes(tile, rows):
            for q in range(4):
                nc.sync.dma_start(out=tile[32 * q : 32 * q + 4 * G, :].bitcast(I32), in_=rows(q).bitcast(I32))

        nc.sync.dma_start(
            out=xs_rows[:].bitcast(I32).rearrange("r (q t) -> r q t", q=4),
            in_=x_scales[0].rearrange("(q r) t -> r q t", r=4).bitcast(I32),
        )
        nc.sync.dma_start(out=xw[:], in_=x_words[0].rearrange("p t d -> p (t d)").bitcast(I32))
        nc.sync.dma_start(offsets[:], offs)
        load_expert_planes(w1sc, w1_scales)
        load_words(w1w[0], w1_words[0:2])
        load_words(w1w[1], w1_words[2:4])
        load_expert_planes(w2sc, w2_scales)
        load_words(w2w[0], w2_words[0:2])
        nc.sync.dma_start(out=w1sw[:], in_=w1s_words[0].rearrange("p l d -> p (l d)").bitcast(I32))
        load_pass_planes(w1ssc, lambda q: w1s_scales[0, 4 * q : 4 * q + 4, :].rearrange("r (g l) -> g r l", g=G))
        for g in range(G):
            nc.sync.dma_start(out=w2sw[g][:], in_=w2s_words[g].rearrange("p n d -> p (n d)").bitcast(I32))
        nc.sync.dma_start(out=gates[:], in_=gate)
        load_words(w2w[1], w2_words[2:4])
        load_pass_planes(w2ssc, lambda q: w2s_scales[:, 4 * q : 4 * q + 4, :])
        make_identity(nc, ident[:])

        staged = xs_rows[:].bitcast(I32).rearrange("r (a b t) -> r b a t", a=2, b=2)
        for b in range(2):
            nc.vector.tensor_copy(xs[32 * b : 32 * b + 4, :].bitcast(I32).rearrange("r (a t) -> r a t", a=2), staged[:, b])
        nc.vector.tensor_copy(xs[64:P, 0:T].bitcast(I32), xs[0:64, T : 2 * T].bitcast(I32))

        xg = held([P, T], U32, "xg")
        xgs = held([P, T], U8, "xgs")
        w2p = held([P, 2, 2 * N], U8, "w2p")
        w2scp = held([P, 2 * N], U8, "w2scp")
        w1sscp = held([P, PASS], U8, "w1sscp")
        hb = [held([P, HALF, 4], BF16, "hb0"), placed([P, HALF, 4], BF16, "hb1", H_1_AT)]
        hsc = held([P, E * C], U8, "hsc")
        w1sp = held([P, HS], I32, "w1sp")
        hssc = [held([P, T], U8, "hssc%d" % g) for g in range(G)]
        own = 6
        first_relus = held([P, 2 * P, 4], F32, "first_relus")
        relus = placed([P, (own - 2) * P, 4], F32, "relus", RELUS_AT)
        last_relus = held([P, (STEPS - own) * P, 4], F32, "last_relus")

        def slots(first, last):
            return offsets[:, first // 16 : last // 16]

        def deal(out, in_, run):
            nc.vector.tensor_copy(
                out=out.rearrange("p (g t c i) -> p g c t i", t=4, c=P // run, i=run),
                in_=in_.rearrange("p (g c i t) -> p g c t i", t=4, c=P // run, i=run),
            )

        def interleaved(dst, src):
            return dst.rearrange("p (c i) t -> p c t i", i=4), src.rearrange("p t (c i) -> p c t i", i=4)

        def quantize(codes, scales, values):
            nc.vector.quantize_mx(out=codes.bitcast(FP8X4), scales=scales, in_=values.rearrange("p s t -> p (s t)"))

        pre_r, turned, pre_s = {}, {}, {}

        def routed_first(e):
            cols = slice(C * e, C * (e + 1))
            nc.vector.tensor_copy(xg[:, cols], xw[:].bitcast(U32).indirect(slots(C * e, C * (e + 1))))
            nc.vector.tensor_copy(xgs[:, cols], xs[:, 0:T].indirect(slots(C * e, C * (e + 1))))
            pre_r[e] = bank(e, [P, H])
            nc.tensor.matmul_mx(
                out=pre_r[e][:], lhsT=xg[:, cols].bitcast(FP8X4), lhsT_scale=xgs[:, cols],
                rhs=w1w[e // 2][:, e % 2, :].bitcast(FP4X4), rhs_scale=w1sc[:, H * e : H * (e + 1)],
                start=True, stop=True,
            )

        def routed_relu(e, buffer):
            sorted_relu = held([P, 4, P], F32, "relu_r%d" % buffer)
            nc.scalar.activation(sorted_relu[:], pre_r[e][:].rearrange("s (p t) -> s t p", t=4), ACT.Relu)
            turned[e] = bank(4 + e, [P, 4, C])
            for t in range(4):
                nc.tensor.transpose(turned[e][:, t, :], sorted_relu[:, t, :], ident[:])

        def routed_square(e):
            nc.scalar.activation(
                hb[e // 2][:, C * (e % 2) : C * (e % 2 + 1), :], turned[e][:].rearrange("p t s -> p s t"), ACT.Square
            )

        def routed_second(number, a, blocks, words, plane):
            sums = bank(number, [P, 2, HALF])
            for j, t in enumerate(blocks):
                for i in range(2):
                    cols = slice(C * i, C * (i + 1))
                    nc.tensor.matmul_mx(
                        out=sums[:, j, cols],
                        lhsT=words[:, i, 2 * P * t : 2 * P * (t + 1)].bitcast(FP4X4),
                        lhsT_scale=plane[:, N * i + P * t : N * i + P * (t + 1)],
                        rhs=hq[a][:, cols].bitcast(FP8X4), rhs_scale=hsc[:, HALF * a + C * i : HALF * a + C * (i + 1)],
                        start=True, stop=True,
                    )
            return sums

        def gated(tile, a, sums):
            weights = gates[:, HALF * a : HALF * (a + 1)].unsqueeze(1).to_broadcast([P, 2, HALF])
            nc.vector.tensor_tensor(tile[:], weights, sums[:], ALU.mult)
            return tile

        def relu_of(step):
            tile, at = (first_relus, step) if step < 2 else (relus, step - 2) if step < own else (last_relus, step - own)
            return tile[:, P * at : P * (at + 1), :]

        def shared_first(step):
            g, u = divmod(step, 4)
            pre_s[step] = bank(4 + u, [P, 4, P])
            for t in range(4):
                nc.tensor.matmul_mx(
                    out=pre_s[step][:, t, :],
                    lhsT=w1sp[:, PASS * g + P * t : PASS * g + P * (t + 1)].bitcast(FP8X4),
                    lhsT_scale=w1sscp[4 * g : P, P * t : P * (t + 1)],
                    rhs=xw[:, P * u : P * (u + 1)].bitcast(FP8X4), rhs_scale=xs[:, P * u : P * (u + 1)],
                    start=True, stop=True,
                )
            sums = pre_s[step][:].rearrange("p t s -> p s t")
            if step < SCALAR_STEPS:
                nc.scalar.activation(relu_of(step), sums, ACT.Relu)
            else:
                nc.vector.tensor_scalar_max(relu_of(step), sums, 0.0)

        def vector_square(step):
            cut = max(GPSIMD_COLUMNS[-1] - P * step, 0)
            nc.vector.scalar_tensor_tensor(
                hs[1][:, P * (step - 4) + cut : P * (step - 3), :],
                pre_s[step][:].rearrange("p t s -> p s t")[:, cut:P], 0.0, relu_of(step)[:, cut:P],
                ALU.max, ALU.mult,
            )

        for e in range(E):
            routed_first(e)
        for e in range(E):
            routed_relu(e, e)
        for e in range(E):
            routed_square(e)
        deal(w2scp[:], w2sc[:, 0 : 2 * N], 16)
        flat = "p e b -> p (e b)"
        deal(w2p[:].rearrange(flat).bitcast(U16), w2w[0][:].rearrange(flat).bitcast(U16), 8)
        deal(w1sp[:], w1sw[:], 4)
        deal(w1sscp[:], w1ssc[:], 16)
        hq = [held([P, HALF], U32, "w1ssc")]
        quantize(hq[0][:], hsc[:, 0:HALF], hb[0][:])
        w2sp = held([P, G * N], I32, "w2sp")
        for g in range(G):
            deal(w2sp[:, N * g : N * (g + 1)], w2sw[g][:], 4)
        near = [routed_second(u, 0, (2 * u, 2 * u + 1), w2p, w2scp) for u in range(2)]
        hq.append(placed([P, HALF], U32, "hq1", HQ_1_AT))
        quantize(hq[1][:], hsc[:, HALF:T], hb[1][:])
        y = [gated(placed([P, 2, HALF], F32, "y0", Y_0_AT), 0, near[0])]
        for step in range(SCALAR_STEPS):
            shared_first(step)
        moved = held([P, 4, HALF], F32, "moved")
        for u in range(2):
            shared_first(SCALAR_STEPS + u)
            far = routed_second(2 + u, 1, (u, u + 2), w2w[1], w2sc[:, 2 * N : 4 * N])
            plain = gated(held([P, 2, HALF], F32, "plain%d" % u), 1, far)
            for j in range(2):
                block = u + 2 * j
                nc.sync.dma_start(out=moved[32 * block : 32 * (block + 1), :, :], in_=plain[:, j, :])
        y.append(gated(held([P, 2, HALF], F32, "y1"), 0, near[1]))
        hs = [placed([P, T, 4], BF16, "hs0", H_1_AT), placed([P, T, 4], BF16, "hs1", HS_1_AT)]
        for step in range(SCALAR_STEPS + 2, STEPS):
            shared_first(step)
        for step in range(GPSIMD_COLUMNS[-1] // P, STEPS):
            vector_square(step)
        for first, last in zip(GPSIMD_COLUMNS, GPSIMD_COLUMNS[1:]):
            values = first_relus[:, first:last, :] if last <= 2 * P else relus[:, first - 2 * P : last - 2 * P, :]
            at = first % T
            nc.gpsimd.tensor_tensor(hs[first // T][:, at : at + last - first, :], values, values, ALU.mult)

        def deal_w2s_plane(engine, tile, first, last):
            engine.tensor_copy(
                out=tile[:].rearrange("p t (c i) -> p c t i", i=16),
                in_=w2ssc[:].rearrange("p (c i t) -> p c t i", i=16, t=4)[:, :, first:last, :],
            )

        w2sscp = [placed([P, 2, P], U8, "w2sscp0", RELUS_AT + 2 * ROW)]
        deal_w2s_plane(nc.vector, w2sscp[0], 0, 2)
        hsq = [placed([P, T], U32, "hsq0", RELUS_AT + ROW), held([P, T], U32, "hsq1")]
        for g in range(G):
            quantize(hsq[g][:], hssc[g][:], hs[g][:])
        w2sscp.append(placed([P, 2, P], U8, "w2sscp1", HS_1_AT))
        deal_w2s_plane(nc.gpsimd, w2sscp[1], 2, 4)
        win = [held([P, T], F32, "win%d" % t) for t in range(4)]
        for t in range(4):
            nc.scalar.activation(win[t][:].indirect(slots(0, HALF)), y[t // 2][:, t % 2, :], ACT.Copy)
        for t in range(2):
            nc.scalar.activation(win[t][:].indirect(slots(HALF, T)), moved[:, t, :], ACT.Copy)
        for t in range(2, 4):
            cut = SCALAR_SLOTS[t]
            nc.vector.tensor_copy(win[t][:].indirect(slots(HALF + cut, T)), moved[:, t, cut:HALF])
        for t in range(2, 4):
            cut = SCALAR_SLOTS[t]
            nc.scalar.activation(win[t][:].indirect(slots(HALF, HALF + cut)), moved[:, t, 0:cut], ACT.Copy)

        ys = [bank(number, [P, T]) for number in range(4)]
        for t in range(4):
            for g in range(G):
                nc.tensor.matmul_mx(
                    out=ys[t][:],
                    lhsT=w2sp[:, N * g + P * t : N * g + P * (t + 1)].bitcast(FP8X4),
                    lhsT_scale=w2sscp[t // 2][4 * g : P, t % 2, :],
                    rhs=hsq[g][:].bitcast(FP8X4), rhs_scale=hssc[g][:],
                    start=(g == 0), stop=(g == G - 1),
                )

        total = held([P, 4, T], F32, "total")
        rows = out_0.rearrange("(p t) c -> p t c", t=4)
        for t in range(3):
            nc.vector.tensor_tensor(total[:, t, :], ys[t][:], win[t][:], ALU.add)
            if t > 0:
                first = 0 if t == 1 else t
                nc.sync.dma_start(out=rows[:, first : t + 1, :], in_=total[:, first : t + 1, :])
        for a in range(2):
            cols = slice(HALF * a, HALF * (a + 1))
            nc.vector.tensor_tensor(total[:, 3, cols], ys[3][:, cols], win[3][:, cols], ALU.add)
        nc.sync.dma_start(out=rows[:, 3, :], in_=total[:, 3, :])

        oq = held([P, T], U32, "oq")
        osc = held([P, T], U8, "osc")
        words_out = out_1[0].rearrange("p t d -> p (t d)").bitcast(I32)
        ob = [held([P, HALF, 4], BF16, "ob%d" % a) for a in range(2)]

        def rounded(a, first, last):
            return interleaved(ob[a][:, first:last, :], total[:, :, HALF * a + first : HALF * a + last])

        nc.scalar.copy(*rounded(1, 0, SCALAR_TOKENS))
        nc.vector.tensor_copy(*rounded(0, 0, HALF))
        nc.vector.tensor_copy(*rounded(1, SCALAR_TOKENS, HALF))
        for a in range(2):
            cols = slice(HALF * a, HALF * (a + 1))
            quantize(oq[:, cols], osc[:, cols], ob[a][:])
            nc.sync.dma_start(out=words_out[:, cols], in_=oq[:, cols].bitcast(I32))
        for q in range(4):
            (nc.sync if q == 3 else nc.scalar).dma_start(
                out=out_2[0, 4 * q : 4 * q + 4, :].bitcast(I32),
                in_=osc[32 * q : 32 * q + 4, :].bitcast(I32),
            )
